import numpy as np
import ml_dtypes


def mxq(x, axis, fmt="e4m3"):
    dtype, down = {"e4m3": (ml_dtypes.float8_e4m3fn, 7), "e5m2": (ml_dtypes.float8_e5m2, 14)}[fmt]
    v = np.moveaxis(np.asarray(x, np.float32).astype(ml_dtypes.bfloat16).astype(np.float64), axis, -1)
    blocks = v.reshape(v.shape[:-1] + (-1, 32))
    amax = np.abs(blocks).max(-1, keepdims=True)
    byte = np.maximum(np.where(amax > 0, np.frexp(amax)[1] - 1 + 127, 0) - down, 1)
    scale = np.exp2(byte - 127.0)
    codes = (blocks / scale).astype(np.float32).astype(dtype).astype(np.float64)
    return np.moveaxis((codes * scale).reshape(v.shape), -1, axis)


WIDE = False


def mx_kscale(k):
    if not WIDE:
        return np.ones(k)
    levels = np.array([10, -10, 5, -5, 0])
    if k % 512:
        return np.exp2(np.random.permutation(np.resize(levels, k // 32))).repeat(32)
    a = np.empty((k // 512, 16))
    for p in range(k // 512):
        a[p, :8] = np.random.permutation(np.resize(levels, 8))
        for g in range(8):
            far = levels[np.abs(levels - a[p, g]) >= 10]
            a[p, g + 8] = far[np.random.randint(len(far))]
    return np.exp2(a.ravel()).repeat(32)


def f64(x):
    return np.asarray(x).astype(np.float64)


def striped(idx):
    return np.tile(idx.reshape(-1, 16).T, (8, 1)).astype(np.uint16)


def unstriped(offs):
    return offs[:16].T.reshape(-1).astype(np.int64)


def pack_weight(w):
    k, n = w.shape
    w = f64(np.asarray(w, np.float32).astype(ml_dtypes.bfloat16)).reshape(k // 32, 32, n)
    amax = np.abs(w).max(1)
    byte = np.clip(np.where(amax > 0, np.frexp(amax)[1] - 1 + 127 - 7, 1), 1, 254)
    scaled = (w * np.exp2(127.0 - byte)[:, None, :]).reshape(k, n).astype(np.float32)
    words = np.ascontiguousarray(scaled.reshape(k // 512, 128, 4, n).transpose(0, 1, 3, 2)).astype(ml_dtypes.float8_e4m3fn).view(np.uint8)
    return words, np.ascontiguousarray(byte.astype(np.uint8).reshape(k // 512, 16, n))


def unpack_weight(words, scales):
    g, p, n, _ = words.shape
    vals = np.ascontiguousarray(words).view(ml_dtypes.float8_e4m3fn).astype(np.float64) * np.repeat(np.exp2(scales.astype(np.float64) - 127.0), 8, axis=1)[..., None]
    return vals.transpose(0, 1, 3, 2).reshape(g * 512, n)


def relu(v):
    return np.maximum(v, 0.0)


K, T, S, H, N = 1024, 1024, 512, 512, 128


def setup_inputs():
    n = np.random.standard_normal
    s = mx_kscale(K)[:, None]
    u = mx_kscale(H)
    packed_w1 = pack_weight(n((K, N)) / np.sqrt(2 * K) / s)
    packed_w3 = pack_weight(n((H, N)) / np.sqrt(2 * H) / u[:, None])
    return {
        "xT": (n((K, T)) * s).astype(np.float32),
        "w1_words": packed_w1[0],
        "w1_scales": packed_w1[1],
        "w2": (n((K, H)) / np.sqrt(K) / s * u).astype(np.float32),
        "w3_words": packed_w3[0],
        "w3_scales": packed_w3[1],
        "offs": striped(np.random.permutation(T)[:S]),
    }


def reference(xT, w1_words, w1_scales, w2, w3_words, w3_scales, offs):
    xq = mxq(f64(xT)[:, unstriped(offs)], 0, "e4m3")
    h = relu(mxq(f64(w2), 0, "e4m3").T @ xq)
    return unpack_weight(w1_words, w1_scales).T @ xq + unpack_weight(w3_words, w3_scales).T @ mxq(h, 0, "e4m3")

@@ -1,0 +1,184 @@
+from contextlib import ExitStack
+
+import concourse.mybir as mybir
+
+K, T, S, H, N = 1024, 1024, 512, 512, 128
+FLOPS = 2 * S * (K * H + K * N + H * N)
+
+F32 = mybir.dt.float32
+BF16 = mybir.dt.bfloat16
+I32 = mybir.dt.int32
+U32 = mybir.dt.uint32
+U16 = mybir.dt.uint16
+U8 = mybir.dt.uint8
+FP8X4 = mybir.dt.float8_e4m3fn_x4
+COPY = mybir.ActivationFunctionType.Copy
+RELU = mybir.ActivationFunctionType.Relu
+
+P = 128
+PACK = 4
+K_PASS = P * PACK
+CHUNK = 128
+CHUNKS = S // CHUNK
+PLANE_STEP = 4
+
+X_PIECES = [(0, 0, 512, 256), (0, 512, 1024, 192), (1, 0, 512, 384), (1, 512, 768, 128), (1, 768, 1024, 112)]
+W2_PIECES = [(0, 0, 256, "s"), (0, 256, 512, "s"), (1, 0, 256, "v"), (1, 256, 384, "s"), (1, 384, 512, "s")]
+GATHER = 256
+
+
+def tile_picked_lora_relu_e_kernel(tc, xT, w1_words, w1_scales, w2, w3_words, w3_scales, offs, out):
+    nc = tc.nc
+
+    def move(engine, dst, src):
+        if engine == "s":
+            nc.scalar.activation(out=dst, in_=src, func=COPY)
+        else:
+            nc.vector.tensor_copy(out=dst, in_=src)
+
+    with ExitStack() as ctx:
+        keep = ctx.enter_context(tc.tile_pool(name="keep", bufs=1))
+        psum = ctx.enter_context(tc.psum_pool(name="psum", bufs=1))
+
+        offsets = keep.tile([P, S // 16], U16, name="offsets")
+        x_scales = keep.tile([P, T], U8, name="x_scales", align_bytes=64)
+        w1_sc = keep.tile([P, 2 * N], U8, name="w1_sc", align_bytes=64)
+        w3_sc = keep.tile([P, N], U8, name="w3_sc", align_bytes=64)
+        nc.vector.memset(w1_sc[:].bitcast(I32), 0)
+        nc.vector.memset(w3_sc[:].bitcast(I32), 0)
+        nc.vector.memset(x_scales[:].bitcast(I32), 0)
+
+        x_raw = []
+        for i, (z, t0, t1, ts) in enumerate(X_PIECES):
+            raw = keep.tile([P, PACK, t1 - t0], F32, name=f"x_raw{i}")
+            nc.sync.dma_start(out=raw[:], in_=xT[z * K_PASS : (z + 1) * K_PASS, t0:t1].rearrange("(p j) t -> p j t", j=PACK))
+            x_raw.append(raw)
+            if i == 0:
+                nc.sync.dma_start(offsets[:], offs)
+        w1_rows = w1_scales.rearrange("z (q r) n -> r q z n", r=4)
+        for r in range(4):
+            nc.scalar.dma_start(out=w1_sc[r:P:32, :].bitcast(I32).rearrange("q (z n) -> q z n", z=2), in_=w1_rows[r].bitcast(I32))
+        w1_w = keep.tile([P, 2, N], I32, name="w1_w", align_bytes=64)
+        w2_raw = []
+        for i, (z, c0, c1, e) in enumerate(W2_PIECES):
+            raw = keep.tile([P, PACK, c1 - c0], F32, name=f"w2_raw{i}")
+            nc.sync.dma_start(out=raw[:], in_=w2[z * K_PASS : (z + 1) * K_PASS, c0:c1].rearrange("(p j) c -> p j c", j=PACK))
+            w2_raw.append(raw)
+            if i == 2:
+                nc.sync.dma_start(out=w1_w[:], in_=w1_words.rearrange("z p n t -> p z (n t)").bitcast(I32))
+        w3_w = keep.tile([P, N], I32, name="w3_w", align_bytes=64)
+        nc.sync.dma_start(out=w3_w[:], in_=w3_words[0].rearrange("p n t -> p (n t)").bitcast(I32))
+        w3_rows = w3_scales[0].rearrange("(q r) n -> r q n", r=4)
+        for r in range(4):
+            nc.sync.dma_start(out=w3_sc[r:P:32, :].bitcast(I32), in_=w3_rows[r].bitcast(I32))
+
+        x_words = [keep.tile([P, T], U32, name=f"x_words{z}", align_bytes=64) for z in range(2)]
+        xg_words = {}
+        xg_scales = {}
+        for i, (z, t0, t1, ts) in enumerate(X_PIECES):
+            n = t1 - t0
+            grouped = keep.tile([P, n * PACK], BF16, name=f"x_bf{i}", align_bytes=64)
+            for e, a, b in (("s", 0, ts), ("v", ts, n)):
+                move(
+                    e,
+                    grouped[:, a * PACK : b * PACK].rearrange("p (c i j) -> p c j i", i=4, j=PACK),
+                    x_raw[i][:, :, a:b].rearrange("p j (c i) -> p c j i", i=4),
+                )
+            nc.vector.quantize_mx(
+                out=x_words[z][:, t0:t1].bitcast(FP8X4),
+                scales=x_scales[PLANE_STEP * z : P, t0:t1],
+                in_=grouped[:],
+            )
+            if z == 0 and t1 == T:
+                g = keep.tile([P, S], U32, name="xg_words0", align_bytes=64)
+                nc.vector.tensor_copy(out=g[:], in_=x_words[0][:].indirect(offsets[:]))
+                for c in range(CHUNKS):
+                    xg_words[0, c] = g[:, c * CHUNK : (c + 1) * CHUNK]
+
+        def gather_last(g0):
+            lst = offsets[:, g0 // 16 : (g0 + GATHER) // 16]
+            gs = keep.tile([P, GATHER], U8, name=f"xg_scales{g0}", align_bytes=64)
+            nc.vector.tensor_copy(out=gs[:], in_=x_scales[:].indirect(lst))
+            gw = keep.tile([P, GATHER], U32, name=f"xg_words1_{g0}", align_bytes=64)
+            nc.vector.tensor_copy(out=gw[:], in_=x_words[1][:].indirect(lst))
+            for c in range(g0 // CHUNK, (g0 + GATHER) // CHUNK):
+                cols = slice(c * CHUNK - g0, (c + 1) * CHUNK - g0)
+                xg_words[1, c] = gw[:, cols]
+                for z in range(2):
+                    xg_scales[z, c] = gs[PLANE_STEP * z : P, cols]
+
+        gather_last(0)
+        gather_last(GATHER)
+
+        w2_codes = [keep.tile([P, H], U32, name=f"w2_codes{z}", align_bytes=64) for z in range(2)]
+        w2_sc = [keep.tile([P, H], U8, name=f"w2_sc{z}", align_bytes=64) for z in range(2)]
+        w2_bf0 = keep.tile([P, H * PACK], BF16, name="w2_bf0", align_bytes=64)
+        w2_bf1 = [keep.tile([P, H * PACK // 2], BF16, name=f"w2_bf1_{hf}", align_bytes=64) for hf in range(2)]
+        for i, (z, c0, c1, e) in enumerate(W2_PIECES):
+            src = w2_raw[i][:].rearrange("p j (m t) -> p m j t", t=PACK)
+            m0, m1 = c0 // PACK, c1 // PACK
+            if z == 0:
+                dst = w2_bf0[:].rearrange("p (t m j) -> p m j t", t=PACK, j=PACK)[:, m0:m1]
+            else:
+                hf = m0 // 64
+                dst = w2_bf1[hf][:].rearrange("p (t m j) -> p m j t", t=PACK, j=PACK)[:, m0 - 64 * hf : m1 - 64 * hf]
+            move(e, dst, src)
+            if z == 0 and c1 == H:
+                nc.vector.quantize_mx(out=w2_codes[0][:].bitcast(FP8X4), scales=w2_sc[0][:], in_=w2_bf0[:])
+            if z == 1 and m1 % 64 == 0:
+                hf = m0 // 64
+                for t in range(PACK):
+                    cols = slice(t * P + 64 * hf, t * P + 64 * (hf + 1))
+                    nc.vector.quantize_mx(out=w2_codes[1][:, cols].bitcast(FP8X4), scales=w2_sc[1][:, cols], in_=w2_bf1[hf][:, t * 256 : (t + 1) * 256])
+
+        h_ps = [psum.tile([P, PACK, CHUNK], F32, name=f"h_ps{c}") for c in range(CHUNKS)]
+        o_ps = [psum.tile([P, CHUNK], F32, name=f"o_ps{c}") for c in range(CHUNKS)]
+
+        def h_pass(c, t, z):
+            cols = slice(t * P, (t + 1) * P)
+            nc.tensor.matmul_mx(
+                out=h_ps[c][:, t, :],
+                lhsT=w2_codes[z][:, cols].bitcast(FP8X4),
+                lhsT_scale=w2_sc[z][:, cols],
+                rhs=xg_words[z, c].bitcast(FP8X4),
+                rhs_scale=xg_scales[z, c],
+                start=(z == 0),
+                stop=(z == 1),
+            )
+
+        for c in range(CHUNKS):
+            for z in range(2):
+                nc.tensor.matmul_mx(
+                    out=o_ps[c][:],
+                    lhsT=w1_w[:, z, :].bitcast(FP8X4),
+                    lhsT_scale=w1_sc[:, z * N : (z + 1) * N],
+                    rhs=xg_words[z, c].bitcast(FP8X4),
+                    rhs_scale=xg_scales[z, c],
+                    start=(z == 0),
+                    stop=False,
+                )
+        for c in range(CHUNKS):
+            h_pass(c, 0, 0)
+        for c in range(CHUNKS):
+            h_pass(c, 0, 1)
+            for t in range(1, PACK):
+                h_pass(c, t, 0)
+                h_pass(c, t, 1)
+        for c in range(CHUNKS):
+            h_bf = keep.tile([P, CHUNK * PACK], BF16, name=f"h_bf{c}", align_bytes=64)
+            nc.scalar.activation(out=h_bf[:].rearrange("p (n t) -> p n t", t=PACK), in_=h_ps[c][:].rearrange("p t n -> p n t"), func=RELU)
+            h_words = keep.tile([P, CHUNK], U32, name=f"h_words{c}", align_bytes=64)
+            h_sc = keep.tile([P, CHUNK], U8, name=f"h_sc{c}", align_bytes=64)
+            nc.vector.quantize_mx(out=h_words[:].bitcast(FP8X4), scales=h_sc[:], in_=h_bf[:])
+            nc.tensor.matmul_mx(
+                out=o_ps[c][:],
+                lhsT=w3_w[:].bitcast(FP8X4),
+                lhsT_scale=w3_sc[:],
+                rhs=h_words[:].bitcast(FP8X4),
+                rhs_scale=h_sc[:],
+                start=False,
+                stop=True,
+            )
+            res = keep.tile([P, CHUNK], F32, name=f"res{c}")
+            nc.vector.tensor_copy(out=res[:], in_=o_ps[c][:])
+            nc.sync.dma_start(out=out[:, c * CHUNK : (c + 1) * CHUNK], in_=res[:])

@@ -22,8 +22,15 @@ CHUNK = 128
 CHUNKS = S // CHUNK
 PLANE_STEP = 4
 
-X_PIECES = [(0, 0, 512, 256), (0, 512, 1024, 192), (1, 0, 512, 384), (1, 512, 768, 128), (1, 768, 1024, 112)]
-W2_PIECES = [(0, 0, 256, "s"), (0, 256, 512, "s"), (1, 0, 256, "v"), (1, 256, 384, "s"), (1, 384, 512, "s")]
+X_PIECES = [
+    (0, 0, 512, (("v", 256), ("s", 256))),
+    (0, 512, 1024, (("v", 256), ("s", 256))),
+    (1, 0, 512, (("s", 256), ("v", 128), ("s", 128))),
+    (1, 512, 768, (("v", 128), ("s", 128))),
+    (1, 768, 1024, (("v", 128), ("s", 128))),
+]
+W2_PIECES = [(0, 0, 256, 256), (0, 256, 512, 256), (1, 0, 256, 128), (1, 256, 384, 128), (1, 384, 512, 64)]
+WARM = (4, 6)
 GATHER = 256
 
 
@@ -55,17 +62,16 @@ def tile_picked_lora_relu_e_kernel(tc, xT, w1_words, w1_scales, w2, w3_words, w3
             x_raw.append(raw)
             if i == 0:
                 nc.sync.dma_start(offsets[:], offs)
-        w1_rows = w1_scales.rearrange("z (q r) n -> r q z n", r=4)
-        for r in range(4):
-            nc.scalar.dma_start(out=w1_sc[r:P:32, :].bitcast(I32).rearrange("q (z n) -> q z n", z=2), in_=w1_rows[r].bitcast(I32))
-        w1_w = keep.tile([P, 2, N], I32, name="w1_w", align_bytes=64)
         w2_raw = []
         for i, (z, c0, c1, e) in enumerate(W2_PIECES):
             raw = keep.tile([P, PACK, c1 - c0], F32, name=f"w2_raw{i}")
             nc.sync.dma_start(out=raw[:], in_=w2[z * K_PASS : (z + 1) * K_PASS, c0:c1].rearrange("(p j) c -> p j c", j=PACK))
             w2_raw.append(raw)
-            if i == 2:
-                nc.sync.dma_start(out=w1_w[:], in_=w1_words.rearrange("z p n t -> p z (n t)").bitcast(I32))
+        w1_w = keep.tile([P, 2, N], I32, name="w1_w", align_bytes=64)
+        nc.sync.dma_start(out=w1_w[:], in_=w1_words.rearrange("z p n t -> p z (n t)").bitcast(I32))
+        w1_rows = w1_scales.rearrange("z (q r) n -> r q z n", r=4)
+        for r in range(4):
+            nc.sync.dma_start(out=w1_sc[r:P:32, :].bitcast(I32).rearrange("q (z n) -> q z n", z=2), in_=w1_rows[r].bitcast(I32))
         w3_w = keep.tile([P, N], I32, name="w3_w", align_bytes=64)
         nc.sync.dma_start(out=w3_w[:], in_=w3_words[0].rearrange("p n t -> p (n t)").bitcast(I32))
         w3_rows = w3_scales[0].rearrange("(q r) n -> r q n", r=4)
@@ -76,19 +82,20 @@ def tile_picked_lora_relu_e_kernel(tc, xT, w1_words, w1_scales, w2, w3_words, w3
         xg_words = {}
         xg_scales = {}
         for i, (z, t0, t1, ts) in enumerate(X_PIECES):
-            n = t1 - t0
-            grouped = keep.tile([P, n * PACK], BF16, name=f"x_bf{i}", align_bytes=64)
-            for e, a, b in (("s", 0, ts), ("v", ts, n)):
+            a = 0
+            for e, n in ts:
+                grouped = keep.tile([P, n * PACK], BF16, name=f"x_bf{i}_{a}", align_bytes=64)
                 move(
                     e,
-                    grouped[:, a * PACK : b * PACK].rearrange("p (c i j) -> p c j i", i=4, j=PACK),
-                    x_raw[i][:, :, a:b].rearrange("p j (c i) -> p c j i", i=4),
+                    grouped[:].rearrange("p (c i j) -> p c j i", i=4, j=PACK),
+                    x_raw[i][:, :, a : a + n].rearrange("p j (c i) -> p c j i", i=4),
                 )
-            nc.vector.quantize_mx(
-                out=x_words[z][:, t0:t1].bitcast(FP8X4),
-                scales=x_scales[PLANE_STEP * z : P, t0:t1],
-                in_=grouped[:],
-            )
+                nc.vector.quantize_mx(
+                    out=x_words[z][:, t0 + a : t0 + a + n].bitcast(FP8X4),
+                    scales=x_scales[PLANE_STEP * z : P, t0 + a : t0 + a + n],
+                    in_=grouped[:],
+                )
+                a += n
             if z == 0 and t1 == T:
                 g = keep.tile([P, S], U32, name="xg_words0", align_bytes=64)
                 nc.vector.tensor_copy(out=g[:], in_=x_words[0][:].indirect(offsets[:]))
@@ -122,7 +129,10 @@ def tile_picked_lora_relu_e_kernel(tc, xT, w1_words, w1_scales, w2, w3_words, w3
             else:
                 hf = m0 // 64
                 dst = w2_bf1[hf][:].rearrange("p (t m j) -> p m j t", t=PACK, j=PACK)[:, m0 - 64 * hf : m1 - 64 * hf]
-            move(e, dst, src)
+            ms = e // PACK
+            move("s", dst[:, 0:ms], src[:, 0:ms])
+            if ms < m1 - m0:
+                move("v", dst[:, ms : m1 - m0], src[:, ms : m1 - m0])
             if z == 0 and c1 == H:
                 nc.vector.quantize_mx(out=w2_codes[0][:].bitcast(FP8X4), scales=w2_sc[0][:], in_=w2_bf0[:])
             if z == 1 and m1 % 64 == 0:
@@ -146,6 +156,24 @@ def tile_picked_lora_relu_e_kernel(tc, xT, w1_words, w1_scales, w2, w3_words, w3
                 stop=(z == 1),
             )
 
+        for z in range(2):
+            for i in range(WARM[z]):
+                nc.tensor.matmul_mx(
+                    out=o_ps[i % CHUNKS][:],
+                    lhsT=xg_words[z, 2].bitcast(FP8X4),
+                    lhsT_scale=xg_scales[z, 2],
+                    rhs=xg_words[z, 3].bitcast(FP8X4),
+                    rhs_scale=xg_scales[z, 3],
+                    start=True,
+                    stop=True,
+                )
+        for c in range(CHUNKS):
+            h_pass(c, 0, 0)
+        for c in range(CHUNKS):
+            h_pass(c, 0, 1)
+            for t in range(1, PACK):
+                h_pass(c, t, 0)
+                h_pass(c, t, 1)
         for c in range(CHUNKS):
             for z in range(2):
                 nc.tensor.matmul_mx(
@@ -157,14 +185,6 @@ def tile_picked_lora_relu_e_kernel(tc, xT, w1_words, w1_scales, w2, w3_words, w3
                     start=(z == 0),
                     stop=False,
                 )
-        for c in range(CHUNKS):
-            h_pass(c, 0, 0)
-        for c in range(CHUNKS):
-            h_pass(c, 0, 1)
-            for t in range(1, PACK):
-                h_pass(c, t, 0)
-                h_pass(c, t, 1)
-        for c in range(CHUNKS):
             h_bf = keep.tile([P, CHUNK * PACK], BF16, name=f"h_bf{c}", align_bytes=64)
             nc.scalar.activation(out=h_bf[:].rearrange("p (n t) -> p n t", t=PACK), in_=h_ps[c][:].rearrange("p t n -> p n t"), func=RELU)
             h_words = keep.tile([P, CHUNK], U32, name=f"h_words{c}", align_bytes=64)

@@ -25,12 +25,13 @@ PLANE_STEP = 4
 X_PIECES = [
     (0, 0, 512, (("v", 256), ("s", 256))),
     (0, 512, 1024, (("v", 256), ("s", 256))),
-    (1, 0, 512, (("s", 256), ("v", 128), ("s", 128))),
+    (1, 0, 256, (("s", 256),)),
+    (1, 256, 512, (("s", 256),)),
     (1, 512, 768, (("v", 128), ("s", 128))),
     (1, 768, 1024, (("v", 128), ("s", 128))),
 ]
 W2_PIECES = [(0, 0, 256, 256), (0, 256, 512, 256), (1, 0, 256, 128), (1, 256, 384, 128), (1, 384, 512, 64)]
-WARM = (4, 6)
+WARM = 10
 GATHER = 256
 
 
@@ -156,17 +157,16 @@ def tile_picked_lora_relu_e_kernel(tc, xT, w1_words, w1_scales, w2, w3_words, w3
                 stop=(z == 1),
             )
 
-        for z in range(2):
-            for i in range(WARM[z]):
-                nc.tensor.matmul_mx(
-                    out=o_ps[i % CHUNKS][:],
-                    lhsT=xg_words[z, 2].bitcast(FP8X4),
-                    lhsT_scale=xg_scales[z, 2],
-                    rhs=xg_words[z, 3].bitcast(FP8X4),
-                    rhs_scale=xg_scales[z, 3],
-                    start=True,
-                    stop=True,
-                )
+        for i in range(WARM):
+            nc.tensor.matmul_mx(
+                out=o_ps[i % CHUNKS][:],
+                lhsT=xg_words[0, CHUNKS - 2].bitcast(FP8X4),
+                lhsT_scale=xg_scales[0, CHUNKS - 2],
+                rhs=xg_words[0, CHUNKS - 1].bitcast(FP8X4),
+                rhs_scale=xg_scales[0, CHUNKS - 1],
+                start=True,
+                stop=True,
+            )
         for c in range(CHUNKS):
             h_pass(c, 0, 0)
         for c in range(CHUNKS):

@@ -23,14 +23,11 @@ CHUNKS = S // CHUNK
 PLANE_STEP = 4
 
 X_PIECES = [
-    (0, 0, 512, (("v", 256), ("s", 256))),
-    (0, 512, 1024, (("v", 256), ("s", 256))),
-    (1, 0, 256, (("s", 256),)),
-    (1, 256, 512, (("s", 256),)),
-    (1, 512, 768, (("v", 128), ("s", 128))),
-    (1, 768, 1024, (("v", 128), ("s", 128))),
+    (0, 0, 1024, (("v", 256), ("s", 256), ("v", 256), ("s", 256))),
+    (1, 0, 512, (("s", 256), ("v", 128), ("s", 128))),
+    (1, 512, 1024, (("v", 256), ("s", 256))),
 ]
-W2_PIECES = [(0, 0, 256, 256), (0, 256, 512, 256), (1, 0, 256, 128), (1, 256, 384, 128), (1, 384, 512, 64)]
+W2_PIECES = [(0, 0, 512, 384), (1, 0, 256, 192), (1, 256, 512, 128)]
 WARM = 10
 GATHER = 256
 
@@ -46,6 +43,7 @@ def tile_picked_lora_relu_e_kernel(tc, xT, w1_words, w1_scales, w2, w3_words, w3
 
     with ExitStack() as ctx:
         keep = ctx.enter_context(tc.tile_pool(name="keep", bufs=1))
+        late = ctx.enter_context(tc.tile_pool(name="late", bufs=1))
         psum = ctx.enter_context(tc.psum_pool(name="psum", bufs=1))
 
         offsets = keep.tile([P, S // 16], U16, name="offsets")
@@ -97,31 +95,25 @@ def tile_picked_lora_relu_e_kernel(tc, xT, w1_words, w1_scales, w2, w3_words, w3
                     in_=grouped[:],
                 )
                 a += n
-            if z == 0 and t1 == T:
-                g = keep.tile([P, S], U32, name="xg_words0", align_bytes=64)
-                nc.vector.tensor_copy(out=g[:], in_=x_words[0][:].indirect(offsets[:]))
-                for c in range(CHUNKS):
-                    xg_words[0, c] = g[:, c * CHUNK : (c + 1) * CHUNK]
-
-        def gather_last(g0):
-            lst = offsets[:, g0 // 16 : (g0 + GATHER) // 16]
-            gs = keep.tile([P, GATHER], U8, name=f"xg_scales{g0}", align_bytes=64)
-            nc.vector.tensor_copy(out=gs[:], in_=x_scales[:].indirect(lst))
-            gw = keep.tile([P, GATHER], U32, name=f"xg_words1_{g0}", align_bytes=64)
-            nc.vector.tensor_copy(out=gw[:], in_=x_words[1][:].indirect(lst))
-            for c in range(g0 // CHUNK, (g0 + GATHER) // CHUNK):
-                cols = slice(c * CHUNK - g0, (c + 1) * CHUNK - g0)
-                xg_words[1, c] = gw[:, cols]
-                for z in range(2):
-                    xg_scales[z, c] = gs[PLANE_STEP * z : P, cols]
-
-        gather_last(0)
-        gather_last(GATHER)
+            if t1 == T:
+                if z == 1:
+                    gs = keep.tile([P, S], U8, name="xg_scales", align_bytes=64)
+                    nc.vector.tensor_copy(out=gs[:], in_=x_scales[:].indirect(offsets[:]))
+                    for c in range(CHUNKS):
+                        for zz in range(2):
+                            xg_scales[zz, c] = gs[PLANE_STEP * zz : P, c * CHUNK : (c + 1) * CHUNK]
+                gw = keep.tile([P, GATHER], U32, name=f"xg_words{z}", align_bytes=64)
+                nc.vector.tensor_copy(out=gw[:], in_=x_words[z][:].indirect(offsets[:, 0 : GATHER // 16]))
+                for c in range(GATHER // CHUNK):
+                    xg_words[z, c] = gw[:, c * CHUNK : (c + 1) * CHUNK]
 
         w2_codes = [keep.tile([P, H], U32, name=f"w2_codes{z}", align_bytes=64) for z in range(2)]
         w2_sc = [keep.tile([P, H], U8, name=f"w2_sc{z}", align_bytes=64) for z in range(2)]
         w2_bf0 = keep.tile([P, H * PACK], BF16, name="w2_bf0", align_bytes=64)
-        w2_bf1 = [keep.tile([P, H * PACK // 2], BF16, name=f"w2_bf1_{hf}", align_bytes=64) for hf in range(2)]
+        w2_bf1 = [
+            keep.tile([P, H * PACK // 2], BF16, name="w2_bf1_0", align_bytes=64),
+            late.tile([P, H * PACK // 2], BF16, name="w2_bf1_1", align_bytes=64, offset=0),
+        ]
         for i, (z, c0, c1, e) in enumerate(W2_PIECES):
             src = w2_raw[i][:].rearrange("p j (m t) -> p m j t", t=PACK)
             m0, m1 = c0 // PACK, c1 // PACK
@@ -142,6 +134,12 @@ def tile_picked_lora_relu_e_kernel(tc, xT, w1_words, w1_scales, w2, w3_words, w3
                     cols = slice(t * P + 64 * hf, t * P + 64 * (hf + 1))
                     nc.vector.quantize_mx(out=w2_codes[1][:, cols].bitcast(FP8X4), scales=w2_sc[1][:, cols], in_=w2_bf1[hf][:, t * 256 : (t + 1) * 256])
 
+        for c in range(GATHER // CHUNK, CHUNKS):
+            for z in range(2):
+                gw = late.tile([P, CHUNK], U32, name=f"xg_late{z}{c}", align_bytes=64, offset=512 * (2 * (c - GATHER // CHUNK) + z))
+                nc.vector.tensor_copy(out=gw[:], in_=x_words[z][:].indirect(offsets[:, c * CHUNK // 16 : (c + 1) * CHUNK // 16]))
+                xg_words[z, c] = gw[:]
+
         h_ps = [psum.tile([P, PACK, CHUNK], F32, name=f"h_ps{c}") for c in range(CHUNKS)]
         o_ps = [psum.tile([P, CHUNK], F32, name=f"o_ps{c}") for c in range(CHUNKS)]
 
@@ -160,18 +158,15 @@ def tile_picked_lora_relu_e_kernel(tc, xT, w1_words, w1_scales, w2, w3_words, w3
         for i in range(WARM):
             nc.tensor.matmul_mx(
                 out=o_ps[i % CHUNKS][:],
-                lhsT=xg_words[0, CHUNKS - 2].bitcast(FP8X4),
-                lhsT_scale=xg_scales[0, CHUNKS - 2],
-                rhs=xg_words[0, CHUNKS - 1].bitcast(FP8X4),
-                rhs_scale=xg_scales[0, CHUNKS - 1],
+                lhsT=xg_words[1, 0].bitcast(FP8X4),
+                lhsT_scale=xg_scales[1, 0],
+                rhs=xg_words[1, 1].bitcast(FP8X4),
+                rhs_scale=xg_scales[1, 1],
                 start=True,
                 stop=True,
             )
         for c in range(CHUNKS):
-            h_pass(c, 0, 0)
-        for c in range(CHUNKS):
-            h_pass(c, 0, 1)
-            for t in range(1, PACK):
+            for t in range(PACK):
                 h_pass(c, t, 0)
                 h_pass(c, t, 1)
         for c in range(CHUNKS):

@@ -23,13 +23,16 @@ CHUNKS = S // CHUNK
 PLANE_STEP = 4
 
 X_PIECES = [
-    (0, 0, 1024, (("v", 256), ("s", 256), ("v", 256), ("s", 256))),
-    (1, 0, 512, (("s", 256), ("v", 128), ("s", 128))),
-    (1, 512, 1024, (("v", 256), ("s", 256))),
+    (0, 0, 512, (("s", 256), ("v", 256))),
+    (0, 512, 1024, (("v", 256), ("s", 128), ("v", 128))),
+    (1, 0, 512, (("s", 256), ("v", 256))),
+    (1, 512, 768, (("s", 256),)),
+    (1, 768, 1024, (("v", 128), ("s", 128))),
 ]
-W2_PIECES = [(0, 0, 512, 384), (1, 0, 256, 192), (1, 256, 512, 128)]
-WARM = 10
-GATHER = 256
+W2_PIECES = [(0, 0, 256, 256), (0, 256, 512, 256), (1, 0, 256, 256), (1, 256, 512, 80)]
+RELU_ON = "vsvs"
+OUT_GROUPS = [(0, 2, "s"), (2, 1, "v"), (3, 1, "s")]
+WARM = (4, 4, 2, 1)
 
 
 def tile_picked_lora_relu_e_kernel(tc, xT, w1_words, w1_scales, w2, w3_words, w3_scales, offs, out):
@@ -47,41 +50,82 @@ def tile_picked_lora_relu_e_kernel(tc, xT, w1_words, w1_scales, w2, w3_words, w3
         psum = ctx.enter_context(tc.psum_pool(name="psum", bufs=1))
 
         offsets = keep.tile([P, S // 16], U16, name="offsets")
-        x_scales = keep.tile([P, T], U8, name="x_scales", align_bytes=64)
+        x_scales = late.tile([P, T], U8, name="x_scales", align_bytes=64, offset=0)
         w1_sc = keep.tile([P, 2 * N], U8, name="w1_sc", align_bytes=64)
         w3_sc = keep.tile([P, N], U8, name="w3_sc", align_bytes=64)
         nc.vector.memset(w1_sc[:].bitcast(I32), 0)
         nc.vector.memset(w3_sc[:].bitcast(I32), 0)
         nc.vector.memset(x_scales[:].bitcast(I32), 0)
 
-        x_raw = []
-        for i, (z, t0, t1, ts) in enumerate(X_PIECES):
-            raw = keep.tile([P, PACK, t1 - t0], F32, name=f"x_raw{i}")
-            nc.sync.dma_start(out=raw[:], in_=xT[z * K_PASS : (z + 1) * K_PASS, t0:t1].rearrange("(p j) t -> p j t", j=PACK))
-            x_raw.append(raw)
-            if i == 0:
-                nc.sync.dma_start(offsets[:], offs)
-        w2_raw = []
-        for i, (z, c0, c1, e) in enumerate(W2_PIECES):
-            raw = keep.tile([P, PACK, c1 - c0], F32, name=f"w2_raw{i}")
-            nc.sync.dma_start(out=raw[:], in_=w2[z * K_PASS : (z + 1) * K_PASS, c0:c1].rearrange("(p j) c -> p j c", j=PACK))
-            w2_raw.append(raw)
+        x_raw = {}
+        w2_raw = {}
         w1_w = keep.tile([P, 2, N], I32, name="w1_w", align_bytes=64)
-        nc.sync.dma_start(out=w1_w[:], in_=w1_words.rearrange("z p n t -> p z (n t)").bitcast(I32))
-        w1_rows = w1_scales.rearrange("z (q r) n -> r q z n", r=4)
-        for r in range(4):
-            nc.sync.dma_start(out=w1_sc[r:P:32, :].bitcast(I32).rearrange("q (z n) -> q z n", z=2), in_=w1_rows[r].bitcast(I32))
         w3_w = keep.tile([P, N], I32, name="w3_w", align_bytes=64)
-        nc.sync.dma_start(out=w3_w[:], in_=w3_words[0].rearrange("p n t -> p (n t)").bitcast(I32))
-        w3_rows = w3_scales[0].rearrange("(q r) n -> r q n", r=4)
-        for r in range(4):
-            nc.sync.dma_start(out=w3_sc[r:P:32, :].bitcast(I32), in_=w3_rows[r].bitcast(I32))
+
+        def load_x(i):
+            z, t0, t1, parts = X_PIECES[i]
+            x_raw[i] = keep.tile([P, PACK, t1 - t0], F32, name=f"x_raw{i}")
+            nc.sync.dma_start(out=x_raw[i][:], in_=xT[z * K_PASS : (z + 1) * K_PASS, t0:t1].rearrange("(p j) t -> p j t", j=PACK))
+
+        def load_w2(i):
+            z, c0, c1, share = W2_PIECES[i]
+            w2_raw[i] = keep.tile([P, PACK, c1 - c0], F32, name=f"w2_raw{i}")
+            nc.sync.dma_start(out=w2_raw[i][:], in_=w2[z * K_PASS : (z + 1) * K_PASS, c0:c1].rearrange("(p j) c -> p j c", j=PACK))
+
+        def load_list():
+            nc.sync.dma_start(offsets[:], offs)
+
+        def load_w1_words():
+            nc.sync.dma_start(out=w1_w[:], in_=w1_words.rearrange("z p n t -> p z (n t)").bitcast(I32))
+
+        def load_w1_scales():
+            w1_rows = w1_scales.rearrange("z (q r) n -> r q z n", r=4)
+            for r in range(4):
+                nc.sync.dma_start(out=w1_sc[r:P:32, :].bitcast(I32).rearrange("q (z n) -> q z n", z=2), in_=w1_rows[r].bitcast(I32))
+
+        def load_w3_words():
+            nc.sync.dma_start(out=w3_w[:], in_=w3_words[0].rearrange("p n t -> p (n t)").bitcast(I32))
+
+        def load_w3_scales():
+            w3_rows = w3_scales[0].rearrange("(q r) n -> r q n", r=4)
+            for r in range(4):
+                nc.sync.dma_start(out=w3_sc[r:P:32, :].bitcast(I32), in_=w3_rows[r].bitcast(I32))
+
+        load_x(0)
+        load_list()
+        load_x(1)
+        load_x(2)
+        load_x(3)
+        load_x(4)
+        load_w2(0)
+        load_w2(1)
+        load_w2(2)
+        load_w2(3)
+        load_w1_words()
+        load_w1_scales()
+        load_w3_words()
+        load_w3_scales()
 
         x_words = [keep.tile([P, T], U32, name=f"x_words{z}", align_bytes=64) for z in range(2)]
         xg_words = {}
-        xg_scales = {}
+        xg_scales = keep.tile([P, S], U8, name="xg_scales", align_bytes=64)
+
+        def gather_words(z, first, count, offset=None):
+            if offset is None:
+                gw = keep.tile([P, count * CHUNK], U32, name=f"xg_words{z}_{first}", align_bytes=64)
+            else:
+                gw = late.tile([P, count * CHUNK], U32, name=f"xg_words{z}_{first}", align_bytes=64, offset=offset)
+            nc.vector.tensor_copy(out=gw[:], in_=x_words[z][:].indirect(offsets[:, first * CHUNK // 16 : (first + count) * CHUNK // 16]))
+            for c in range(count):
+                xg_words[z, first + c] = (gw, c * CHUNK)
+
+        def x_operand(z, first, count):
+            gw, a = xg_words[z, first]
+            return gw[:, a : a + count * CHUNK].bitcast(FP8X4), xg_scales[PLANE_STEP * z : P, first * CHUNK : (first + count) * CHUNK]
+
         for i, (z, t0, t1, ts) in enumerate(X_PIECES):
             a = 0
+            parts = []
             for e, n in ts:
                 grouped = keep.tile([P, n * PACK], BF16, name=f"x_bf{i}_{a}", align_bytes=64)
                 move(
@@ -89,104 +133,117 @@ def tile_picked_lora_relu_e_kernel(tc, xT, w1_words, w1_scales, w2, w3_words, w3
                     grouped[:].rearrange("p (c i j) -> p c j i", i=4, j=PACK),
                     x_raw[i][:, :, a : a + n].rearrange("p j (c i) -> p c j i", i=4),
                 )
+                parts.append((grouped, t0 + a, n))
+                a += n
+            for grouped, b, n in parts:
                 nc.vector.quantize_mx(
-                    out=x_words[z][:, t0 + a : t0 + a + n].bitcast(FP8X4),
-                    scales=x_scales[PLANE_STEP * z : P, t0 + a : t0 + a + n],
+                    out=x_words[z][:, b : b + n].bitcast(FP8X4),
+                    scales=x_scales[PLANE_STEP * z : P, b : b + n],
                     in_=grouped[:],
                 )
-                a += n
-            if t1 == T:
-                if z == 1:
-                    gs = keep.tile([P, S], U8, name="xg_scales", align_bytes=64)
-                    nc.vector.tensor_copy(out=gs[:], in_=x_scales[:].indirect(offsets[:]))
-                    for c in range(CHUNKS):
-                        for zz in range(2):
-                            xg_scales[zz, c] = gs[PLANE_STEP * zz : P, c * CHUNK : (c + 1) * CHUNK]
-                gw = keep.tile([P, GATHER], U32, name=f"xg_words{z}", align_bytes=64)
-                nc.vector.tensor_copy(out=gw[:], in_=x_words[z][:].indirect(offsets[:, 0 : GATHER // 16]))
-                for c in range(GATHER // CHUNK):
-                    xg_words[z, c] = gw[:, c * CHUNK : (c + 1) * CHUNK]
+            if t1 == T and z == 0:
+                gather_words(0, 0, CHUNKS)
+        nc.vector.tensor_copy(out=xg_scales[:], in_=x_scales[:].indirect(offsets[:]))
+        gather_words(1, 0, 3, offset=0)
 
         w2_codes = [keep.tile([P, H], U32, name=f"w2_codes{z}", align_bytes=64) for z in range(2)]
         w2_sc = [keep.tile([P, H], U8, name=f"w2_sc{z}", align_bytes=64) for z in range(2)]
-        w2_bf0 = keep.tile([P, H * PACK], BF16, name="w2_bf0", align_bytes=64)
-        w2_bf1 = [
-            keep.tile([P, H * PACK // 2], BF16, name="w2_bf1_0", align_bytes=64),
-            late.tile([P, H * PACK // 2], BF16, name="w2_bf1_1", align_bytes=64, offset=0),
-        ]
+        dealt = [late.tile([P, H * PACK], BF16, name=f"w2_bf{z}", align_bytes=64, offset=4096 * (z + 1)) for z in range(2)]
         for i, (z, c0, c1, e) in enumerate(W2_PIECES):
             src = w2_raw[i][:].rearrange("p j (m t) -> p m j t", t=PACK)
             m0, m1 = c0 // PACK, c1 // PACK
-            if z == 0:
-                dst = w2_bf0[:].rearrange("p (t m j) -> p m j t", t=PACK, j=PACK)[:, m0:m1]
-            else:
-                hf = m0 // 64
-                dst = w2_bf1[hf][:].rearrange("p (t m j) -> p m j t", t=PACK, j=PACK)[:, m0 - 64 * hf : m1 - 64 * hf]
+            dst = dealt[z][:].rearrange("p (t m j) -> p m j t", t=PACK, j=PACK)[:, m0:m1]
             ms = e // PACK
-            move("s", dst[:, 0:ms], src[:, 0:ms])
+            if ms > 0:
+                move("s", dst[:, 0:ms], src[:, 0:ms])
             if ms < m1 - m0:
                 move("v", dst[:, ms : m1 - m0], src[:, ms : m1 - m0])
-            if z == 0 and c1 == H:
-                nc.vector.quantize_mx(out=w2_codes[0][:].bitcast(FP8X4), scales=w2_sc[0][:], in_=w2_bf0[:])
-            if z == 1 and m1 % 64 == 0:
-                hf = m0 // 64
+            if c1 == H and z == 0:
+                nc.vector.quantize_mx(out=w2_codes[z][:].bitcast(FP8X4), scales=w2_sc[z][:], in_=dealt[z][:])
+            if c1 == H and z == 1:
                 for t in range(PACK):
-                    cols = slice(t * P + 64 * hf, t * P + 64 * (hf + 1))
-                    nc.vector.quantize_mx(out=w2_codes[1][:, cols].bitcast(FP8X4), scales=w2_sc[1][:, cols], in_=w2_bf1[hf][:, t * 256 : (t + 1) * 256])
-
-        for c in range(GATHER // CHUNK, CHUNKS):
-            for z in range(2):
-                gw = late.tile([P, CHUNK], U32, name=f"xg_late{z}{c}", align_bytes=64, offset=512 * (2 * (c - GATHER // CHUNK) + z))
-                nc.vector.tensor_copy(out=gw[:], in_=x_words[z][:].indirect(offsets[:, c * CHUNK // 16 : (c + 1) * CHUNK // 16]))
-                xg_words[z, c] = gw[:]
+                    cols = slice(t * P, (t + 1) * P)
+                    nc.vector.quantize_mx(out=w2_codes[z][:, cols].bitcast(FP8X4), scales=w2_sc[z][:, cols], in_=dealt[z][:, t * H : (t + 1) * H])
+            if c1 == H and z == 1:
+                gather_words(1, 3, 1, offset=4096 * (z + 1) + 3072)
 
         h_ps = [psum.tile([P, PACK, CHUNK], F32, name=f"h_ps{c}") for c in range(CHUNKS)]
-        o_ps = [psum.tile([P, CHUNK], F32, name=f"o_ps{c}") for c in range(CHUNKS)]
+        o_ps = [psum.tile([P, n * CHUNK], F32, name=f"o_ps{c}") for c, n, e in OUT_GROUPS]
 
-        def h_pass(c, t, z):
+        def h_pass(z, c, t):
+            words, scales = x_operand(z, c, 1)
             cols = slice(t * P, (t + 1) * P)
             nc.tensor.matmul_mx(
                 out=h_ps[c][:, t, :],
                 lhsT=w2_codes[z][:, cols].bitcast(FP8X4),
                 lhsT_scale=w2_sc[z][:, cols],
-                rhs=xg_words[z, c].bitcast(FP8X4),
-                rhs_scale=xg_scales[z, c],
-                start=(z == 0),
-                stop=(z == 1),
+                rhs=words,
+                rhs_scale=scales,
+                start=(z == 0 and t == 0),
+                stop=(z == 1 and t == PACK - 1),
             )
 
-        for i in range(WARM):
-            nc.tensor.matmul_mx(
-                out=o_ps[i % CHUNKS][:],
-                lhsT=xg_words[1, 0].bitcast(FP8X4),
-                lhsT_scale=xg_scales[1, 0],
-                rhs=xg_words[1, 1].bitcast(FP8X4),
-                rhs_scale=xg_scales[1, 1],
-                start=True,
-                stop=True,
-            )
-        for c in range(CHUNKS):
+        def h_first_passes():
+            for c in range(CHUNKS):
+                for t in range(PACK):
+                    h_pass(0, c, t)
+
+        def h_last_passes():
             for t in range(PACK):
-                h_pass(c, t, 0)
-                h_pass(c, t, 1)
-        for c in range(CHUNKS):
-            for z in range(2):
+                for c in range(2):
+                    h_pass(1, c, t)
+            for c in range(2, CHUNKS):
+                for t in range(PACK):
+                    h_pass(1, c, t)
+
+        def w1_passes(z):
+            for g, (c, n, e) in enumerate(OUT_GROUPS):
+                words, scales = x_operand(z, c, n)
                 nc.tensor.matmul_mx(
-                    out=o_ps[c][:],
+                    out=o_ps[g][:],
                     lhsT=w1_w[:, z, :].bitcast(FP8X4),
                     lhsT_scale=w1_sc[:, z * N : (z + 1) * N],
-                    rhs=xg_words[z, c].bitcast(FP8X4),
-                    rhs_scale=xg_scales[z, c],
+                    rhs=words,
+                    rhs_scale=scales,
                     start=(z == 0),
                     stop=False,
                 )
-            h_bf = keep.tile([P, CHUNK * PACK], BF16, name=f"h_bf{c}", align_bytes=64)
-            nc.scalar.activation(out=h_bf[:].rearrange("p (n t) -> p n t", t=PACK), in_=h_ps[c][:].rearrange("p t n -> p n t"), func=RELU)
-            h_words = keep.tile([P, CHUNK], U32, name=f"h_words{c}", align_bytes=64)
-            h_sc = keep.tile([P, CHUNK], U8, name=f"h_sc{c}", align_bytes=64)
-            nc.vector.quantize_mx(out=h_words[:].bitcast(FP8X4), scales=h_sc[:], in_=h_bf[:])
+
+        def warm_up():
+            for i, n in enumerate(WARM):
+                words, scales = x_operand(0, 0, n)
+                nc.tensor.matmul_mx(
+                    out=h_ps[i][:, 0:n, :].rearrange("p t n -> p (t n)"),
+                    lhsT=x_operand(0, 0, 1)[0],
+                    lhsT_scale=x_operand(0, 0, 1)[1],
+                    rhs=words,
+                    rhs_scale=scales,
+                    start=True,
+                    stop=True,
+                )
+
+        warm_up()
+        h_first_passes()
+        h_last_passes()
+        w1_passes(0)
+        w1_passes(1)
+
+        h_bf = {}
+        for c, n, e in OUT_GROUPS:
+            h_bf[c] = keep.tile([P, n * CHUNK * PACK], BF16, name=f"h_bf{c}", align_bytes=64)
+            for i in range(n):
+                dst = h_bf[c][:, i * CHUNK * PACK : (i + 1) * CHUNK * PACK].rearrange("p (n t) -> p n t", t=PACK)
+                src = h_ps[c + i][:].rearrange("p t n -> p n t")
+                if RELU_ON[c + i] == "s":
+                    nc.scalar.activation(out=dst, in_=src, func=RELU)
+                else:
+                    nc.vector.tensor_scalar_max(out=dst, in0=src, scalar1=0.0)
+        for g, (c, n, e) in enumerate(OUT_GROUPS):
+            h_words = keep.tile([P, n * CHUNK], U32, name=f"h_words{c}", align_bytes=64)
+            h_sc = keep.tile([P, n * CHUNK], U8, name=f"h_sc{c}", align_bytes=64)
+            nc.vector.quantize_mx(out=h_words[:].bitcast(FP8X4), scales=h_sc[:], in_=h_bf[c][:])
             nc.tensor.matmul_mx(
-                out=o_ps[c][:],
+                out=o_ps[g][:],
                 lhsT=w3_w[:].bitcast(FP8X4),
                 lhsT_scale=w3_sc[:],
                 rhs=h_words[:].bitcast(FP8X4),
@@ -194,6 +251,6 @@ def tile_picked_lora_relu_e_kernel(tc, xT, w1_words, w1_scales, w2, w3_words, w3
                 start=False,
                 stop=True,
             )
-            res = keep.tile([P, CHUNK], F32, name=f"res{c}")
-            nc.vector.tensor_copy(out=res[:], in_=o_ps[c][:])
-            nc.sync.dma_start(out=out[:, c * CHUNK : (c + 1) * CHUNK], in_=res[:])
+            res = keep.tile([P, n * CHUNK], F32, name=f"res{c}")
+            move(e, res[:], o_ps[g][:])
+            nc.sync.dma_start(out=out[:, c * CHUNK : (c + n) * CHUNK], in_=res[:])

@@ -20,16 +20,9 @@ PACK = 4
 K_PASS = P * PACK
 CHUNK = 128
 CHUNKS = S // CHUNK
-PLANE_STEP = 4
+HALF = S // 2
 
-X_PIECES = [
-    (0, 0, 512, (("s", 256), ("v", 256))),
-    (0, 512, 1024, (("v", 256), ("s", 128), ("v", 128))),
-    (1, 0, 512, (("s", 256), ("v", 256))),
-    (1, 512, 768, (("s", 256),)),
-    (1, 768, 1024, (("v", 128), ("s", 128))),
-]
-W2_PIECES = [(0, 0, 256, 256), (0, 256, 512, 256), (1, 0, 256, 256), (1, 256, 512, 80)]
+X_SHARES = (352, 384, 432, 432)
 RELU_ON = "vsvs"
 OUT_GROUPS = [(0, 2, "s"), (2, 1, "v"), (3, 1, "s")]
 WARM = (4, 4, 2, 1)
@@ -50,125 +43,123 @@ def tile_picked_lora_relu_e_kernel(tc, xT, w1_words, w1_scales, w2, w3_words, w3
         psum = ctx.enter_context(tc.psum_pool(name="psum", bufs=1))
 
         offsets = keep.tile([P, S // 16], U16, name="offsets")
-        x_scales = late.tile([P, T], U8, name="x_scales", align_bytes=64, offset=0)
         w1_sc = keep.tile([P, 2 * N], U8, name="w1_sc", align_bytes=64)
         w3_sc = keep.tile([P, N], U8, name="w3_sc", align_bytes=64)
         nc.vector.memset(w1_sc[:].bitcast(I32), 0)
         nc.vector.memset(w3_sc[:].bitcast(I32), 0)
-        nc.vector.memset(x_scales[:].bitcast(I32), 0)
 
         x_raw = {}
-        w2_raw = {}
+        for z in range(2):
+            rows = xT[z * K_PASS : (z + 1) * K_PASS, :].rearrange("(p j) t -> p j t", j=PACK)
+            for u in range(2):
+                x_raw[z, u] = late.tile([P, 2, T], F32, name=f"x_raw{z}{u}", align_bytes=64, offset=8192 * (2 * z + u))
+                nc.sync.dma_start(out=x_raw[z, u][:], in_=rows[:, 2 * u : 2 * u + 2, :])
+                if z == 0 and u == 0:
+                    nc.sync.dma_start(offsets[:], offs)
+        w2_raw = []
+        for z in range(2):
+            raw = keep.tile([P, PACK, H], F32, name=f"w2_raw{z}")
+            nc.sync.dma_start(out=raw[:], in_=w2[z * K_PASS : (z + 1) * K_PASS, :].rearrange("(p j) c -> p j c", j=PACK))
+            w2_raw.append(raw)
         w1_w = keep.tile([P, 2, N], I32, name="w1_w", align_bytes=64)
         w3_w = keep.tile([P, N], I32, name="w3_w", align_bytes=64)
+        nc.sync.dma_start(out=w1_w[:], in_=w1_words.rearrange("z p n t -> p z (n t)").bitcast(I32))
+        w1_rows = w1_scales.rearrange("z (q r) n -> r q z n", r=4)
+        for r in range(4):
+            nc.sync.dma_start(out=w1_sc[r:P:32, :].bitcast(I32).rearrange("q (z n) -> q z n", z=2), in_=w1_rows[r].bitcast(I32))
+        nc.sync.dma_start(out=w3_w[:], in_=w3_words[0].rearrange("p n t -> p (n t)").bitcast(I32))
+        w3_rows = w3_scales[0].rearrange("(q r) n -> r q n", r=4)
+        for r in range(4):
+            nc.sync.dma_start(out=w3_sc[r:P:32, :].bitcast(I32), in_=w3_rows[r].bitcast(I32))
 
-        def load_x(i):
-            z, t0, t1, parts = X_PIECES[i]
-            x_raw[i] = keep.tile([P, PACK, t1 - t0], F32, name=f"x_raw{i}")
-            nc.sync.dma_start(out=x_raw[i][:], in_=xT[z * K_PASS : (z + 1) * K_PASS, t0:t1].rearrange("(p j) t -> p j t", j=PACK))
+        pairs = {}
+        flat = {}
+        woven = {}
+        x_words = [keep.tile([P, S], U32, name=f"x_words{z}", align_bytes=64) for z in range(2)]
+        x_scales = [keep.tile([P, S], U8, name=f"x_scales{z}", align_bytes=64) for z in range(2)]
 
-        def load_w2(i):
-            z, c0, c1, share = W2_PIECES[i]
-            w2_raw[i] = keep.tile([P, PACK, c1 - c0], F32, name=f"w2_raw{i}")
-            nc.sync.dma_start(out=w2_raw[i][:], in_=w2[z * K_PASS : (z + 1) * K_PASS, c0:c1].rearrange("(p j) c -> p j c", j=PACK))
-
-        def load_list():
-            nc.sync.dma_start(offsets[:], offs)
-
-        def load_w1_words():
-            nc.sync.dma_start(out=w1_w[:], in_=w1_words.rearrange("z p n t -> p z (n t)").bitcast(I32))
-
-        def load_w1_scales():
-            w1_rows = w1_scales.rearrange("z (q r) n -> r q z n", r=4)
-            for r in range(4):
-                nc.sync.dma_start(out=w1_sc[r:P:32, :].bitcast(I32).rearrange("q (z n) -> q z n", z=2), in_=w1_rows[r].bitcast(I32))
-
-        def load_w3_words():
-            nc.sync.dma_start(out=w3_w[:], in_=w3_words[0].rearrange("p n t -> p (n t)").bitcast(I32))
-
-        def load_w3_scales():
-            w3_rows = w3_scales[0].rearrange("(q r) n -> r q n", r=4)
-            for r in range(4):
-                nc.sync.dma_start(out=w3_sc[r:P:32, :].bitcast(I32), in_=w3_rows[r].bitcast(I32))
-
-        load_x(0)
-        load_list()
-        load_x(1)
-        load_x(2)
-        load_x(3)
-        load_x(4)
-        load_w2(0)
-        load_w2(1)
-        load_w2(2)
-        load_w2(3)
-        load_w1_words()
-        load_w1_scales()
-        load_w3_words()
-        load_w3_scales()
-
-        x_words = [keep.tile([P, T], U32, name=f"x_words{z}", align_bytes=64) for z in range(2)]
-        xg_words = {}
-        xg_scales = keep.tile([P, S], U8, name="xg_scales", align_bytes=64)
-
-        def gather_words(z, first, count, offset=None):
-            if offset is None:
-                gw = keep.tile([P, count * CHUNK], U32, name=f"xg_words{z}_{first}", align_bytes=64)
-            else:
-                gw = late.tile([P, count * CHUNK], U32, name=f"xg_words{z}_{first}", align_bytes=64, offset=offset)
-            nc.vector.tensor_copy(out=gw[:], in_=x_words[z][:].indirect(offsets[:, first * CHUNK // 16 : (first + count) * CHUNK // 16]))
-            for c in range(count):
-                xg_words[z, first + c] = (gw, c * CHUNK)
-
-        def x_operand(z, first, count):
-            gw, a = xg_words[z, first]
-            return gw[:, a : a + count * CHUNK].bitcast(FP8X4), xg_scales[PLANE_STEP * z : P, first * CHUNK : (first + count) * CHUNK]
-
-        for i, (z, t0, t1, ts) in enumerate(X_PIECES):
-            a = 0
-            parts = []
-            for e, n in ts:
-                grouped = keep.tile([P, n * PACK], BF16, name=f"x_bf{i}_{a}", align_bytes=64)
+        def round_pairs(z, u):
+            pairs[z, u] = keep.tile([P, T], U32, name=f"pairs{z}{u}", align_bytes=64)
+            share = X_SHARES[2 * z + u]
+            for e, a, b in (("s", 0, share), ("v", share, T)):
                 move(
                     e,
-                    grouped[:].rearrange("p (c i j) -> p c j i", i=4, j=PACK),
-                    x_raw[i][:, :, a : a + n].rearrange("p j (c i) -> p c j i", i=4),
+                    pairs[z, u][:, a:b].bitcast(BF16).rearrange("p (c i e) -> p c e i", i=4, e=2),
+                    x_raw[z, u][:, :, a:b].rearrange("p e (c i) -> p c e i", i=4),
                 )
-                parts.append((grouped, t0 + a, n))
-                a += n
-            for grouped, b, n in parts:
-                nc.vector.quantize_mx(
-                    out=x_words[z][:, b : b + n].bitcast(FP8X4),
-                    scales=x_scales[PLANE_STEP * z : P, b : b + n],
-                    in_=grouped[:],
+
+        def gather(z, u, a, b):
+            if (z, u) not in flat:
+                flat[z, u] = keep.tile([P, 2, S], U32, name=f"flat{z}", align_bytes=64) if u == 0 else flat[z, 0]
+            nc.vector.tensor_copy(out=flat[z, u][:, u, a:b], in_=pairs[z, u][:].indirect(offsets[:, a // 16 : b // 16]))
+
+        def weave(e, z, a, b, offset=None):
+            if offset is None:
+                woven[z, a] = keep.tile([P, b - a, 2], U32, name=f"woven{z}_{a}", align_bytes=64)
+            else:
+                woven[z, a] = late.tile([P, b - a, 2], U32, name=f"woven{z}_{a}", align_bytes=64, offset=offset)
+            if e == "s":
+                nc.scalar.copy(out=woven[z, a][:], in_=flat[z, 0][:, :, a:b].rearrange("p u s -> p s u"))
+            else:
+                nc.vector.tensor_copy(
+                    out=woven[z, a][:].rearrange("p s u -> p (s u)").bitcast(BF16).rearrange("p (s u e) -> p s u e", u=2, e=2),
+                    in_=flat[z, 0][:, :, a:b].bitcast(BF16).rearrange("p u (s e) -> p s u e", e=2),
                 )
-            if t1 == T and z == 0:
-                gather_words(0, 0, CHUNKS)
-        nc.vector.tensor_copy(out=xg_scales[:], in_=x_scales[:].indirect(offsets[:]))
-        gather_words(1, 0, 3, offset=0)
+
+        def quantise_x(z, a, b):
+            nc.vector.quantize_mx(
+                out=x_words[z][:, a:b].bitcast(FP8X4),
+                scales=x_scales[z][:, a:b],
+                in_=woven[z, a][:].rearrange("p s u -> p (s u)").bitcast(BF16),
+            )
 
         w2_codes = [keep.tile([P, H], U32, name=f"w2_codes{z}", align_bytes=64) for z in range(2)]
         w2_sc = [keep.tile([P, H], U8, name=f"w2_sc{z}", align_bytes=64) for z in range(2)]
-        dealt = [late.tile([P, H * PACK], BF16, name=f"w2_bf{z}", align_bytes=64, offset=4096 * (z + 1)) for z in range(2)]
-        for i, (z, c0, c1, e) in enumerate(W2_PIECES):
-            src = w2_raw[i][:].rearrange("p j (m t) -> p m j t", t=PACK)
-            m0, m1 = c0 // PACK, c1 // PACK
-            dst = dealt[z][:].rearrange("p (t m j) -> p m j t", t=PACK, j=PACK)[:, m0:m1]
-            ms = e // PACK
-            if ms > 0:
-                move("s", dst[:, 0:ms], src[:, 0:ms])
-            if ms < m1 - m0:
-                move("v", dst[:, ms : m1 - m0], src[:, ms : m1 - m0])
-            if c1 == H and z == 0:
-                nc.vector.quantize_mx(out=w2_codes[z][:].bitcast(FP8X4), scales=w2_sc[z][:], in_=dealt[z][:])
-            if c1 == H and z == 1:
-                for t in range(PACK):
-                    cols = slice(t * P, (t + 1) * P)
-                    nc.vector.quantize_mx(out=w2_codes[z][:, cols].bitcast(FP8X4), scales=w2_sc[z][:, cols], in_=dealt[z][:, t * H : (t + 1) * H])
-            if c1 == H and z == 1:
-                gather_words(1, 3, 1, offset=4096 * (z + 1) + 3072)
+        dealt = {}
+
+        def round_w2(e, z, t0, t1):
+            dealt[z, t0] = keep.tile([P, (t1 - t0) * H], BF16, name=f"w2_bf{z}{t0}", align_bytes=64)
+            src = w2_raw[z][:].rearrange("p j (m t) -> p m j t", t=PACK)[:, :, :, t0:t1]
+            move(e, dealt[z, t0][:].rearrange("p (t m j) -> p m j t", t=t1 - t0, j=PACK), src)
+
+        def quantise_w2(z, base, t0, t1):
+            cols = slice(t0 * P, t1 * P)
+            nc.vector.quantize_mx(out=w2_codes[z][:, cols].bitcast(FP8X4), scales=w2_sc[z][:, cols], in_=dealt[z, base][:, (t0 - base) * H : (t1 - base) * H])
+
+        round_pairs(0, 0)
+        gather(0, 0, 0, S)
+        round_pairs(0, 1)
+        gather(0, 1, 0, S)
+        round_pairs(1, 0)
+        gather(1, 0, 0, S)
+        weave("s", 0, 0, HALF, offset=8192 * 2)
+        round_pairs(1, 1)
+        quantise_x(0, 0, HALF)
+        weave("s", 0, HALF, S, offset=8192 * 3)
+        gather(1, 1, 0, HALF)
+        quantise_x(0, HALF, S)
+        gather(1, 1, HALF, S)
+        round_w2("s", 0, 0, 2)
+        quantise_w2(0, 0, 0, 2)
+        weave("v", 1, 0, HALF)
+        weave("v", 1, HALF, S)
+        quantise_x(1, 0, HALF)
+        quantise_x(1, HALF, S)
+        round_w2("s", 0, 2, 4)
+        round_w2("v", 1, 2, 4)
+        quantise_w2(0, 2, 2, 4)
+        round_w2("s", 1, 0, 2)
+        quantise_w2(1, 2, 2, 3)
+        quantise_w2(1, 2, 3, 4)
+        quantise_w2(1, 0, 0, 1)
+        quantise_w2(1, 0, 1, 2)
 
         h_ps = [psum.tile([P, PACK, CHUNK], F32, name=f"h_ps{c}") for c in range(CHUNKS)]
         o_ps = [psum.tile([P, n * CHUNK], F32, name=f"o_ps{c}") for c, n, e in OUT_GROUPS]
+
+        def x_operand(z, first, count):
+            tokens = slice(first * CHUNK, (first + count) * CHUNK)
+            return x_words[z][:, tokens].bitcast(FP8X4), x_scales[z][:, tokens]
 
         def h_pass(z, c, t):
             words, scales = x_operand(z, c, 1)
@@ -180,23 +171,31 @@ def tile_picked_lora_relu_e_kernel(tc, xT, w1_words, w1_scales, w2, w3_words, w3
                 rhs=words,
                 rhs_scale=scales,
                 start=(z == 0 and t == 0),
-                stop=(z == 1 and t == PACK - 1),
+                stop=(z == 1 and t == 1),
             )
 
-        def h_first_passes():
+        for i, n in enumerate(WARM):
+            words, scales = x_operand(0, 0, n)
+            nc.tensor.matmul_mx(
+                out=h_ps[i][:, 0:n, :].rearrange("p t n -> p (t n)"),
+                lhsT=x_operand(0, 3, 1)[0],
+                lhsT_scale=x_operand(0, 3, 1)[1],
+                rhs=words,
+                rhs_scale=scales,
+                start=True,
+                stop=True,
+            )
+        for half in range(2):
             for c in range(CHUNKS):
-                for t in range(PACK):
+                for t in range(2 * half, 2 * half + 2):
                     h_pass(0, c, t)
-
-        def h_last_passes():
-            for t in range(PACK):
-                for c in range(2):
-                    h_pass(1, c, t)
-            for c in range(2, CHUNKS):
-                for t in range(PACK):
-                    h_pass(1, c, t)
-
-        def w1_passes(z):
+        for t in (2, 3, 0, 1):
+            for c in range(2):
+                h_pass(1, c, t)
+        for c in range(2, CHUNKS):
+            for t in (2, 3, 0, 1):
+                h_pass(1, c, t)
+        for z in range(2):
             for g, (c, n, e) in enumerate(OUT_GROUPS):
                 words, scales = x_operand(z, c, n)
                 nc.tensor.matmul_mx(
@@ -208,25 +207,6 @@ def tile_picked_lora_relu_e_kernel(tc, xT, w1_words, w1_scales, w2, w3_words, w3
                     start=(z == 0),
                     stop=False,
                 )
-
-        def warm_up():
-            for i, n in enumerate(WARM):
-                words, scales = x_operand(0, 0, n)
-                nc.tensor.matmul_mx(
-                    out=h_ps[i][:, 0:n, :].rearrange("p t n -> p (t n)"),
-                    lhsT=x_operand(0, 0, 1)[0],
-                    lhsT_scale=x_operand(0, 0, 1)[1],
-                    rhs=words,
-                    rhs_scale=scales,
-                    start=True,
-                    stop=True,
-                )
-
-        warm_up()
-        h_first_passes()
-        h_last_passes()
-        w1_passes(0)
-        w1_passes(1)
 
         h_bf = {}
         for c, n, e in OUT_GROUPS:

@@ -25,7 +25,7 @@ HALF = S // 2
 X_SHARES = (352, 384, 432, 432)
 RELU_ON = "vsvs"
 OUT_GROUPS = [(0, 2, "s"), (2, 1, "v"), (3, 1, "s")]
-WARM = (4, 4, 2, 1)
+WARM = (2, 2, 2, 2)
 
 
 def tile_picked_lora_relu_e_kernel(tc, xT, w1_words, w1_scales, w2, w3_words, w3_scales, offs, out):
@@ -56,17 +56,16 @@ def tile_picked_lora_relu_e_kernel(tc, xT, w1_words, w1_scales, w2, w3_words, w3
                 nc.sync.dma_start(out=x_raw[z, u][:], in_=rows[:, 2 * u : 2 * u + 2, :])
                 if z == 0 and u == 0:
                     nc.sync.dma_start(offsets[:], offs)
-        w2_raw = []
-        for z in range(2):
-            raw = keep.tile([P, PACK, H], F32, name=f"w2_raw{z}")
-            nc.sync.dma_start(out=raw[:], in_=w2[z * K_PASS : (z + 1) * K_PASS, :].rearrange("(p j) c -> p j c", j=PACK))
-            w2_raw.append(raw)
         w1_w = keep.tile([P, 2, N], I32, name="w1_w", align_bytes=64)
         w3_w = keep.tile([P, N], I32, name="w3_w", align_bytes=64)
-        nc.sync.dma_start(out=w1_w[:], in_=w1_words.rearrange("z p n t -> p z (n t)").bitcast(I32))
-        w1_rows = w1_scales.rearrange("z (q r) n -> r q z n", r=4)
-        for r in range(4):
-            nc.sync.dma_start(out=w1_sc[r:P:32, :].bitcast(I32).rearrange("q (z n) -> q z n", z=2), in_=w1_rows[r].bitcast(I32))
+        w2_raw = [keep.tile([P, PACK, H], F32, name=f"w2_raw{z}") for z in range(2)]
+        for z in range(2):
+            nc.sync.dma_start(out=w2_raw[z][:], in_=w2[z * K_PASS : (z + 1) * K_PASS, :].rearrange("(p j) c -> p j c", j=PACK))
+            if z == 0:
+                nc.sync.dma_start(out=w1_w[:], in_=w1_words.rearrange("z p n t -> p z (n t)").bitcast(I32))
+                w1_rows = w1_scales.rearrange("z (q r) n -> r q z n", r=4)
+                for r in range(4):
+                    nc.sync.dma_start(out=w1_sc[r:P:32, :].bitcast(I32).rearrange("q (z n) -> q z n", z=2), in_=w1_rows[r].bitcast(I32))
         nc.sync.dma_start(out=w3_w[:], in_=w3_words[0].rearrange("p n t -> p (n t)").bitcast(I32))
         w3_rows = w3_scales[0].rearrange("(q r) n -> r q n", r=4)
         for r in range(4):
@@ -149,13 +148,11 @@ def tile_picked_lora_relu_e_kernel(tc, xT, w1_words, w1_scales, w2, w3_words, w3
         round_w2("v", 1, 2, 4)
         quantise_w2(0, 2, 2, 4)
         round_w2("s", 1, 0, 2)
-        quantise_w2(1, 2, 2, 3)
-        quantise_w2(1, 2, 3, 4)
-        quantise_w2(1, 0, 0, 1)
-        quantise_w2(1, 0, 1, 2)
+        quantise_w2(1, 2, 2, 4)
+        quantise_w2(1, 0, 0, 2)
 
-        h_ps = [psum.tile([P, PACK, CHUNK], F32, name=f"h_ps{c}") for c in range(CHUNKS)]
-        o_ps = [psum.tile([P, n * CHUNK], F32, name=f"o_ps{c}") for c, n, e in OUT_GROUPS]
+        h_ps = [psum.tile([P, PACK, CHUNK], F32, name=f"h_ps{c}", offset=2048 * c) for c in range(CHUNKS)]
+        o_ps = [psum.tile([P, n * CHUNK], F32, name=f"o_ps{c}", offset=(0 if c == 0 else 2048 * (c + 2))) for c, n, e in OUT_GROUPS]
 
         def x_operand(z, first, count):
             tokens = slice(first * CHUNK, (first + count) * CHUNK)
@@ -174,29 +171,9 @@ def tile_picked_lora_relu_e_kernel(tc, xT, w1_words, w1_scales, w2, w3_words, w3
                 stop=(z == 1 and t == 1),
             )
 
-        for i, n in enumerate(WARM):
-            words, scales = x_operand(0, 0, n)
-            nc.tensor.matmul_mx(
-                out=h_ps[i][:, 0:n, :].rearrange("p t n -> p (t n)"),
-                lhsT=x_operand(0, 3, 1)[0],
-                lhsT_scale=x_operand(0, 3, 1)[1],
-                rhs=words,
-                rhs_scale=scales,
-                start=True,
-                stop=True,
-            )
-        for half in range(2):
-            for c in range(CHUNKS):
-                for t in range(2 * half, 2 * half + 2):
-                    h_pass(0, c, t)
-        for t in (2, 3, 0, 1):
-            for c in range(2):
-                h_pass(1, c, t)
-        for c in range(2, CHUNKS):
-            for t in (2, 3, 0, 1):
-                h_pass(1, c, t)
-        for z in range(2):
-            for g, (c, n, e) in enumerate(OUT_GROUPS):
+        def w1_passes(z, groups):
+            for g in groups:
+                c, n, e = OUT_GROUPS[g]
                 words, scales = x_operand(z, c, n)
                 nc.tensor.matmul_mx(
                     out=o_ps[g][:],
@@ -207,6 +184,26 @@ def tile_picked_lora_relu_e_kernel(tc, xT, w1_words, w1_scales, w2, w3_words, w3
                     start=(z == 0),
                     stop=False,
                 )
+
+        for i, n in enumerate(WARM):
+            words, scales = x_operand(0, 0, n)
+            nc.tensor.matmul_mx(
+                out=h_ps[i][:, 0:n, :].rearrange("p t n -> p (t n)"),
+                lhsT=w1_w[:, 0, :].bitcast(FP8X4),
+                lhsT_scale=w1_sc[:, 0:N],
+                rhs=words,
+                rhs_scale=scales,
+                start=True,
+                stop=True,
+            )
+        w1_passes(0, (1, 2))
+        w1_passes(1, (1, 2))
+        for z, pair in ((0, 0), (0, 2), (1, 2), (1, 0)):
+            for c in range(CHUNKS):
+                for t in (pair, pair + 1):
+                    h_pass(z, c, t)
+        w1_passes(0, (0,))
+        w1_passes(1, (0,))
 
         h_bf = {}
         for c, n, e in OUT_GROUPS:

@@ -25,7 +25,7 @@ HALF = S // 2
 X_SHARES = (352, 384, 432, 432)
 RELU_ON = "vsvs"
 OUT_GROUPS = [(0, 2, "s"), (2, 1, "v"), (3, 1, "s")]
-WARM = (2, 2, 2, 2)
+WARM = (2, 2, 2, 4)
 
 
 def tile_picked_lora_relu_e_kernel(tc, xT, w1_words, w1_scales, w2, w3_words, w3_scales, offs, out):
@@ -45,9 +45,12 @@ def tile_picked_lora_relu_e_kernel(tc, xT, w1_words, w1_scales, w2, w3_words, w3
         offsets = keep.tile([P, S // 16], U16, name="offsets")
         w1_sc = keep.tile([P, 2 * N], U8, name="w1_sc", align_bytes=64)
         w3_sc = keep.tile([P, N], U8, name="w3_sc", align_bytes=64)
-        nc.vector.memset(w1_sc[:].bitcast(I32), 0)
         nc.vector.memset(w3_sc[:].bitcast(I32), 0)
+        nc.vector.memset(w1_sc[:].bitcast(I32), 0)
 
+        w3_rows = w3_scales[0].rearrange("(q r) n -> r q n", r=4)
+        for r in range(4):
+            nc.scalar.dma_start(out=w3_sc[r:P:32, :].bitcast(I32), in_=w3_rows[r].bitcast(I32))
         x_raw = {}
         for z in range(2):
             rows = xT[z * K_PASS : (z + 1) * K_PASS, :].rearrange("(p j) t -> p j t", j=PACK)
@@ -60,16 +63,16 @@ def tile_picked_lora_relu_e_kernel(tc, xT, w1_words, w1_scales, w2, w3_words, w3
         w3_w = keep.tile([P, N], I32, name="w3_w", align_bytes=64)
         w2_raw = [keep.tile([P, PACK, H], F32, name=f"w2_raw{z}") for z in range(2)]
         for z in range(2):
-            nc.sync.dma_start(out=w2_raw[z][:], in_=w2[z * K_PASS : (z + 1) * K_PASS, :].rearrange("(p j) c -> p j c", j=PACK))
+            run = w2[z * K_PASS : (z + 1) * K_PASS, :].rearrange("(p j) c -> p (j c)", j=PACK)
+            cuts = (0, PACK * H) if z == 0 else (0, PACK * H - H // 2, PACK * H)
+            for a, b in zip(cuts, cuts[1:]):
+                nc.sync.dma_start(out=w2_raw[z][:].rearrange("p j c -> p (j c)")[:, a:b], in_=run[:, a:b])
             if z == 0:
-                nc.sync.dma_start(out=w1_w[:], in_=w1_words.rearrange("z p n t -> p z (n t)").bitcast(I32))
-                w1_rows = w1_scales.rearrange("z (q r) n -> r q z n", r=4)
-                for r in range(4):
-                    nc.sync.dma_start(out=w1_sc[r:P:32, :].bitcast(I32).rearrange("q (z n) -> q z n", z=2), in_=w1_rows[r].bitcast(I32))
-        nc.sync.dma_start(out=w3_w[:], in_=w3_words[0].rearrange("p n t -> p (n t)").bitcast(I32))
-        w3_rows = w3_scales[0].rearrange("(q r) n -> r q n", r=4)
+                nc.sync.dma_start(out=w3_w[:], in_=w3_words[0].rearrange("p n t -> p (n t)").bitcast(I32))
+        nc.sync.dma_start(out=w1_w[:], in_=w1_words.rearrange("z p n t -> p z (n t)").bitcast(I32))
+        w1_rows = w1_scales.rearrange("z (q r) n -> r q z n", r=4)
         for r in range(4):
-            nc.sync.dma_start(out=w3_sc[r:P:32, :].bitcast(I32), in_=w3_rows[r].bitcast(I32))
+            nc.sync.dma_start(out=w1_sc[r:P:32, :].bitcast(I32).rearrange("q (z n) -> q z n", z=2), in_=w1_rows[r].bitcast(I32))
 
         pairs = {}
         flat = {}
@@ -116,14 +119,20 @@ def tile_picked_lora_relu_e_kernel(tc, xT, w1_words, w1_scales, w2, w3_words, w3
         w2_sc = [keep.tile([P, H], U8, name=f"w2_sc{z}", align_bytes=64) for z in range(2)]
         dealt = {}
 
-        def round_w2(e, z, t0, t1):
-            dealt[z, t0] = keep.tile([P, (t1 - t0) * H], BF16, name=f"w2_bf{z}{t0}", align_bytes=64)
-            src = w2_raw[z][:].rearrange("p j (m t) -> p m j t", t=PACK)[:, :, :, t0:t1]
-            move(e, dealt[z, t0][:].rearrange("p (t m j) -> p m j t", t=t1 - t0, j=PACK), src)
+        def round_w2(e, z, t0, t1, m0=0, m1=P):
+            dealt[z, t0, m0] = keep.tile([P, (t1 - t0) * (m1 - m0) * PACK], BF16, name=f"w2_bf{z}{t0}_{m0}", align_bytes=64)
+            src = w2_raw[z][:].rearrange("p j (m t) -> p m j t", t=PACK)[:, m0:m1, :, t0:t1]
+            move(e, dealt[z, t0, m0][:].rearrange("p (t m j) -> p m j t", t=t1 - t0, j=PACK), src)
 
-        def quantise_w2(z, base, t0, t1):
-            cols = slice(t0 * P, t1 * P)
-            nc.vector.quantize_mx(out=w2_codes[z][:, cols].bitcast(FP8X4), scales=w2_sc[z][:, cols], in_=dealt[z, base][:, (t0 - base) * H : (t1 - base) * H])
+        def quantise_w2(z, t0, t1, m0=0, m1=P):
+            if m1 - m0 == P:
+                cols = slice(t0 * P, t1 * P)
+                nc.vector.quantize_mx(out=w2_codes[z][:, cols].bitcast(FP8X4), scales=w2_sc[z][:, cols], in_=dealt[z, t0, 0][:])
+            else:
+                width = (m1 - m0) * PACK
+                for t in range(t0, t1):
+                    cols = slice(t * P + m0, t * P + m1)
+                    nc.vector.quantize_mx(out=w2_codes[z][:, cols].bitcast(FP8X4), scales=w2_sc[z][:, cols], in_=dealt[z, t0, m0][:, (t - t0) * width : (t - t0 + 1) * width])
 
         round_pairs(0, 0)
         gather(0, 0, 0, S)
@@ -139,17 +148,19 @@ def tile_picked_lora_relu_e_kernel(tc, xT, w1_words, w1_scales, w2, w3_words, w3
         quantise_x(0, HALF, S)
         gather(1, 1, HALF, S)
         round_w2("s", 0, 0, 2)
-        quantise_w2(0, 0, 0, 2)
+        quantise_w2(0, 0, 2)
         weave("v", 1, 0, HALF)
         weave("v", 1, HALF, S)
         quantise_x(1, 0, HALF)
         quantise_x(1, HALF, S)
         round_w2("s", 0, 2, 4)
         round_w2("v", 1, 2, 4)
-        quantise_w2(0, 2, 2, 4)
-        round_w2("s", 1, 0, 2)
-        quantise_w2(1, 2, 2, 4)
-        quantise_w2(1, 0, 0, 2)
+        quantise_w2(0, 2, 4)
+        round_w2("s", 1, 0, 2, 0, 64)
+        round_w2("s", 1, 0, 2, 64, 128)
+        quantise_w2(1, 2, 4)
+        quantise_w2(1, 0, 2, 0, 64)
+        quantise_w2(1, 0, 2, 64, 128)
 
         h_ps = [psum.tile([P, PACK, CHUNK], F32, name=f"h_ps{c}", offset=2048 * c) for c in range(CHUNKS)]
         o_ps = [psum.tile([P, n * CHUNK], F32, name=f"o_ps{c}", offset=(0 if c == 0 else 2048 * (c + 2))) for c, n, e in OUT_GROUPS]
@@ -189,21 +200,20 @@ def tile_picked_lora_relu_e_kernel(tc, xT, w1_words, w1_scales, w2, w3_words, w3
             words, scales = x_operand(0, 0, n)
             nc.tensor.matmul_mx(
                 out=h_ps[i][:, 0:n, :].rearrange("p t n -> p (t n)"),
-                lhsT=w1_w[:, 0, :].bitcast(FP8X4),
-                lhsT_scale=w1_sc[:, 0:N],
+                lhsT=w3_w[:].bitcast(FP8X4),
+                lhsT_scale=w3_sc[:],
                 rhs=words,
                 rhs_scale=scales,
                 start=True,
                 stop=True,
             )
-        w1_passes(0, (1, 2))
-        w1_passes(1, (1, 2))
         for z, pair in ((0, 0), (0, 2), (1, 2), (1, 0)):
             for c in range(CHUNKS):
                 for t in (pair, pair + 1):
                     h_pass(z, c, t)
-        w1_passes(0, (0,))
-        w1_passes(1, (0,))
+        for g in range(len(OUT_GROUPS)):
+            w1_passes(0, (g,))
+            w1_passes(1, (g,))
 
         h_bf = {}
         for c, n, e in OUT_GROUPS:

@@ -25,7 +25,6 @@ HALF = S // 2
 X_SHARES = (352, 384, 432, 432)
 RELU_ON = "vsvs"
 OUT_GROUPS = [(0, 2, "s"), (2, 1, "v"), (3, 1, "s")]
-WARM = (2, 2, 2, 4)
 
 
 def tile_picked_lora_relu_e_kernel(tc, xT, w1_words, w1_scales, w2, w3_words, w3_scales, offs, out):
@@ -45,12 +44,12 @@ def tile_picked_lora_relu_e_kernel(tc, xT, w1_words, w1_scales, w2, w3_words, w3
         offsets = keep.tile([P, S // 16], U16, name="offsets")
         w1_sc = keep.tile([P, 2 * N], U8, name="w1_sc", align_bytes=64)
         w3_sc = keep.tile([P, N], U8, name="w3_sc", align_bytes=64)
-        nc.vector.memset(w3_sc[:].bitcast(I32), 0)
         nc.vector.memset(w1_sc[:].bitcast(I32), 0)
+        nc.vector.memset(w3_sc[:].bitcast(I32), 0)
 
-        w3_rows = w3_scales[0].rearrange("(q r) n -> r q n", r=4)
+        w1_rows = w1_scales.rearrange("z (q r) n -> r q z n", r=4)
         for r in range(4):
-            nc.scalar.dma_start(out=w3_sc[r:P:32, :].bitcast(I32), in_=w3_rows[r].bitcast(I32))
+            nc.scalar.dma_start(out=w1_sc[r:P:32, :].bitcast(I32).rearrange("q (z n) -> q z n", z=2), in_=w1_rows[r].bitcast(I32))
         x_raw = {}
         for z in range(2):
             rows = xT[z * K_PASS : (z + 1) * K_PASS, :].rearrange("(p j) t -> p j t", j=PACK)
@@ -68,11 +67,11 @@ def tile_picked_lora_relu_e_kernel(tc, xT, w1_words, w1_scales, w2, w3_words, w3
             for a, b in zip(cuts, cuts[1:]):
                 nc.sync.dma_start(out=w2_raw[z][:].rearrange("p j c -> p (j c)")[:, a:b], in_=run[:, a:b])
             if z == 0:
-                nc.sync.dma_start(out=w3_w[:], in_=w3_words[0].rearrange("p n t -> p (n t)").bitcast(I32))
-        nc.sync.dma_start(out=w1_w[:], in_=w1_words.rearrange("z p n t -> p z (n t)").bitcast(I32))
-        w1_rows = w1_scales.rearrange("z (q r) n -> r q z n", r=4)
+                nc.sync.dma_start(out=w1_w[:], in_=w1_words.rearrange("z p n t -> p z (n t)").bitcast(I32))
+        nc.sync.dma_start(out=w3_w[:], in_=w3_words[0].rearrange("p n t -> p (n t)").bitcast(I32))
+        w3_rows = w3_scales[0].rearrange("(q r) n -> r q n", r=4)
         for r in range(4):
-            nc.sync.dma_start(out=w1_sc[r:P:32, :].bitcast(I32).rearrange("q (z n) -> q z n", z=2), in_=w1_rows[r].bitcast(I32))
+            nc.sync.dma_start(out=w3_sc[r:P:32, :].bitcast(I32), in_=w3_rows[r].bitcast(I32))
 
         pairs = {}
         flat = {}
@@ -163,7 +162,7 @@ def tile_picked_lora_relu_e_kernel(tc, xT, w1_words, w1_scales, w2, w3_words, w3
         quantise_w2(1, 0, 2, 64, 128)
 
         h_ps = [psum.tile([P, PACK, CHUNK], F32, name=f"h_ps{c}", offset=2048 * c) for c in range(CHUNKS)]
-        o_ps = [psum.tile([P, n * CHUNK], F32, name=f"o_ps{c}", offset=(0 if c == 0 else 2048 * (c + 2))) for c, n, e in OUT_GROUPS]
+        o_ps = [psum.tile([P, n * CHUNK], F32, name=f"o_ps{c}", offset=2048 * (4 + c)) for c, n, e in OUT_GROUPS]
 
         def x_operand(z, first, count):
             tokens = slice(first * CHUNK, (first + count) * CHUNK)
@@ -196,24 +195,12 @@ def tile_picked_lora_relu_e_kernel(tc, xT, w1_words, w1_scales, w2, w3_words, w3
                     stop=False,
                 )
 
-        for i, n in enumerate(WARM):
-            words, scales = x_operand(0, 0, n)
-            nc.tensor.matmul_mx(
-                out=h_ps[i][:, 0:n, :].rearrange("p t n -> p (t n)"),
-                lhsT=w3_w[:].bitcast(FP8X4),
-                lhsT_scale=w3_sc[:],
-                rhs=words,
-                rhs_scale=scales,
-                start=True,
-                stop=True,
-            )
+        for z in range(2):
+            w1_passes(z, range(len(OUT_GROUPS)))
         for z, pair in ((0, 0), (0, 2), (1, 2), (1, 0)):
             for c in range(CHUNKS):
                 for t in (pair, pair + 1):
                     h_pass(z, c, t)
-        for g in range(len(OUT_GROUPS)):
-            w1_passes(0, (g,))
-            w1_passes(1, (g,))
 
         h_bf = {}
         for c, n, e in OUT_GROUPS:

@@ -18,213 +18,238 @@ RELU = mybir.ActivationFunctionType.Relu
 P = 128
 PACK = 4
 K_PASS = P * PACK
+PASSES = K // K_PASS
+LIST_COLUMN = 16
+SCALE_ROWS = 4
+QUADRANT = 32
 CHUNK = 128
 CHUNKS = S // CHUNK
 HALF = S // 2
+LOW, HIGH = 0, 2
 
-X_SHARES = (352, 384, 432, 432)
-RELU_ON = "vsvs"
-OUT_GROUPS = [(0, 2, "s"), (2, 1, "v"), (3, 1, "s")]
+SCALAR_TOKENS = {(0, 0): 384, (0, 1): 416, (1, 0): 448, (1, 1): 496}
+OUT_GROUPS = [(0, 2, "scalar"), (2, 1, "vector"), (3, 1, "scalar")]
+
+X_LOAD_BYTES = 2 * T * 4
+FIRST_DEALT_AT = 2 * PASSES * X_LOAD_BYTES
+VECTOR_DEALT_AT = FIRST_DEALT_AT + 2 * H * 2
 
 
 def tile_picked_lora_relu_e_kernel(tc, xT, w1_words, w1_scales, w2, w3_words, w3_scales, offs, out):
     nc = tc.nc
 
-    def move(engine, dst, src):
-        if engine == "s":
+    def copy(engine, dst, src):
+        if engine == "scalar":
             nc.scalar.activation(out=dst, in_=src, func=COPY)
         else:
             nc.vector.tensor_copy(out=dst, in_=src)
 
     with ExitStack() as ctx:
         keep = ctx.enter_context(tc.tile_pool(name="keep", bufs=1))
-        late = ctx.enter_context(tc.tile_pool(name="late", bufs=1))
+        shared = ctx.enter_context(tc.tile_pool(name="shared", bufs=1))
         psum = ctx.enter_context(tc.psum_pool(name="psum", bufs=1))
 
-        offsets = keep.tile([P, S // 16], U16, name="offsets")
-        w1_sc = keep.tile([P, 2 * N], U8, name="w1_sc", align_bytes=64)
-        w3_sc = keep.tile([P, N], U8, name="w3_sc", align_bytes=64)
+        def sbuf(shape, dtype, name, at=None):
+            if at is None:
+                return keep.tile(shape, dtype, name=name, align_bytes=64)
+            return shared.tile(shape, dtype, name=name, align_bytes=64, offset=at)
+
+        def x_load_at(z, u):
+            return X_LOAD_BYTES * (2 * z + u)
+
+        offsets = keep.tile([P, S // LIST_COLUMN], U16, name="offsets")
+        w1_sc = sbuf([P, PASSES * N], U8, "w1_sc")
+        w3_sc = sbuf([P, N], U8, "w3_sc")
         nc.vector.memset(w1_sc[:].bitcast(I32), 0)
         nc.vector.memset(w3_sc[:].bitcast(I32), 0)
 
-        w1_rows = w1_scales.rearrange("z (q r) n -> r q z n", r=4)
-        for r in range(4):
-            nc.scalar.dma_start(out=w1_sc[r:P:32, :].bitcast(I32).rearrange("q (z n) -> q z n", z=2), in_=w1_rows[r].bitcast(I32))
+        w1_rows = w1_scales.rearrange("z (q r) n -> r q z n", r=SCALE_ROWS)
+        for r in range(SCALE_ROWS):
+            nc.scalar.dma_start(out=w1_sc[r:P:QUADRANT, :].bitcast(I32).rearrange("q (z n) -> q z n", z=PASSES), in_=w1_rows[r].bitcast(I32))
         x_raw = {}
-        for z in range(2):
+        for z in range(PASSES):
             rows = xT[z * K_PASS : (z + 1) * K_PASS, :].rearrange("(p j) t -> p j t", j=PACK)
             for u in range(2):
-                x_raw[z, u] = late.tile([P, 2, T], F32, name=f"x_raw{z}{u}", align_bytes=64, offset=8192 * (2 * z + u))
+                x_raw[z, u] = sbuf([P, 2, T], F32, f"x_raw{z}{u}", at=x_load_at(z, u))
                 nc.sync.dma_start(out=x_raw[z, u][:], in_=rows[:, 2 * u : 2 * u + 2, :])
-                if z == 0 and u == 0:
+                if (z, u) == (0, 0):
                     nc.sync.dma_start(offsets[:], offs)
-        w1_w = keep.tile([P, 2, N], I32, name="w1_w", align_bytes=64)
-        w3_w = keep.tile([P, N], I32, name="w3_w", align_bytes=64)
-        w2_raw = [keep.tile([P, PACK, H], F32, name=f"w2_raw{z}") for z in range(2)]
-        for z in range(2):
+        w1_codes = sbuf([P, PASSES, N], I32, "w1_codes")
+        w3_codes = sbuf([P, N], I32, "w3_codes")
+        w2_raw = [keep.tile([P, PACK, H], F32, name=f"w2_raw{z}") for z in range(PASSES)]
+
+        def load_w2(z, a, b):
             run = w2[z * K_PASS : (z + 1) * K_PASS, :].rearrange("(p j) c -> p (j c)", j=PACK)
-            cuts = (0, PACK * H) if z == 0 else (0, PACK * H - H // 2, PACK * H)
-            for a, b in zip(cuts, cuts[1:]):
-                nc.sync.dma_start(out=w2_raw[z][:].rearrange("p j c -> p (j c)")[:, a:b], in_=run[:, a:b])
-            if z == 0:
-                nc.sync.dma_start(out=w1_w[:], in_=w1_words.rearrange("z p n t -> p z (n t)").bitcast(I32))
-        nc.sync.dma_start(out=w3_w[:], in_=w3_words[0].rearrange("p n t -> p (n t)").bitcast(I32))
-        w3_rows = w3_scales[0].rearrange("(q r) n -> r q n", r=4)
-        for r in range(4):
-            nc.sync.dma_start(out=w3_sc[r:P:32, :].bitcast(I32), in_=w3_rows[r].bitcast(I32))
+            nc.sync.dma_start(out=w2_raw[z][:].rearrange("p j c -> p (j c)")[:, a:b], in_=run[:, a:b])
+
+        load_w2(0, 0, PACK * H)
+        nc.sync.dma_start(out=w1_codes[:], in_=w1_words.rearrange("z p n t -> p z (n t)").bitcast(I32))
+        load_w2(1, 0, PACK * H - H // 2)
+        load_w2(1, PACK * H - H // 2, PACK * H)
+        nc.sync.dma_start(out=w3_codes[:], in_=w3_words[0].rearrange("p n t -> p (n t)").bitcast(I32))
+        w3_rows = w3_scales[0].rearrange("(q r) n -> r q n", r=SCALE_ROWS)
+        for r in range(SCALE_ROWS):
+            nc.sync.dma_start(out=w3_sc[r:P:QUADRANT, :].bitcast(I32), in_=w3_rows[r].bitcast(I32))
 
         pairs = {}
-        flat = {}
+        picked = {}
         woven = {}
-        x_words = [keep.tile([P, S], U32, name=f"x_words{z}", align_bytes=64) for z in range(2)]
-        x_scales = [keep.tile([P, S], U8, name=f"x_scales{z}", align_bytes=64) for z in range(2)]
+        x_first = sbuf([P, S], U32, "x_first")
+        x_last = [sbuf([P, HALF], U32, "x_last0"), sbuf([P, HALF], U32, "x_last1", at=VECTOR_DEALT_AT)]
+        x_sc = [sbuf([P, S], U8, f"x_sc{z}") for z in range(PASSES)]
+
+        def x_codes(z, a, b):
+            return x_first[:, a:b] if z == 0 else x_last[a // HALF][:, a % HALF : a % HALF + b - a]
 
         def round_pairs(z, u):
-            pairs[z, u] = keep.tile([P, T], U32, name=f"pairs{z}{u}", align_bytes=64)
-            share = X_SHARES[2 * z + u]
-            for e, a, b in (("s", 0, share), ("v", share, T)):
-                move(
-                    e,
+            pairs[z, u] = sbuf([P, T], U32, f"pairs{z}{u}")
+            for engine, a, b in (("scalar", 0, SCALAR_TOKENS[z, u]), ("vector", SCALAR_TOKENS[z, u], T)):
+                copy(
+                    engine,
                     pairs[z, u][:, a:b].bitcast(BF16).rearrange("p (c i e) -> p c e i", i=4, e=2),
                     x_raw[z, u][:, :, a:b].rearrange("p e (c i) -> p c e i", i=4),
                 )
 
         def gather(z, u, a, b):
-            if (z, u) not in flat:
-                flat[z, u] = keep.tile([P, 2, S], U32, name=f"flat{z}", align_bytes=64) if u == 0 else flat[z, 0]
-            nc.vector.tensor_copy(out=flat[z, u][:, u, a:b], in_=pairs[z, u][:].indirect(offsets[:, a // 16 : b // 16]))
+            if z not in picked:
+                picked[z] = sbuf([P, 2, S], U32, f"picked{z}")
+            nc.vector.tensor_copy(out=picked[z][:, u, a:b], in_=pairs[z, u][:].indirect(offsets[:, a // LIST_COLUMN : b // LIST_COLUMN]))
 
-        def weave(e, z, a, b, offset=None):
-            if offset is None:
-                woven[z, a] = keep.tile([P, b - a, 2], U32, name=f"woven{z}_{a}", align_bytes=64)
-            else:
-                woven[z, a] = late.tile([P, b - a, 2], U32, name=f"woven{z}_{a}", align_bytes=64, offset=offset)
-            if e == "s":
-                nc.scalar.copy(out=woven[z, a][:], in_=flat[z, 0][:, :, a:b].rearrange("p u s -> p s u"))
+        def weave(engine, z, half, at=None):
+            woven[z, half] = sbuf([P, HALF, 2], U32, f"woven{z}{half}", at=at)
+            source = picked[z][:, :, half * HALF : (half + 1) * HALF]
+            if engine == "scalar":
+                nc.scalar.copy(out=woven[z, half][:], in_=source.rearrange("p u s -> p s u"))
             else:
                 nc.vector.tensor_copy(
-                    out=woven[z, a][:].rearrange("p s u -> p (s u)").bitcast(BF16).rearrange("p (s u e) -> p s u e", u=2, e=2),
-                    in_=flat[z, 0][:, :, a:b].bitcast(BF16).rearrange("p u (s e) -> p s u e", e=2),
+                    out=woven[z, half][:].rearrange("p s u -> p (s u)").bitcast(BF16).rearrange("p (s u e) -> p s u e", u=2, e=2),
+                    in_=source.bitcast(BF16).rearrange("p u (s e) -> p s u e", e=2),
                 )
 
-        def quantise_x(z, a, b):
+        def quantise_x(z, half):
+            a, b = half * HALF, (half + 1) * HALF
             nc.vector.quantize_mx(
-                out=x_words[z][:, a:b].bitcast(FP8X4),
-                scales=x_scales[z][:, a:b],
-                in_=woven[z, a][:].rearrange("p s u -> p (s u)").bitcast(BF16),
+                out=x_codes(z, a, b).bitcast(FP8X4),
+                scales=x_sc[z][:, a:b],
+                in_=woven[z, half][:].rearrange("p s u -> p (s u)").bitcast(BF16),
             )
 
-        w2_codes = [keep.tile([P, H], U32, name=f"w2_codes{z}", align_bytes=64) for z in range(2)]
-        w2_sc = [keep.tile([P, H], U8, name=f"w2_sc{z}", align_bytes=64) for z in range(2)]
+        w2_codes = [sbuf([P, H], U32, f"w2_codes{z}") for z in range(PASSES)]
+        w2_sc = [sbuf([P, H], U8, f"w2_sc{z}") for z in range(PASSES)]
         dealt = {}
 
-        def round_w2(e, z, t0, t1, m0=0, m1=P):
-            dealt[z, t0, m0] = keep.tile([P, (t1 - t0) * (m1 - m0) * PACK], BF16, name=f"w2_bf{z}{t0}_{m0}", align_bytes=64)
-            src = w2_raw[z][:].rearrange("p j (m t) -> p m j t", t=PACK)[:, m0:m1, :, t0:t1]
-            move(e, dealt[z, t0, m0][:].rearrange("p (t m j) -> p m j t", t=t1 - t0, j=PACK), src)
+        def round_w2(engine, z, first, m0=0, m1=P, at=None):
+            dealt[z, first, m0] = sbuf([P, 2 * (m1 - m0) * PACK], BF16, f"dealt{z}{first}_{m0}", at=at)
+            source = w2_raw[z][:].rearrange("p j (m t) -> p m j t", t=PACK)[:, m0:m1, :, first : first + 2]
+            copy(engine, dealt[z, first, m0][:].rearrange("p (t m j) -> p m j t", t=2, j=PACK), source)
 
-        def quantise_w2(z, t0, t1, m0=0, m1=P):
-            if m1 - m0 == P:
-                cols = slice(t0 * P, t1 * P)
-                nc.vector.quantize_mx(out=w2_codes[z][:, cols].bitcast(FP8X4), scales=w2_sc[z][:, cols], in_=dealt[z, t0, 0][:])
-            else:
-                width = (m1 - m0) * PACK
-                for t in range(t0, t1):
-                    cols = slice(t * P + m0, t * P + m1)
-                    nc.vector.quantize_mx(out=w2_codes[z][:, cols].bitcast(FP8X4), scales=w2_sc[z][:, cols], in_=dealt[z, t0, m0][:, (t - t0) * width : (t - t0 + 1) * width])
+        def quantise_w2(z, first):
+            cols = slice(first * P, (first + 2) * P)
+            nc.vector.quantize_mx(out=w2_codes[z][:, cols].bitcast(FP8X4), scales=w2_sc[z][:, cols], in_=dealt[z, first, 0][:])
 
-        round_pairs(0, 0)
-        gather(0, 0, 0, S)
-        round_pairs(0, 1)
-        gather(0, 1, 0, S)
-        round_pairs(1, 0)
-        gather(1, 0, 0, S)
-        weave("s", 0, 0, HALF, offset=8192 * 2)
+        def quantise_w2_part(z, first, m0, m1):
+            width = (m1 - m0) * PACK
+            for i in range(2):
+                cols = slice((first + i) * P + m0, (first + i) * P + m1)
+                nc.vector.quantize_mx(out=w2_codes[z][:, cols].bitcast(FP8X4), scales=w2_sc[z][:, cols], in_=dealt[z, first, m0][:, i * width : (i + 1) * width])
+
+        for z, u in ((0, 0), (0, 1), (1, 0)):
+            round_pairs(z, u)
+            gather(z, u, 0, S)
+        weave("scalar", 0, 0, at=x_load_at(1, 0))
         round_pairs(1, 1)
-        quantise_x(0, 0, HALF)
-        weave("s", 0, HALF, S, offset=8192 * 3)
+        quantise_x(0, 0)
+        weave("scalar", 0, 1, at=x_load_at(1, 1))
         gather(1, 1, 0, HALF)
-        quantise_x(0, HALF, S)
+        quantise_x(0, 1)
         gather(1, 1, HALF, S)
-        round_w2("s", 0, 0, 2)
-        quantise_w2(0, 0, 2)
-        weave("v", 1, 0, HALF)
-        weave("v", 1, HALF, S)
-        quantise_x(1, 0, HALF)
-        quantise_x(1, HALF, S)
-        round_w2("s", 0, 2, 4)
-        round_w2("v", 1, 2, 4)
-        quantise_w2(0, 2, 4)
-        round_w2("s", 1, 0, 2, 0, 64)
-        round_w2("s", 1, 0, 2, 64, 128)
-        quantise_w2(1, 2, 4)
-        quantise_w2(1, 0, 2, 0, 64)
-        quantise_w2(1, 0, 2, 64, 128)
+        round_w2("scalar", 0, LOW, at=FIRST_DEALT_AT)
+        quantise_w2(0, LOW)
+        weave("vector", 1, 0)
+        quantise_x(1, 0)
+        weave("vector", 1, 1, at=FIRST_DEALT_AT)
+        round_w2("scalar", 0, HIGH)
+        round_w2("vector", 1, HIGH, at=VECTOR_DEALT_AT)
+        quantise_w2(0, HIGH)
+        round_w2("scalar", 1, LOW, 0, P // 2)
+        round_w2("scalar", 1, LOW, P // 2, P)
+        quantise_w2(1, HIGH)
+        quantise_w2_part(1, LOW, 0, P // 2)
+        quantise_w2_part(1, LOW, P // 2, P)
+        quantise_x(1, 1)
 
-        h_ps = [psum.tile([P, PACK, CHUNK], F32, name=f"h_ps{c}", offset=2048 * c) for c in range(CHUNKS)]
-        o_ps = [psum.tile([P, n * CHUNK], F32, name=f"o_ps{c}", offset=2048 * (4 + c)) for c, n, e in OUT_GROUPS]
+        h_ps = [psum.tile([P, PACK, CHUNK], F32, name=f"h_ps{c}") for c in range(CHUNKS)]
+        out_ps = [psum.tile([P, count * CHUNK], F32, name=f"out_ps{c}") for c, count, engine in OUT_GROUPS]
 
-        def x_operand(z, first, count):
-            tokens = slice(first * CHUNK, (first + count) * CHUNK)
-            return x_words[z][:, tokens].bitcast(FP8X4), x_scales[z][:, tokens]
+        def x_operand(z, c, count):
+            a, b = c * CHUNK, (c + count) * CHUNK
+            return x_codes(z, a, b).bitcast(FP8X4), x_sc[z][:, a:b]
 
-        def h_pass(z, c, t):
+        def h_passes(z, first, c):
             words, scales = x_operand(z, c, 1)
-            cols = slice(t * P, (t + 1) * P)
-            nc.tensor.matmul_mx(
-                out=h_ps[c][:, t, :],
-                lhsT=w2_codes[z][:, cols].bitcast(FP8X4),
-                lhsT_scale=w2_sc[z][:, cols],
-                rhs=words,
-                rhs_scale=scales,
-                start=(z == 0 and t == 0),
-                stop=(z == 1 and t == 1),
-            )
-
-        def w1_passes(z, groups):
-            for g in groups:
-                c, n, e = OUT_GROUPS[g]
-                words, scales = x_operand(z, c, n)
+            for t in (first, first + 1):
+                cols = slice(t * P, (t + 1) * P)
                 nc.tensor.matmul_mx(
-                    out=o_ps[g][:],
-                    lhsT=w1_w[:, z, :].bitcast(FP8X4),
-                    lhsT_scale=w1_sc[:, z * N : (z + 1) * N],
+                    out=h_ps[c][:, t, :],
+                    lhsT=w2_codes[z][:, cols].bitcast(FP8X4),
+                    lhsT_scale=w2_sc[z][:, cols],
                     rhs=words,
                     rhs_scale=scales,
-                    start=(z == 0),
-                    stop=False,
+                    start=(z == 0 and t == LOW),
+                    stop=(z == 1 and t == LOW + 1),
                 )
 
-        for z in range(2):
-            w1_passes(z, range(len(OUT_GROUPS)))
-        for z, pair in ((0, 0), (0, 2), (1, 2), (1, 0)):
+        def w1_pass(z, g):
+            c, count, engine = OUT_GROUPS[g]
+            words, scales = x_operand(z, c, count)
+            nc.tensor.matmul_mx(
+                out=out_ps[g][:],
+                lhsT=w1_codes[:, z, :].bitcast(FP8X4),
+                lhsT_scale=w1_sc[:, z * N : (z + 1) * N],
+                rhs=words,
+                rhs_scale=scales,
+                start=(z == 0),
+                stop=False,
+            )
+
+        for g in range(len(OUT_GROUPS)):
+            w1_pass(0, g)
+        w1_pass(1, 0)
+        for first in (LOW, HIGH):
             for c in range(CHUNKS):
-                for t in (pair, pair + 1):
-                    h_pass(z, c, t)
+                h_passes(0, first, c)
+        for first in (HIGH, LOW):
+            for c in range(CHUNKS // 2):
+                h_passes(1, first, c)
+        for c in range(CHUNKS // 2, CHUNKS):
+            for first in (HIGH, LOW):
+                h_passes(1, first, c)
+        for g in range(1, len(OUT_GROUPS)):
+            w1_pass(1, g)
 
         h_bf = {}
-        for c, n, e in OUT_GROUPS:
-            h_bf[c] = keep.tile([P, n * CHUNK * PACK], BF16, name=f"h_bf{c}", align_bytes=64)
-            for i in range(n):
+        for c, count, engine in OUT_GROUPS:
+            h_bf[c] = sbuf([P, count * CHUNK * PACK], BF16, f"h_bf{c}")
+            for i in range(count):
                 dst = h_bf[c][:, i * CHUNK * PACK : (i + 1) * CHUNK * PACK].rearrange("p (n t) -> p n t", t=PACK)
                 src = h_ps[c + i][:].rearrange("p t n -> p n t")
-                if RELU_ON[c + i] == "s":
-                    nc.scalar.activation(out=dst, in_=src, func=RELU)
-                else:
+                if (c + i) % 2 == 0:
                     nc.vector.tensor_scalar_max(out=dst, in0=src, scalar1=0.0)
-        for g, (c, n, e) in enumerate(OUT_GROUPS):
-            h_words = keep.tile([P, n * CHUNK], U32, name=f"h_words{c}", align_bytes=64)
-            h_sc = keep.tile([P, n * CHUNK], U8, name=f"h_sc{c}", align_bytes=64)
-            nc.vector.quantize_mx(out=h_words[:].bitcast(FP8X4), scales=h_sc[:], in_=h_bf[c][:])
+                else:
+                    nc.scalar.activation(out=dst, in_=src, func=RELU)
+        for g, (c, count, engine) in enumerate(OUT_GROUPS):
+            h_codes = sbuf([P, count * CHUNK], U32, f"h_codes{c}")
+            h_sc = sbuf([P, count * CHUNK], U8, f"h_sc{c}")
+            nc.vector.quantize_mx(out=h_codes[:].bitcast(FP8X4), scales=h_sc[:], in_=h_bf[c][:])
             nc.tensor.matmul_mx(
-                out=o_ps[g][:],
-                lhsT=w3_w[:].bitcast(FP8X4),
+                out=out_ps[g][:],
+                lhsT=w3_codes[:].bitcast(FP8X4),
                 lhsT_scale=w3_sc[:],
-                rhs=h_words[:].bitcast(FP8X4),
+                rhs=h_codes[:].bitcast(FP8X4),
                 rhs_scale=h_sc[:],
                 start=False,
                 stop=True,
             )
-            res = keep.tile([P, n * CHUNK], F32, name=f"res{c}")
-            move(e, res[:], o_ps[g][:])
-            nc.sync.dma_start(out=out[:, c * CHUNK : (c + n) * CHUNK], in_=res[:])
+            result = keep.tile([P, count * CHUNK], F32, name=f"result{c}")
+            copy(engine, result[:], out_ps[g][:])
+            nc.sync.dma_start(out=out[:, c * CHUNK : (c + count) * CHUNK], in_=result[:])

@@ -28,11 +28,15 @@ HALF = S // 2
 LOW, HIGH = 0, 2
 
 SCALAR_TOKENS = {(0, 0): 384, (0, 1): 416, (1, 0): 448, (1, 1): 496}
-OUT_GROUPS = [(0, 2, "scalar"), (2, 1, "vector"), (3, 1, "scalar")]
+OUT_GROUPS = [(0, 2, "scalar"), (2, 1, "scalar"), (3, 1, "vector")]
+
+WARM_UP = [256, 256, 256, 256]
+BANK = 2048
 
 X_LOAD_BYTES = 2 * T * 4
 FIRST_DEALT_AT = 2 * PASSES * X_LOAD_BYTES
 VECTOR_DEALT_AT = FIRST_DEALT_AT + 2 * H * 2
+W2_RAW_AT = VECTOR_DEALT_AT + 2 * H * 2
 
 
 def tile_picked_lora_relu_e_kernel(tc, xT, w1_words, w1_scales, w2, w3_words, w3_scales, offs, out):
@@ -63,9 +67,6 @@ def tile_picked_lora_relu_e_kernel(tc, xT, w1_words, w1_scales, w2, w3_words, w3
         nc.vector.memset(w1_sc[:].bitcast(I32), 0)
         nc.vector.memset(w3_sc[:].bitcast(I32), 0)
 
-        w1_rows = w1_scales.rearrange("z (q r) n -> r q z n", r=SCALE_ROWS)
-        for r in range(SCALE_ROWS):
-            nc.scalar.dma_start(out=w1_sc[r:P:QUADRANT, :].bitcast(I32).rearrange("q (z n) -> q z n", z=PASSES), in_=w1_rows[r].bitcast(I32))
         x_raw = {}
         for z in range(PASSES):
             rows = xT[z * K_PASS : (z + 1) * K_PASS, :].rearrange("(p j) t -> p j t", j=PACK)
@@ -76,16 +77,19 @@ def tile_picked_lora_relu_e_kernel(tc, xT, w1_words, w1_scales, w2, w3_words, w3
                     nc.sync.dma_start(offsets[:], offs)
         w1_codes = sbuf([P, PASSES, N], I32, "w1_codes")
         w3_codes = sbuf([P, N], I32, "w3_codes")
-        w2_raw = [keep.tile([P, PACK, H], F32, name=f"w2_raw{z}") for z in range(PASSES)]
+        w2_raw = [sbuf([P, PACK, H], F32, f"w2_raw{z}", at=W2_RAW_AT + z * X_LOAD_BYTES) for z in range(PASSES)]
 
         def load_w2(z, a, b):
             run = w2[z * K_PASS : (z + 1) * K_PASS, :].rearrange("(p j) c -> p (j c)", j=PACK)
             nc.sync.dma_start(out=w2_raw[z][:].rearrange("p j c -> p (j c)")[:, a:b], in_=run[:, a:b])
 
         load_w2(0, 0, PACK * H)
-        nc.sync.dma_start(out=w1_codes[:], in_=w1_words.rearrange("z p n t -> p z (n t)").bitcast(I32))
         load_w2(1, 0, PACK * H - H // 2)
         load_w2(1, PACK * H - H // 2, PACK * H)
+        nc.sync.dma_start(out=w1_codes[:], in_=w1_words.rearrange("z p n t -> p z (n t)").bitcast(I32))
+        w1_rows = w1_scales.rearrange("z (q r) n -> r q z n", r=SCALE_ROWS)
+        for r in range(SCALE_ROWS):
+            nc.sync.dma_start(out=w1_sc[r:P:QUADRANT, :].bitcast(I32).rearrange("q (z n) -> q z n", z=PASSES), in_=w1_rows[r].bitcast(I32))
         nc.sync.dma_start(out=w3_codes[:], in_=w3_words[0].rearrange("p n t -> p (n t)").bitcast(I32))
         w3_rows = w3_scales[0].rearrange("(q r) n -> r q n", r=SCALE_ROWS)
         for r in range(SCALE_ROWS):
@@ -94,12 +98,12 @@ def tile_picked_lora_relu_e_kernel(tc, xT, w1_words, w1_scales, w2, w3_words, w3
         pairs = {}
         picked = {}
         woven = {}
-        x_first = sbuf([P, S], U32, "x_first")
+        x_first = [sbuf([P, HALF], U32, "x_first0"), sbuf([P, HALF], U32, "x_first1", at=x_load_at(1, 1))]
         x_last = [sbuf([P, HALF], U32, "x_last0"), sbuf([P, HALF], U32, "x_last1", at=VECTOR_DEALT_AT)]
         x_sc = [sbuf([P, S], U8, f"x_sc{z}") for z in range(PASSES)]
 
         def x_codes(z, a, b):
-            return x_first[:, a:b] if z == 0 else x_last[a // HALF][:, a % HALF : a % HALF + b - a]
+            return (x_first, x_last)[z][a // HALF][:, a % HALF : a % HALF + b - a]
 
         def round_pairs(z, u):
             pairs[z, u] = sbuf([P, T], U32, f"pairs{z}{u}")
@@ -143,6 +147,13 @@ def tile_picked_lora_relu_e_kernel(tc, xT, w1_words, w1_scales, w2, w3_words, w3
             source = w2_raw[z][:].rearrange("p j (m t) -> p m j t", t=PACK)[:, m0:m1, :, first : first + 2]
             copy(engine, dealt[z, first, m0][:].rearrange("p (t m j) -> p m j t", t=2, j=PACK), source)
 
+        def round_w2_half(engine, first, half, at=None):
+            if half == 0:
+                dealt[1, first, 0] = sbuf([P, 2 * P * PACK], BF16, f"dealt1{first}", at=at)
+            m = slice(half * (P // 2), (half + 1) * (P // 2))
+            source = w2_raw[1][:].rearrange("p j (m t) -> p m j t", t=PACK)[:, m, :, first : first + 2]
+            copy(engine, dealt[1, first, 0][:].rearrange("p (t m j) -> p m j t", t=2, j=PACK)[:, m, :, :], source)
+
         def quantise_w2(z, first):
             cols = slice(first * P, (first + 2) * P)
             nc.vector.quantize_mx(out=w2_codes[z][:, cols].bitcast(FP8X4), scales=w2_sc[z][:, cols], in_=dealt[z, first, 0][:])
@@ -153,33 +164,48 @@ def tile_picked_lora_relu_e_kernel(tc, xT, w1_words, w1_scales, w2, w3_words, w3
                 cols = slice((first + i) * P + m0, (first + i) * P + m1)
                 nc.vector.quantize_mx(out=w2_codes[z][:, cols].bitcast(FP8X4), scales=w2_sc[z][:, cols], in_=dealt[z, first, m0][:, i * width : (i + 1) * width])
 
-        for z, u in ((0, 0), (0, 1), (1, 0)):
-            round_pairs(z, u)
-            gather(z, u, 0, S)
+        round_pairs(0, 0)
+        gather(0, 0, 0, S)
+        round_pairs(0, 1)
+        gather(0, 1, 0, S)
+        round_pairs(1, 0)
+        gather(1, 0, 0, S)
         weave("scalar", 0, 0, at=x_load_at(1, 0))
+        weave("scalar", 0, 1, at=x_load_at(1, 0) + 2048)
         round_pairs(1, 1)
         quantise_x(0, 0)
-        weave("scalar", 0, 1, at=x_load_at(1, 1))
-        gather(1, 1, 0, HALF)
         quantise_x(0, 1)
+        gather(1, 1, 0, HALF)
         gather(1, 1, HALF, S)
-        round_w2("scalar", 0, LOW, at=FIRST_DEALT_AT)
-        quantise_w2(0, LOW)
         weave("vector", 1, 0)
+        weave("vector", 1, 1)
+        round_w2("scalar", 0, LOW)
+        quantise_w2(0, LOW)
         quantise_x(1, 0)
-        weave("vector", 1, 1, at=FIRST_DEALT_AT)
         round_w2("scalar", 0, HIGH)
-        round_w2("vector", 1, HIGH, at=VECTOR_DEALT_AT)
+        round_w2_half("vector", HIGH, 0, at=VECTOR_DEALT_AT)
+        round_w2_half("vector", HIGH, 1)
         quantise_w2(0, HIGH)
-        round_w2("scalar", 1, LOW, 0, P // 2)
-        round_w2("scalar", 1, LOW, P // 2, P)
+        round_w2_half("scalar", LOW, 0)
+        round_w2_half("scalar", LOW, 1)
         quantise_w2(1, HIGH)
-        quantise_w2_part(1, LOW, 0, P // 2)
-        quantise_w2_part(1, LOW, P // 2, P)
+        quantise_w2(1, LOW)
         quantise_x(1, 1)
 
-        h_ps = [psum.tile([P, PACK, CHUNK], F32, name=f"h_ps{c}") for c in range(CHUNKS)]
-        out_ps = [psum.tile([P, count * CHUNK], F32, name=f"out_ps{c}") for c, count, engine in OUT_GROUPS]
+        h_ps = [psum.tile([P, PACK, CHUNK], F32, name=f"h_ps{c}", offset=c * BANK) for c in range(CHUNKS)]
+        out_ps = [psum.tile([P, count * CHUNK], F32, name=f"out_ps{c}", offset=g * BANK) for g, (c, count, engine) in enumerate(OUT_GROUPS)]
+
+        for i, width in enumerate(WARM_UP):
+            unread = psum.tile([P, width], F32, name=f"unread{i}", offset=(CHUNKS + i) * BANK)
+            nc.tensor.matmul_mx(
+                out=unread[:],
+                lhsT=x_codes(0, S - P, S).bitcast(FP8X4),
+                lhsT_scale=x_sc[0][:, S - P : S],
+                rhs=x_codes(0, 0, width).bitcast(FP8X4),
+                rhs_scale=x_sc[0][:, 0:width],
+                start=True,
+                stop=True,
+            )
 
         def x_operand(z, c, count):
             a, b = c * CHUNK, (c + count) * CHUNK
@@ -212,9 +238,6 @@ def tile_picked_lora_relu_e_kernel(tc, xT, w1_words, w1_scales, w2, w3_words, w3
                 stop=False,
             )
 
-        for g in range(len(OUT_GROUPS)):
-            w1_pass(0, g)
-        w1_pass(1, 0)
         for first in (LOW, HIGH):
             for c in range(CHUNKS):
                 h_passes(0, first, c)
@@ -224,8 +247,6 @@ def tile_picked_lora_relu_e_kernel(tc, xT, w1_words, w1_scales, w2, w3_words, w3
         for c in range(CHUNKS // 2, CHUNKS):
             for first in (HIGH, LOW):
                 h_passes(1, first, c)
-        for g in range(1, len(OUT_GROUPS)):
-            w1_pass(1, g)
 
         h_bf = {}
         for c, count, engine in OUT_GROUPS:
@@ -237,6 +258,9 @@ def tile_picked_lora_relu_e_kernel(tc, xT, w1_words, w1_scales, w2, w3_words, w3
                     nc.vector.tensor_scalar_max(out=dst, in0=src, scalar1=0.0)
                 else:
                     nc.scalar.activation(out=dst, in_=src, func=RELU)
+        for g in range(len(OUT_GROUPS)):
+            for z in range(PASSES):
+                w1_pass(z, g)
         for g, (c, count, engine) in enumerate(OUT_GROUPS):
             h_codes = sbuf([P, count * CHUNK], U32, f"h_codes{c}")
             h_sc = sbuf([P, count * CHUNK], U8, f"h_sc{c}")

@@ -27,7 +27,7 @@ CHUNKS = S // CHUNK
 HALF = S // 2
 LOW, HIGH = 0, 2
 
-SCALAR_TOKENS = {(0, 0): 384, (0, 1): 416, (1, 0): 448, (1, 1): 496}
+SCALAR_TOKENS = {(0, 0): 352, (0, 1): 352, (1, 0): 400, (1, 1): 480}
 OUT_GROUPS = [(0, 2, "scalar"), (2, 1, "scalar"), (3, 1, "vector")]
 
 WARM_UP = [256, 256, 256, 256]
@@ -67,6 +67,9 @@ def tile_picked_lora_relu_e_kernel(tc, xT, w1_words, w1_scales, w2, w3_words, w3
         nc.vector.memset(w1_sc[:].bitcast(I32), 0)
         nc.vector.memset(w3_sc[:].bitcast(I32), 0)
 
+        w1_rows = w1_scales.rearrange("z (q r) n -> r q z n", r=SCALE_ROWS)
+        for r in range(SCALE_ROWS):
+            nc.scalar.dma_start(out=w1_sc[r:P:QUADRANT, :].bitcast(I32).rearrange("q (z n) -> q z n", z=PASSES), in_=w1_rows[r].bitcast(I32))
         x_raw = {}
         for z in range(PASSES):
             rows = xT[z * K_PASS : (z + 1) * K_PASS, :].rearrange("(p j) t -> p j t", j=PACK)
@@ -75,7 +78,7 @@ def tile_picked_lora_relu_e_kernel(tc, xT, w1_words, w1_scales, w2, w3_words, w3
                 nc.sync.dma_start(out=x_raw[z, u][:], in_=rows[:, 2 * u : 2 * u + 2, :])
                 if (z, u) == (0, 0):
                     nc.sync.dma_start(offsets[:], offs)
-        w1_codes = sbuf([P, PASSES, N], I32, "w1_codes")
+        w1_codes = [sbuf([P, N], I32, f"w1_codes{z}") for z in range(PASSES)]
         w3_codes = sbuf([P, N], I32, "w3_codes")
         w2_raw = [sbuf([P, PACK, H], F32, f"w2_raw{z}", at=W2_RAW_AT + z * X_LOAD_BYTES) for z in range(PASSES)]
 
@@ -83,13 +86,14 @@ def tile_picked_lora_relu_e_kernel(tc, xT, w1_words, w1_scales, w2, w3_words, w3
             run = w2[z * K_PASS : (z + 1) * K_PASS, :].rearrange("(p j) c -> p (j c)", j=PACK)
             nc.sync.dma_start(out=w2_raw[z][:].rearrange("p j c -> p (j c)")[:, a:b], in_=run[:, a:b])
 
+        def load_w1(z):
+            nc.sync.dma_start(out=w1_codes[z][:], in_=w1_words[z].rearrange("p n t -> p (n t)").bitcast(I32))
+
         load_w2(0, 0, PACK * H)
+        load_w1(0)
         load_w2(1, 0, PACK * H - H // 2)
         load_w2(1, PACK * H - H // 2, PACK * H)
-        nc.sync.dma_start(out=w1_codes[:], in_=w1_words.rearrange("z p n t -> p z (n t)").bitcast(I32))
-        w1_rows = w1_scales.rearrange("z (q r) n -> r q z n", r=SCALE_ROWS)
-        for r in range(SCALE_ROWS):
-            nc.sync.dma_start(out=w1_sc[r:P:QUADRANT, :].bitcast(I32).rearrange("q (z n) -> q z n", z=PASSES), in_=w1_rows[r].bitcast(I32))
+        load_w1(1)
         nc.sync.dma_start(out=w3_codes[:], in_=w3_words[0].rearrange("p n t -> p (n t)").bitcast(I32))
         w3_rows = w3_scales[0].rearrange("(q r) n -> r q n", r=SCALE_ROWS)
         for r in range(SCALE_ROWS):
@@ -154,6 +158,12 @@ def tile_picked_lora_relu_e_kernel(tc, xT, w1_words, w1_scales, w2, w3_words, w3
             source = w2_raw[1][:].rearrange("p j (m t) -> p m j t", t=PACK)[:, m, :, first : first + 2]
             copy(engine, dealt[1, first, 0][:].rearrange("p (t m j) -> p m j t", t=2, j=PACK)[:, m, :, :], source)
 
+        def round_w2_part(engine, z, first, m0, m1):
+            if (z, first, 0) not in dealt:
+                dealt[z, first, 0] = sbuf([P, 2 * P * PACK], BF16, f"dealt{z}{first}")
+            source = w2_raw[z][:].rearrange("p j (m t) -> p m j t", t=PACK)[:, m0:m1, :, first : first + 2]
+            copy(engine, dealt[z, first, 0][:].rearrange("p (t m j) -> p m j t", t=2, j=PACK)[:, m0:m1, :, :], source)
+
         def quantise_w2(z, first):
             cols = slice(first * P, (first + 2) * P)
             nc.vector.quantize_mx(out=w2_codes[z][:, cols].bitcast(FP8X4), scales=w2_sc[z][:, cols], in_=dealt[z, first, 0][:])
@@ -177,12 +187,13 @@ def tile_picked_lora_relu_e_kernel(tc, xT, w1_words, w1_scales, w2, w3_words, w3
         quantise_x(0, 1)
         gather(1, 1, 0, HALF)
         gather(1, 1, HALF, S)
+        round_w2_part("vector", 0, HIGH, 96, 128)
         weave("vector", 1, 0)
         weave("vector", 1, 1)
         round_w2("scalar", 0, LOW)
         quantise_w2(0, LOW)
         quantise_x(1, 0)
-        round_w2("scalar", 0, HIGH)
+        round_w2_part("scalar", 0, HIGH, 0, 96)
         round_w2_half("vector", HIGH, 0, at=VECTOR_DEALT_AT)
         round_w2_half("vector", HIGH, 1)
         quantise_w2(0, HIGH)
@@ -192,11 +203,10 @@ def tile_picked_lora_relu_e_kernel(tc, xT, w1_words, w1_scales, w2, w3_words, w3
         quantise_w2(1, LOW)
         quantise_x(1, 1)
 
-        h_ps = [psum.tile([P, PACK, CHUNK], F32, name=f"h_ps{c}", offset=c * BANK) for c in range(CHUNKS)]
-        out_ps = [psum.tile([P, count * CHUNK], F32, name=f"out_ps{c}", offset=g * BANK) for g, (c, count, engine) in enumerate(OUT_GROUPS)]
+        out_ps = [psum.tile([P, count * CHUNK], F32, name=f"out_ps{c}", offset=(CHUNKS + g) * BANK) for g, (c, count, engine) in enumerate(OUT_GROUPS)]
 
         for i, width in enumerate(WARM_UP):
-            unread = psum.tile([P, width], F32, name=f"unread{i}", offset=(CHUNKS + i) * BANK)
+            unread = psum.tile([P, width], F32, name=f"unread{i}", offset=i * BANK)
             nc.tensor.matmul_mx(
                 out=unread[:],
                 lhsT=x_codes(0, S - P, S).bitcast(FP8X4),
@@ -206,6 +216,8 @@ def tile_picked_lora_relu_e_kernel(tc, xT, w1_words, w1_scales, w2, w3_words, w3
                 start=True,
                 stop=True,
             )
+
+        h_ps = [psum.tile([P, PACK, CHUNK], F32, name=f"h_ps{c}", offset=c * BANK) for c in range(CHUNKS)]
 
         def x_operand(z, c, count):
             a, b = c * CHUNK, (c + count) * CHUNK
@@ -230,7 +242,7 @@ def tile_picked_lora_relu_e_kernel(tc, xT, w1_words, w1_scales, w2, w3_words, w3
             words, scales = x_operand(z, c, count)
             nc.tensor.matmul_mx(
                 out=out_ps[g][:],
-                lhsT=w1_codes[:, z, :].bitcast(FP8X4),
+                lhsT=w1_codes[z][:].bitcast(FP8X4),
                 lhsT_scale=w1_sc[:, z * N : (z + 1) * N],
                 rhs=words,
                 rhs_scale=scales,
@@ -238,6 +250,8 @@ def tile_picked_lora_relu_e_kernel(tc, xT, w1_words, w1_scales, w2, w3_words, w3
                 stop=False,
             )
 
+        for g in range(len(OUT_GROUPS)):
+            w1_pass(0, g)
         for first in (LOW, HIGH):
             for c in range(CHUNKS):
                 h_passes(0, first, c)
@@ -259,8 +273,7 @@ def tile_picked_lora_relu_e_kernel(tc, xT, w1_words, w1_scales, w2, w3_words, w3
                 else:
                     nc.scalar.activation(out=dst, in_=src, func=RELU)
         for g in range(len(OUT_GROUPS)):
-            for z in range(PASSES):
-                w1_pass(z, g)
+            w1_pass(1, g)
         for g, (c, count, engine) in enumerate(OUT_GROUPS):
             h_codes = sbuf([P, count * CHUNK], U32, f"h_codes{c}")
             h_sc = sbuf([P, count * CHUNK], U8, f"h_sc{c}")

@@ -27,10 +27,10 @@ CHUNKS = S // CHUNK
 HALF = S // 2
 LOW, HIGH = 0, 2
 
-SCALAR_TOKENS = {(0, 0): 352, (0, 1): 352, (1, 0): 400, (1, 1): 480}
+SCALAR_TOKENS = {(0, 0): 352, (0, 1): 352, (1, 0): 400, (1, 1): 544}
 OUT_GROUPS = [(0, 2, "scalar"), (2, 1, "scalar"), (3, 1, "vector")]
 
-WARM_UP = [256, 256, 256, 256]
+WARM_UP = [512, 512, 256, 128]
 BANK = 2048
 
 X_LOAD_BYTES = 2 * T * 4
@@ -91,9 +91,9 @@ def tile_picked_lora_relu_e_kernel(tc, xT, w1_words, w1_scales, w2, w3_words, w3
 
         load_w2(0, 0, PACK * H)
         load_w1(0)
+        load_w1(1)
         load_w2(1, 0, PACK * H - H // 2)
         load_w2(1, PACK * H - H // 2, PACK * H)
-        load_w1(1)
         nc.sync.dma_start(out=w3_codes[:], in_=w3_words[0].rearrange("p n t -> p (n t)").bitcast(I32))
         w3_rows = w3_scales[0].rearrange("(q r) n -> r q n", r=SCALE_ROWS)
         for r in range(SCALE_ROWS):
@@ -102,12 +102,12 @@ def tile_picked_lora_relu_e_kernel(tc, xT, w1_words, w1_scales, w2, w3_words, w3
         pairs = {}
         picked = {}
         woven = {}
-        x_first = [sbuf([P, HALF], U32, "x_first0"), sbuf([P, HALF], U32, "x_first1", at=x_load_at(1, 1))]
+        x_first = sbuf([P, S], U32, "x_first")
         x_last = [sbuf([P, HALF], U32, "x_last0"), sbuf([P, HALF], U32, "x_last1", at=VECTOR_DEALT_AT)]
         x_sc = [sbuf([P, S], U8, f"x_sc{z}") for z in range(PASSES)]
 
         def x_codes(z, a, b):
-            return (x_first, x_last)[z][a // HALF][:, a % HALF : a % HALF + b - a]
+            return x_first[:, a:b] if z == 0 else x_last[a // HALF][:, a % HALF : a % HALF + b - a]
 
         def round_pairs(z, u):
             pairs[z, u] = sbuf([P, T], U32, f"pairs{z}{u}")
@@ -182,9 +182,9 @@ def tile_picked_lora_relu_e_kernel(tc, xT, w1_words, w1_scales, w2, w3_words, w3
         gather(1, 0, 0, S)
         weave("scalar", 0, 0, at=x_load_at(1, 0))
         weave("scalar", 0, 1, at=x_load_at(1, 0) + 2048)
-        round_pairs(1, 1)
         quantise_x(0, 0)
         quantise_x(0, 1)
+        round_pairs(1, 1)
         gather(1, 1, 0, HALF)
         gather(1, 1, HALF, S)
         round_w2_part("vector", 0, HIGH, 96, 128)
@@ -206,11 +206,12 @@ def tile_picked_lora_relu_e_kernel(tc, xT, w1_words, w1_scales, w2, w3_words, w3
         out_ps = [psum.tile([P, count * CHUNK], F32, name=f"out_ps{c}", offset=(CHUNKS + g) * BANK) for g, (c, count, engine) in enumerate(OUT_GROUPS)]
 
         for i, width in enumerate(WARM_UP):
+            first = S - P
             unread = psum.tile([P, width], F32, name=f"unread{i}", offset=i * BANK)
             nc.tensor.matmul_mx(
                 out=unread[:],
-                lhsT=x_codes(0, S - P, S).bitcast(FP8X4),
-                lhsT_scale=x_sc[0][:, S - P : S],
+                lhsT=x_codes(0, first, first + P).bitcast(FP8X4),
+                lhsT_scale=x_sc[0][:, first : first + P],
                 rhs=x_codes(0, 0, width).bitcast(FP8X4),
                 rhs_scale=x_sc[0][:, 0:width],
                 start=True,
@@ -252,6 +253,7 @@ def tile_picked_lora_relu_e_kernel(tc, xT, w1_words, w1_scales, w2, w3_words, w3
 
         for g in range(len(OUT_GROUPS)):
             w1_pass(0, g)
+        w1_pass(1, 0)
         for first in (LOW, HIGH):
             for c in range(CHUNKS):
                 h_passes(0, first, c)
@@ -272,7 +274,7 @@ def tile_picked_lora_relu_e_kernel(tc, xT, w1_words, w1_scales, w2, w3_words, w3
                     nc.vector.tensor_scalar_max(out=dst, in0=src, scalar1=0.0)
                 else:
                     nc.scalar.activation(out=dst, in_=src, func=RELU)
-        for g in range(len(OUT_GROUPS)):
+        for g in range(1, len(OUT_GROUPS)):
             w1_pass(1, g)
         for g, (c, count, engine) in enumerate(OUT_GROUPS):
             h_codes = sbuf([P, count * CHUNK], U32, f"h_codes{c}")

@@ -24,19 +24,18 @@ SCALE_ROWS = 4
 QUADRANT = 32
 CHUNK = 128
 CHUNKS = S // CHUNK
+BANK = 2048
 HALF = S // 2
 LOW, HIGH = 0, 2
 
 SCALAR_TOKENS = {(0, 0): 352, (0, 1): 352, (1, 0): 400, (1, 1): 544}
+SCALAR_HIGH_M = 96
 OUT_GROUPS = [(0, 2, "scalar"), (2, 1, "scalar"), (3, 1, "vector")]
-
 WARM_UP = [512, 512, 256, 128]
-BANK = 2048
 
 X_LOAD_BYTES = 2 * T * 4
-FIRST_DEALT_AT = 2 * PASSES * X_LOAD_BYTES
-VECTOR_DEALT_AT = FIRST_DEALT_AT + 2 * H * 2
-W2_RAW_AT = VECTOR_DEALT_AT + 2 * H * 2
+WOVEN_BYTES = HALF * 2 * 4
+LAST_HIGH_AT = 2 * PASSES * X_LOAD_BYTES
 
 
 def tile_picked_lora_relu_e_kernel(tc, xT, w1_words, w1_scales, w2, w3_words, w3_scales, offs, out):
@@ -80,18 +79,15 @@ def tile_picked_lora_relu_e_kernel(tc, xT, w1_words, w1_scales, w2, w3_words, w3
                     nc.sync.dma_start(offsets[:], offs)
         w1_codes = [sbuf([P, N], I32, f"w1_codes{z}") for z in range(PASSES)]
         w3_codes = sbuf([P, N], I32, "w3_codes")
-        w2_raw = [sbuf([P, PACK, H], F32, f"w2_raw{z}", at=W2_RAW_AT + z * X_LOAD_BYTES) for z in range(PASSES)]
+        w2_raw = [sbuf([P, PACK, H], F32, f"w2_raw{z}") for z in range(PASSES)]
 
         def load_w2(z, a, b):
             run = w2[z * K_PASS : (z + 1) * K_PASS, :].rearrange("(p j) c -> p (j c)", j=PACK)
             nc.sync.dma_start(out=w2_raw[z][:].rearrange("p j c -> p (j c)")[:, a:b], in_=run[:, a:b])
 
-        def load_w1(z):
-            nc.sync.dma_start(out=w1_codes[z][:], in_=w1_words[z].rearrange("p n t -> p (n t)").bitcast(I32))
-
         load_w2(0, 0, PACK * H)
-        load_w1(0)
-        load_w1(1)
+        for z in range(PASSES):
+            nc.sync.dma_start(out=w1_codes[z][:], in_=w1_words[z].rearrange("p n t -> p (n t)").bitcast(I32))
         load_w2(1, 0, PACK * H - H // 2)
         load_w2(1, PACK * H - H // 2, PACK * H)
         nc.sync.dma_start(out=w3_codes[:], in_=w3_words[0].rearrange("p n t -> p (n t)").bitcast(I32))
@@ -103,11 +99,12 @@ def tile_picked_lora_relu_e_kernel(tc, xT, w1_words, w1_scales, w2, w3_words, w3
         picked = {}
         woven = {}
         x_first = sbuf([P, S], U32, "x_first")
-        x_last = [sbuf([P, HALF], U32, "x_last0"), sbuf([P, HALF], U32, "x_last1", at=VECTOR_DEALT_AT)]
+        x_last = [sbuf([P, HALF], U32, "x_last0"), sbuf([P, HALF], U32, "x_last1", at=LAST_HIGH_AT)]
         x_sc = [sbuf([P, S], U8, f"x_sc{z}") for z in range(PASSES)]
 
-        def x_codes(z, a, b):
-            return x_first[:, a:b] if z == 0 else x_last[a // HALF][:, a % HALF : a % HALF + b - a]
+        def x_operand(z, a, b):
+            words = x_first[:, a:b] if z == 0 else x_last[a // HALF][:, a % HALF : a % HALF + b - a]
+            return words.bitcast(FP8X4), x_sc[z][:, a:b]
 
         def round_pairs(z, u):
             pairs[z, u] = sbuf([P, T], U32, f"pairs{z}{u}")
@@ -135,70 +132,45 @@ def tile_picked_lora_relu_e_kernel(tc, xT, w1_words, w1_scales, w2, w3_words, w3
                 )
 
         def quantise_x(z, half):
-            a, b = half * HALF, (half + 1) * HALF
-            nc.vector.quantize_mx(
-                out=x_codes(z, a, b).bitcast(FP8X4),
-                scales=x_sc[z][:, a:b],
-                in_=woven[z, half][:].rearrange("p s u -> p (s u)").bitcast(BF16),
-            )
+            words, scales = x_operand(z, half * HALF, (half + 1) * HALF)
+            nc.vector.quantize_mx(out=words, scales=scales, in_=woven[z, half][:].rearrange("p s u -> p (s u)").bitcast(BF16))
 
         w2_codes = [sbuf([P, H], U32, f"w2_codes{z}") for z in range(PASSES)]
         w2_sc = [sbuf([P, H], U8, f"w2_sc{z}") for z in range(PASSES)]
         dealt = {}
 
-        def round_w2(engine, z, first, m0=0, m1=P, at=None):
-            dealt[z, first, m0] = sbuf([P, 2 * (m1 - m0) * PACK], BF16, f"dealt{z}{first}_{m0}", at=at)
+        def round_w2(engine, z, first, m0, m1, at=None):
+            if (z, first) not in dealt:
+                dealt[z, first] = sbuf([P, 2 * P * PACK], BF16, f"dealt{z}{first}", at=at)
             source = w2_raw[z][:].rearrange("p j (m t) -> p m j t", t=PACK)[:, m0:m1, :, first : first + 2]
-            copy(engine, dealt[z, first, m0][:].rearrange("p (t m j) -> p m j t", t=2, j=PACK), source)
-
-        def round_w2_half(engine, first, half, at=None):
-            if half == 0:
-                dealt[1, first, 0] = sbuf([P, 2 * P * PACK], BF16, f"dealt1{first}", at=at)
-            m = slice(half * (P // 2), (half + 1) * (P // 2))
-            source = w2_raw[1][:].rearrange("p j (m t) -> p m j t", t=PACK)[:, m, :, first : first + 2]
-            copy(engine, dealt[1, first, 0][:].rearrange("p (t m j) -> p m j t", t=2, j=PACK)[:, m, :, :], source)
-
-        def round_w2_part(engine, z, first, m0, m1):
-            if (z, first, 0) not in dealt:
-                dealt[z, first, 0] = sbuf([P, 2 * P * PACK], BF16, f"dealt{z}{first}")
-            source = w2_raw[z][:].rearrange("p j (m t) -> p m j t", t=PACK)[:, m0:m1, :, first : first + 2]
-            copy(engine, dealt[z, first, 0][:].rearrange("p (t m j) -> p m j t", t=2, j=PACK)[:, m0:m1, :, :], source)
+            copy(engine, dealt[z, first][:].rearrange("p (t m j) -> p m j t", t=2, j=PACK)[:, m0:m1, :, :], source)
 
         def quantise_w2(z, first):
             cols = slice(first * P, (first + 2) * P)
-            nc.vector.quantize_mx(out=w2_codes[z][:, cols].bitcast(FP8X4), scales=w2_sc[z][:, cols], in_=dealt[z, first, 0][:])
+            nc.vector.quantize_mx(out=w2_codes[z][:, cols].bitcast(FP8X4), scales=w2_sc[z][:, cols], in_=dealt[z, first][:])
 
-        def quantise_w2_part(z, first, m0, m1):
-            width = (m1 - m0) * PACK
-            for i in range(2):
-                cols = slice((first + i) * P + m0, (first + i) * P + m1)
-                nc.vector.quantize_mx(out=w2_codes[z][:, cols].bitcast(FP8X4), scales=w2_sc[z][:, cols], in_=dealt[z, first, m0][:, i * width : (i + 1) * width])
-
-        round_pairs(0, 0)
-        gather(0, 0, 0, S)
-        round_pairs(0, 1)
-        gather(0, 1, 0, S)
-        round_pairs(1, 0)
-        gather(1, 0, 0, S)
-        weave("scalar", 0, 0, at=x_load_at(1, 0))
-        weave("scalar", 0, 1, at=x_load_at(1, 0) + 2048)
-        quantise_x(0, 0)
-        quantise_x(0, 1)
+        for z, u in ((0, 0), (0, 1), (1, 0)):
+            round_pairs(z, u)
+            gather(z, u, 0, S)
+        for half in range(2):
+            weave("scalar", 0, half, at=x_load_at(1, 0) + half * WOVEN_BYTES)
+        for half in range(2):
+            quantise_x(0, half)
         round_pairs(1, 1)
         gather(1, 1, 0, HALF)
         gather(1, 1, HALF, S)
-        round_w2_part("vector", 0, HIGH, 96, 128)
-        weave("vector", 1, 0)
-        weave("vector", 1, 1)
-        round_w2("scalar", 0, LOW)
+        round_w2("vector", 0, HIGH, SCALAR_HIGH_M, P)
+        for half in range(2):
+            weave("vector", 1, half)
+        round_w2("scalar", 0, LOW, 0, P)
         quantise_w2(0, LOW)
         quantise_x(1, 0)
-        round_w2_part("scalar", 0, HIGH, 0, 96)
-        round_w2_half("vector", HIGH, 0, at=VECTOR_DEALT_AT)
-        round_w2_half("vector", HIGH, 1)
+        round_w2("scalar", 0, HIGH, 0, SCALAR_HIGH_M)
+        round_w2("vector", 1, HIGH, 0, P // 2, at=LAST_HIGH_AT)
+        round_w2("vector", 1, HIGH, P // 2, P)
         quantise_w2(0, HIGH)
-        round_w2_half("scalar", LOW, 0)
-        round_w2_half("scalar", LOW, 1)
+        round_w2("scalar", 1, LOW, 0, P // 2)
+        round_w2("scalar", 1, LOW, P // 2, P)
         quantise_w2(1, HIGH)
         quantise_w2(1, LOW)
         quantise_x(1, 1)
@@ -206,26 +178,15 @@ def tile_picked_lora_relu_e_kernel(tc, xT, w1_words, w1_scales, w2, w3_words, w3
         out_ps = [psum.tile([P, count * CHUNK], F32, name=f"out_ps{c}", offset=(CHUNKS + g) * BANK) for g, (c, count, engine) in enumerate(OUT_GROUPS)]
 
         for i, width in enumerate(WARM_UP):
-            first = S - P
             unread = psum.tile([P, width], F32, name=f"unread{i}", offset=i * BANK)
-            nc.tensor.matmul_mx(
-                out=unread[:],
-                lhsT=x_codes(0, first, first + P).bitcast(FP8X4),
-                lhsT_scale=x_sc[0][:, first : first + P],
-                rhs=x_codes(0, 0, width).bitcast(FP8X4),
-                rhs_scale=x_sc[0][:, 0:width],
-                start=True,
-                stop=True,
-            )
+            still, still_scales = x_operand(0, S - CHUNK, S)
+            words, scales = x_operand(0, 0, width)
+            nc.tensor.matmul_mx(out=unread[:], lhsT=still, lhsT_scale=still_scales, rhs=words, rhs_scale=scales, start=True, stop=True)
 
         h_ps = [psum.tile([P, PACK, CHUNK], F32, name=f"h_ps{c}", offset=c * BANK) for c in range(CHUNKS)]
 
-        def x_operand(z, c, count):
-            a, b = c * CHUNK, (c + count) * CHUNK
-            return x_codes(z, a, b).bitcast(FP8X4), x_sc[z][:, a:b]
-
         def h_passes(z, first, c):
-            words, scales = x_operand(z, c, 1)
+            words, scales = x_operand(z, c * CHUNK, (c + 1) * CHUNK)
             for t in (first, first + 1):
                 cols = slice(t * P, (t + 1) * P)
                 nc.tensor.matmul_mx(
@@ -240,7 +201,7 @@ def tile_picked_lora_relu_e_kernel(tc, xT, w1_words, w1_scales, w2, w3_words, w3
 
         def w1_pass(z, g):
             c, count, engine = OUT_GROUPS[g]
-            words, scales = x_operand(z, c, count)
+            words, scales = x_operand(z, c * CHUNK, (c + count) * CHUNK)
             nc.tensor.matmul_mx(
                 out=out_ps[g][:],
                 lhsT=w1_codes[z][:].bitcast(FP8X4),

@@ -31,7 +31,7 @@ LOW, HIGH = 0, 2
 SCALAR_TOKENS = {(0, 0): 352, (0, 1): 352, (1, 0): 400, (1, 1): 544}
 SCALAR_HIGH_M = 96
 OUT_GROUPS = [(0, 2, "scalar"), (2, 1, "scalar"), (3, 1, "vector")]
-WARM_UP = [512, 512, 256, 128]
+WARM_UP = [512, 512, 256]
 
 X_LOAD_BYTES = 2 * T * 4
 WOVEN_BYTES = HALF * 2 * 4
@@ -62,9 +62,7 @@ def tile_picked_lora_relu_e_kernel(tc, xT, w1_words, w1_scales, w2, w3_words, w3
 
         offsets = keep.tile([P, S // LIST_COLUMN], U16, name="offsets")
         w1_sc = sbuf([P, PASSES * N], U8, "w1_sc")
-        w3_sc = sbuf([P, N], U8, "w3_sc")
         nc.vector.memset(w1_sc[:].bitcast(I32), 0)
-        nc.vector.memset(w3_sc[:].bitcast(I32), 0)
 
         w1_rows = w1_scales.rearrange("z (q r) n -> r q z n", r=SCALE_ROWS)
         for r in range(SCALE_ROWS):
@@ -91,9 +89,6 @@ def tile_picked_lora_relu_e_kernel(tc, xT, w1_words, w1_scales, w2, w3_words, w3
         load_w2(1, 0, PACK * H - H // 2)
         load_w2(1, PACK * H - H // 2, PACK * H)
         nc.sync.dma_start(out=w3_codes[:], in_=w3_words[0].rearrange("p n t -> p (n t)").bitcast(I32))
-        w3_rows = w3_scales[0].rearrange("(q r) n -> r q n", r=SCALE_ROWS)
-        for r in range(SCALE_ROWS):
-            nc.sync.dma_start(out=w3_sc[r:P:QUADRANT, :].bitcast(I32), in_=w3_rows[r].bitcast(I32))
 
         pairs = {}
         picked = {}
@@ -157,6 +152,8 @@ def tile_picked_lora_relu_e_kernel(tc, xT, w1_words, w1_scales, w2, w3_words, w3
         for half in range(2):
             quantise_x(0, half)
         round_pairs(1, 1)
+        w3_sc = sbuf([P, N], U8, "w3_sc", at=x_load_at(1, 1))
+        nc.gpsimd.memset(w3_sc[:].bitcast(I32), 0)
         gather(1, 1, 0, HALF)
         gather(1, 1, HALF, S)
         round_w2("vector", 0, HIGH, SCALAR_HIGH_M, P)
@@ -179,9 +176,12 @@ def tile_picked_lora_relu_e_kernel(tc, xT, w1_words, w1_scales, w2, w3_words, w3
 
         for i, width in enumerate(WARM_UP):
             unread = psum.tile([P, width], F32, name=f"unread{i}", offset=i * BANK)
-            still, still_scales = x_operand(0, S - CHUNK, S)
             words, scales = x_operand(0, 0, width)
-            nc.tensor.matmul_mx(out=unread[:], lhsT=still, lhsT_scale=still_scales, rhs=words, rhs_scale=scales, start=True, stop=True)
+            nc.tensor.matmul_mx(out=unread[:], lhsT=x_first[:, S - CHUNK : S].bitcast(FP8X4), lhsT_scale=w3_sc[:], rhs=words, rhs_scale=scales, start=True, stop=True)
+
+        w3_rows = w3_scales[0].rearrange("(q r) n -> r q n", r=SCALE_ROWS)
+        for r in range(SCALE_ROWS):
+            nc.sync.dma_start(out=w3_sc[r:P:QUADRANT, :].bitcast(I32), in_=w3_rows[r].bitcast(I32))
 
         h_ps = [psum.tile([P, PACK, CHUNK], F32, name=f"h_ps{c}", offset=c * BANK) for c in range(CHUNKS)]
 

@@ -28,7 +28,8 @@ BANK = 2048
 HALF = S // 2
 LOW, HIGH = 0, 2
 
-SCALAR_TOKENS = {(0, 0): 352, (0, 1): 352, (1, 0): 400, (1, 1): 544}
+SCALAR_TOKENS = {(0, 0): 352, (0, 1): 352, (1, 0): 400, (1, 1): 752}
+POOL_TOKENS = 288
 SCALAR_HIGH_M = 96
 OUT_GROUPS = [(0, 2, "scalar"), (2, 1, "scalar"), (3, 1, "vector")]
 WARM_UP = [512, 512, 256]
@@ -64,18 +65,24 @@ def tile_picked_lora_relu_e_kernel(tc, xT, w1_words, w1_scales, w2, w3_words, w3
         w1_sc = sbuf([P, PASSES * N], U8, "w1_sc")
         nc.vector.memset(w1_sc[:].bitcast(I32), 0)
 
-        w1_rows = w1_scales.rearrange("z (q r) n -> r q z n", r=SCALE_ROWS)
-        for r in range(SCALE_ROWS):
-            nc.scalar.dma_start(out=w1_sc[r:P:QUADRANT, :].bitcast(I32).rearrange("q (z n) -> q z n", z=PASSES), in_=w1_rows[r].bitcast(I32))
         x_raw = {}
         for z in range(PASSES):
             rows = xT[z * K_PASS : (z + 1) * K_PASS, :].rearrange("(p j) t -> p j t", j=PACK)
             for u in range(2):
                 x_raw[z, u] = sbuf([P, 2, T], F32, f"x_raw{z}{u}", at=x_load_at(z, u))
-                nc.sync.dma_start(out=x_raw[z, u][:], in_=rows[:, 2 * u : 2 * u + 2, :])
+                run = rows[:, 2 * u : 2 * u + 2, :].rearrange("p e t -> p (e t)")
+                flat = x_raw[z, u][:].rearrange("p e t -> p (e t)")
+                if (z, u) == (1, 1):
+                    nc.sync.dma_start(out=flat[:, : T + POOL_TOKENS], in_=run[:, : T + POOL_TOKENS])
+                    nc.sync.dma_start(out=flat[:, T + POOL_TOKENS :], in_=run[:, T + POOL_TOKENS :])
+                else:
+                    nc.sync.dma_start(out=flat, in_=run)
                 if (z, u) == (0, 0):
                     nc.sync.dma_start(offsets[:], offs)
-        w1_codes = [sbuf([P, N], I32, f"w1_codes{z}") for z in range(PASSES)]
+        w1_rows = w1_scales.rearrange("z (q r) n -> r q z n", r=SCALE_ROWS)
+        for r in range(SCALE_ROWS):
+            nc.sync.dma_start(out=w1_sc[r:P:QUADRANT, :].bitcast(I32).rearrange("q (z n) -> q z n", z=PASSES), in_=w1_rows[r].bitcast(I32))
+        w1_codes = sbuf([P, PASSES, N], I32, "w1_codes")
         w3_codes = sbuf([P, N], I32, "w3_codes")
         w2_raw = [sbuf([P, PACK, H], F32, f"w2_raw{z}") for z in range(PASSES)]
 
@@ -83,9 +90,9 @@ def tile_picked_lora_relu_e_kernel(tc, xT, w1_words, w1_scales, w2, w3_words, w3
             run = w2[z * K_PASS : (z + 1) * K_PASS, :].rearrange("(p j) c -> p (j c)", j=PACK)
             nc.sync.dma_start(out=w2_raw[z][:].rearrange("p j c -> p (j c)")[:, a:b], in_=run[:, a:b])
 
-        load_w2(0, 0, PACK * H)
-        for z in range(PASSES):
-            nc.sync.dma_start(out=w1_codes[z][:], in_=w1_words[z].rearrange("p n t -> p (n t)").bitcast(I32))
+        load_w2(0, 0, PACK * H - 3 * H // 4)
+        load_w2(0, PACK * H - 3 * H // 4, PACK * H)
+        nc.sync.dma_start(out=w1_codes[:], in_=w1_words.rearrange("z p n t -> p z (n t)").bitcast(I32))
         load_w2(1, 0, PACK * H - H // 2)
         load_w2(1, PACK * H - H // 2, PACK * H)
         nc.sync.dma_start(out=w3_codes[:], in_=w3_words[0].rearrange("p n t -> p (n t)").bitcast(I32))
@@ -103,7 +110,17 @@ def tile_picked_lora_relu_e_kernel(tc, xT, w1_words, w1_scales, w2, w3_words, w3
 
         def round_pairs(z, u):
             pairs[z, u] = sbuf([P, T], U32, f"pairs{z}{u}")
-            for engine, a, b in (("scalar", 0, SCALAR_TOKENS[z, u]), ("vector", SCALAR_TOKENS[z, u], T)):
+            first = POOL_TOKENS if (z, u) == (1, 1) else 0
+            if first:
+                nc.gpsimd.tensor_scalar(
+                    out=pairs[z, u][:, 0:first].bitcast(BF16).rearrange("p (t e) -> p t e", e=2),
+                    in0=x_raw[z, u][:, :, 0:first].rearrange("p e t -> p t e"),
+                    scalar1=1.0,
+                    scalar2=0.0,
+                    op0=mybir.AluOpType.mult,
+                    op1=mybir.AluOpType.add,
+                )
+            for engine, a, b in (("scalar", first, SCALAR_TOKENS[z, u]), ("vector", SCALAR_TOKENS[z, u], T)):
                 copy(
                     engine,
                     pairs[z, u][:, a:b].bitcast(BF16).rearrange("p (c i e) -> p c e i", i=4, e=2),
@@ -159,7 +176,8 @@ def tile_picked_lora_relu_e_kernel(tc, xT, w1_words, w1_scales, w2, w3_words, w3
         round_w2("vector", 0, HIGH, SCALAR_HIGH_M, P)
         for half in range(2):
             weave("vector", 1, half)
-        round_w2("scalar", 0, LOW, 0, P)
+        round_w2("scalar", 0, LOW, 0, P // 4)
+        round_w2("scalar", 0, LOW, P // 4, P)
         quantise_w2(0, LOW)
         quantise_x(1, 0)
         round_w2("scalar", 0, HIGH, 0, SCALAR_HIGH_M)
@@ -204,7 +222,7 @@ def tile_picked_lora_relu_e_kernel(tc, xT, w1_words, w1_scales, w2, w3_words, w3
             words, scales = x_operand(z, c * CHUNK, (c + count) * CHUNK)
             nc.tensor.matmul_mx(
                 out=out_ps[g][:],
-                lhsT=w1_codes[z][:].bitcast(FP8X4),
+                lhsT=w1_codes[:, z, :].bitcast(FP8X4),
                 lhsT_scale=w1_sc[:, z * N : (z + 1) * N],
                 rhs=words,
                 rhs_scale=scales,

@@ -30,9 +30,9 @@ LOW, HIGH = 0, 2
 
 SCALAR_TOKENS = {(0, 0): 352, (0, 1): 352, (1, 0): 400, (1, 1): 752}
 POOL_TOKENS = 288
-SCALAR_HIGH_M = 96
+SCALAR_HIGH_M = 104
 OUT_GROUPS = [(0, 2, "scalar"), (2, 1, "scalar"), (3, 1, "vector")]
-WARM_UP = [512, 512, 256]
+WARM_UP = [512, 512, 256, 128]
 
 X_LOAD_BYTES = 2 * T * 4
 WOVEN_BYTES = HALF * 2 * 4
@@ -82,7 +82,7 @@ def tile_picked_lora_relu_e_kernel(tc, xT, w1_words, w1_scales, w2, w3_words, w3
         w1_rows = w1_scales.rearrange("z (q r) n -> r q z n", r=SCALE_ROWS)
         for r in range(SCALE_ROWS):
             nc.sync.dma_start(out=w1_sc[r:P:QUADRANT, :].bitcast(I32).rearrange("q (z n) -> q z n", z=PASSES), in_=w1_rows[r].bitcast(I32))
-        w1_codes = sbuf([P, PASSES, N], I32, "w1_codes")
+        w1_codes = [sbuf([P, N], I32, f"w1_codes{z}") for z in range(PASSES)]
         w3_codes = sbuf([P, N], I32, "w3_codes")
         w2_raw = [sbuf([P, PACK, H], F32, f"w2_raw{z}") for z in range(PASSES)]
 
@@ -92,9 +92,10 @@ def tile_picked_lora_relu_e_kernel(tc, xT, w1_words, w1_scales, w2, w3_words, w3
 
         load_w2(0, 0, PACK * H - 3 * H // 4)
         load_w2(0, PACK * H - 3 * H // 4, PACK * H)
-        nc.sync.dma_start(out=w1_codes[:], in_=w1_words.rearrange("z p n t -> p z (n t)").bitcast(I32))
+        nc.sync.dma_start(out=w1_codes[0][:], in_=w1_words[0].rearrange("p n t -> p (n t)").bitcast(I32))
         load_w2(1, 0, PACK * H - H // 2)
         load_w2(1, PACK * H - H // 2, PACK * H)
+        nc.sync.dma_start(out=w1_codes[1][:], in_=w1_words[1].rearrange("p n t -> p (n t)").bitcast(I32))
         nc.sync.dma_start(out=w3_codes[:], in_=w3_words[0].rearrange("p n t -> p (n t)").bitcast(I32))
 
         pairs = {}
@@ -222,7 +223,7 @@ def tile_picked_lora_relu_e_kernel(tc, xT, w1_words, w1_scales, w2, w3_words, w3
             words, scales = x_operand(z, c * CHUNK, (c + count) * CHUNK)
             nc.tensor.matmul_mx(
                 out=out_ps[g][:],
-                lhsT=w1_codes[:, z, :].bitcast(FP8X4),
+                lhsT=w1_codes[z][:].bitcast(FP8X4),
                 lhsT_scale=w1_sc[:, z * N : (z + 1) * N],
                 rhs=words,
                 rhs_scale=scales,
@@ -232,7 +233,6 @@ def tile_picked_lora_relu_e_kernel(tc, xT, w1_words, w1_scales, w2, w3_words, w3
 
         for g in range(len(OUT_GROUPS)):
             w1_pass(0, g)
-        w1_pass(1, 0)
         for first in (LOW, HIGH):
             for c in range(CHUNKS):
                 h_passes(0, first, c)
@@ -253,7 +253,7 @@ def tile_picked_lora_relu_e_kernel(tc, xT, w1_words, w1_scales, w2, w3_words, w3
                     nc.vector.tensor_scalar_max(out=dst, in0=src, scalar1=0.0)
                 else:
                     nc.scalar.activation(out=dst, in_=src, func=RELU)
-        for g in range(1, len(OUT_GROUPS)):
+        for g in range(len(OUT_GROUPS)):
             w1_pass(1, g)
         for g, (c, count, engine) in enumerate(OUT_GROUPS):
             h_codes = sbuf([P, count * CHUNK], U32, f"h_codes{c}")

@@ -28,15 +28,17 @@ BANK = 2048
 HALF = S // 2
 LOW, HIGH = 0, 2
 
-SCALAR_TOKENS = {(0, 0): 352, (0, 1): 352, (1, 0): 400, (1, 1): 752}
-POOL_TOKENS = 288
-SCALAR_HIGH_M = 104
+LAST_STEP = (PASSES - 1, 1)
+
+SCALAR_TOKENS = {(0, 0): 352, (0, 1): 352, (1, 0): 400, (1, 1): 440}
+GPSIMD_TOKENS = 240
+EARLY_M = [P // 4, P // 2]
+SCALAR_HIGH_M = 96
 OUT_GROUPS = [(0, 2, "scalar"), (2, 1, "scalar"), (3, 1, "vector")]
 WARM_UP = [512, 512, 256, 128]
 
-X_LOAD_BYTES = 2 * T * 4
-WOVEN_BYTES = HALF * 2 * 4
-LAST_HIGH_AT = 2 * PASSES * X_LOAD_BYTES
+X_STEP_BYTES = 2 * T * 4
+LAST_HIGH_AT = 2 * PASSES * X_STEP_BYTES
 
 
 def tile_picked_lora_relu_e_kernel(tc, xT, w1_words, w1_scales, w2, w3_words, w3_scales, offs, out):
@@ -58,25 +60,24 @@ def tile_picked_lora_relu_e_kernel(tc, xT, w1_words, w1_scales, w2, w3_words, w3
                 return keep.tile(shape, dtype, name=name, align_bytes=64)
             return shared.tile(shape, dtype, name=name, align_bytes=64, offset=at)
 
-        def x_load_at(z, u):
-            return X_LOAD_BYTES * (2 * z + u)
+        def x_step_at(z, u):
+            return X_STEP_BYTES * (2 * z + u)
 
         offsets = keep.tile([P, S // LIST_COLUMN], U16, name="offsets")
         w1_sc = sbuf([P, PASSES * N], U8, "w1_sc")
         nc.vector.memset(w1_sc[:].bitcast(I32), 0)
 
+        def load_parts(tile_run, hbm_run, cuts):
+            for a, b in zip(cuts, cuts[1:]):
+                nc.sync.dma_start(out=tile_run[:, a:b], in_=hbm_run[:, a:b])
+
         x_raw = {}
         for z in range(PASSES):
             rows = xT[z * K_PASS : (z + 1) * K_PASS, :].rearrange("(p j) t -> p j t", j=PACK)
             for u in range(2):
-                x_raw[z, u] = sbuf([P, 2, T], F32, f"x_raw{z}{u}", at=x_load_at(z, u))
-                run = rows[:, 2 * u : 2 * u + 2, :].rearrange("p e t -> p (e t)")
-                flat = x_raw[z, u][:].rearrange("p e t -> p (e t)")
-                if (z, u) == (1, 1):
-                    nc.sync.dma_start(out=flat[:, : T + POOL_TOKENS], in_=run[:, : T + POOL_TOKENS])
-                    nc.sync.dma_start(out=flat[:, T + POOL_TOKENS :], in_=run[:, T + POOL_TOKENS :])
-                else:
-                    nc.sync.dma_start(out=flat, in_=run)
+                x_raw[z, u] = sbuf([P, 2, T], F32, f"x_raw{z}{u}", at=x_step_at(z, u))
+                cuts = [0, T + GPSIMD_TOKENS, 2 * T] if (z, u) == LAST_STEP else [0, 2 * T]
+                load_parts(x_raw[z, u][:].rearrange("p e t -> p (e t)"), rows[:, 2 * u : 2 * u + 2, :].rearrange("p e t -> p (e t)"), cuts)
                 if (z, u) == (0, 0):
                     nc.sync.dma_start(offsets[:], offs)
         w1_rows = w1_scales.rearrange("z (q r) n -> r q z n", r=SCALE_ROWS)
@@ -86,17 +87,18 @@ def tile_picked_lora_relu_e_kernel(tc, xT, w1_words, w1_scales, w2, w3_words, w3
         w3_codes = sbuf([P, N], I32, "w3_codes")
         w2_raw = [sbuf([P, PACK, H], F32, f"w2_raw{z}") for z in range(PASSES)]
 
-        def load_w2(z, a, b):
+        def load_w2(z):
             run = w2[z * K_PASS : (z + 1) * K_PASS, :].rearrange("(p j) c -> p (j c)", j=PACK)
-            nc.sync.dma_start(out=w2_raw[z][:].rearrange("p j c -> p (j c)")[:, a:b], in_=run[:, a:b])
+            load_parts(w2_raw[z][:].rearrange("p j c -> p (j c)"), run, [0, (PACK - 1) * H + PACK * EARLY_M[z], PACK * H])
 
-        load_w2(0, 0, PACK * H - 3 * H // 4)
-        load_w2(0, PACK * H - 3 * H // 4, PACK * H)
-        nc.sync.dma_start(out=w1_codes[0][:], in_=w1_words[0].rearrange("p n t -> p (n t)").bitcast(I32))
-        load_w2(1, 0, PACK * H - H // 2)
-        load_w2(1, PACK * H - H // 2, PACK * H)
-        nc.sync.dma_start(out=w1_codes[1][:], in_=w1_words[1].rearrange("p n t -> p (n t)").bitcast(I32))
-        nc.sync.dma_start(out=w3_codes[:], in_=w3_words[0].rearrange("p n t -> p (n t)").bitcast(I32))
+        def load_words(tile, words):
+            nc.sync.dma_start(out=tile[:], in_=words.rearrange("p n t -> p (n t)").bitcast(I32))
+
+        load_w2(0)
+        load_words(w1_codes[0], w1_words[0])
+        load_w2(1)
+        load_words(w1_codes[1], w1_words[1])
+        load_words(w3_codes, w3_words[0])
 
         pairs = {}
         picked = {}
@@ -111,17 +113,18 @@ def tile_picked_lora_relu_e_kernel(tc, xT, w1_words, w1_scales, w2, w3_words, w3
 
         def round_pairs(z, u):
             pairs[z, u] = sbuf([P, T], U32, f"pairs{z}{u}")
-            first = POOL_TOKENS if (z, u) == (1, 1) else 0
-            if first:
+            vector_from = GPSIMD_TOKENS if (z, u) == LAST_STEP else 0
+            scalar_from = T - SCALAR_TOKENS[z, u]
+            if vector_from:
                 nc.gpsimd.tensor_scalar(
-                    out=pairs[z, u][:, 0:first].bitcast(BF16).rearrange("p (t e) -> p t e", e=2),
-                    in0=x_raw[z, u][:, :, 0:first].rearrange("p e t -> p t e"),
+                    out=pairs[z, u][:, :vector_from].bitcast(BF16).rearrange("p (t e) -> p t e", e=2),
+                    in0=x_raw[z, u][:, :, :vector_from].rearrange("p e t -> p t e"),
                     scalar1=1.0,
                     scalar2=0.0,
                     op0=mybir.AluOpType.mult,
                     op1=mybir.AluOpType.add,
                 )
-            for engine, a, b in (("scalar", first, SCALAR_TOKENS[z, u]), ("vector", SCALAR_TOKENS[z, u], T)):
+            for engine, a, b in (("scalar", scalar_from, T), ("vector", vector_from, scalar_from)):
                 copy(
                     engine,
                     pairs[z, u][:, a:b].bitcast(BF16).rearrange("p (c i e) -> p c e i", i=4, e=2),
@@ -133,20 +136,21 @@ def tile_picked_lora_relu_e_kernel(tc, xT, w1_words, w1_scales, w2, w3_words, w3
                 picked[z] = sbuf([P, 2, S], U32, f"picked{z}")
             nc.vector.tensor_copy(out=picked[z][:, u, a:b], in_=pairs[z, u][:].indirect(offsets[:, a // LIST_COLUMN : b // LIST_COLUMN]))
 
-        def weave(engine, z, half, at=None):
-            woven[z, half] = sbuf([P, HALF, 2], U32, f"woven{z}{half}", at=at)
-            source = picked[z][:, :, half * HALF : (half + 1) * HALF]
+        def weave(engine, z, a, b, at=None):
+            woven[z, a] = sbuf([P, b - a, 2], U32, f"woven{z}{a}", at=at)
+            source = picked[z][:, :, a:b]
             if engine == "scalar":
-                nc.scalar.copy(out=woven[z, half][:], in_=source.rearrange("p u s -> p s u"))
+                nc.scalar.copy(out=woven[z, a][:], in_=source.rearrange("p u s -> p s u"))
             else:
                 nc.vector.tensor_copy(
-                    out=woven[z, half][:].rearrange("p s u -> p (s u)").bitcast(BF16).rearrange("p (s u e) -> p s u e", u=2, e=2),
+                    out=woven[z, a][:].rearrange("p s u -> p (s u)").bitcast(BF16).rearrange("p (s u e) -> p s u e", u=2, e=2),
                     in_=source.bitcast(BF16).rearrange("p u (s e) -> p s u e", e=2),
                 )
 
-        def quantise_x(z, half):
-            words, scales = x_operand(z, half * HALF, (half + 1) * HALF)
-            nc.vector.quantize_mx(out=words, scales=scales, in_=woven[z, half][:].rearrange("p s u -> p (s u)").bitcast(BF16))
+        def quantise_x(z, a, b, woven_from):
+            words, scales = x_operand(z, a, b)
+            source = woven[z, woven_from][:, a - woven_from : b - woven_from, :]
+            nc.vector.quantize_mx(out=words, scales=scales, in_=source.rearrange("p s u -> p (s u)").bitcast(BF16))
 
         w2_codes = [sbuf([P, H], U32, f"w2_codes{z}") for z in range(PASSES)]
         w2_sc = [sbuf([P, H], U8, f"w2_sc{z}") for z in range(PASSES)]
@@ -165,31 +169,30 @@ def tile_picked_lora_relu_e_kernel(tc, xT, w1_words, w1_scales, w2, w3_words, w3
         for z, u in ((0, 0), (0, 1), (1, 0)):
             round_pairs(z, u)
             gather(z, u, 0, S)
-        for half in range(2):
-            weave("scalar", 0, half, at=x_load_at(1, 0) + half * WOVEN_BYTES)
-        for half in range(2):
-            quantise_x(0, half)
-        round_pairs(1, 1)
-        w3_sc = sbuf([P, N], U8, "w3_sc", at=x_load_at(1, 1))
+        weave("scalar", 0, 0, S, at=x_step_at(1, 0))
+        quantise_x(0, 0, HALF, 0)
+        round_pairs(*LAST_STEP)
+        quantise_x(0, HALF, S, 0)
+        w3_sc = sbuf([P, N], U8, "w3_sc", at=x_step_at(*LAST_STEP))
         nc.gpsimd.memset(w3_sc[:].bitcast(I32), 0)
-        gather(1, 1, 0, HALF)
-        gather(1, 1, HALF, S)
+        gather(*LAST_STEP, 0, HALF)
+        gather(*LAST_STEP, HALF, S)
         round_w2("vector", 0, HIGH, SCALAR_HIGH_M, P)
         for half in range(2):
-            weave("vector", 1, half)
-        round_w2("scalar", 0, LOW, 0, P // 4)
-        round_w2("scalar", 0, LOW, P // 4, P)
+            weave("vector", 1, half * HALF, (half + 1) * HALF)
+        round_w2("scalar", 0, LOW, 0, EARLY_M[0])
+        round_w2("scalar", 0, LOW, EARLY_M[0], P)
         quantise_w2(0, LOW)
-        quantise_x(1, 0)
+        quantise_x(1, 0, HALF, 0)
         round_w2("scalar", 0, HIGH, 0, SCALAR_HIGH_M)
-        round_w2("vector", 1, HIGH, 0, P // 2, at=LAST_HIGH_AT)
-        round_w2("vector", 1, HIGH, P // 2, P)
+        round_w2("vector", 1, HIGH, 0, EARLY_M[1], at=LAST_HIGH_AT)
+        round_w2("vector", 1, HIGH, EARLY_M[1], P)
         quantise_w2(0, HIGH)
-        round_w2("scalar", 1, LOW, 0, P // 2)
-        round_w2("scalar", 1, LOW, P // 2, P)
+        round_w2("scalar", 1, LOW, 0, EARLY_M[1])
+        round_w2("scalar", 1, LOW, EARLY_M[1], P)
         quantise_w2(1, HIGH)
         quantise_w2(1, LOW)
-        quantise_x(1, 1)
+        quantise_x(1, HALF, S, HALF)
 
         out_ps = [psum.tile([P, count * CHUNK], F32, name=f"out_ps{c}", offset=(CHUNKS + g) * BANK) for g, (c, count, engine) in enumerate(OUT_GROUPS)]
 

@@ -28,17 +28,10 @@ BANK = 2048
 HALF = S // 2
 LOW, HIGH = 0, 2
 
-LAST_STEP = (PASSES - 1, 1)
-
-SCALAR_TOKENS = {(0, 0): 352, (0, 1): 352, (1, 0): 400, (1, 1): 440}
-GPSIMD_TOKENS = 240
-EARLY_M = [P // 4, P // 2]
-SCALAR_HIGH_M = 96
+X_LOADS = [(0, 0, 2), (0, 2, 4), (1, 0, 2), (1, 2, 3), (1, 3, 4)]
+EARLY_M = P // 2
+SCALAR_HIGH_M = 88
 OUT_GROUPS = [(0, 2, "scalar"), (2, 1, "scalar"), (3, 1, "vector")]
-WARM_UP = [512, 512, 256, 128]
-
-X_STEP_BYTES = 2 * T * 4
-LAST_HIGH_AT = 2 * PASSES * X_STEP_BYTES
 
 
 def tile_picked_lora_relu_e_kernel(tc, xT, w1_words, w1_scales, w2, w3_words, w3_scales, offs, out):
@@ -52,113 +45,77 @@ def tile_picked_lora_relu_e_kernel(tc, xT, w1_words, w1_scales, w2, w3_words, w3
 
     with ExitStack() as ctx:
         keep = ctx.enter_context(tc.tile_pool(name="keep", bufs=1))
-        shared = ctx.enter_context(tc.tile_pool(name="shared", bufs=1))
         psum = ctx.enter_context(tc.psum_pool(name="psum", bufs=1))
 
-        def sbuf(shape, dtype, name, at=None):
-            if at is None:
-                return keep.tile(shape, dtype, name=name, align_bytes=64)
-            return shared.tile(shape, dtype, name=name, align_bytes=64, offset=at)
-
-        def x_step_at(z, u):
-            return X_STEP_BYTES * (2 * z + u)
+        def sbuf(shape, dtype, name):
+            return keep.tile(shape, dtype, name=name, align_bytes=64)
 
         offsets = keep.tile([P, S // LIST_COLUMN], U16, name="offsets")
+
         w1_sc = sbuf([P, PASSES * N], U8, "w1_sc")
-        nc.vector.memset(w1_sc[:].bitcast(I32), 0)
-
-        def load_parts(tile_run, hbm_run, cuts):
-            for a, b in zip(cuts, cuts[1:]):
-                nc.sync.dma_start(out=tile_run[:, a:b], in_=hbm_run[:, a:b])
-
-        x_raw = {}
-        for z in range(PASSES):
-            rows = xT[z * K_PASS : (z + 1) * K_PASS, :].rearrange("(p j) t -> p j t", j=PACK)
-            for u in range(2):
-                x_raw[z, u] = sbuf([P, 2, T], F32, f"x_raw{z}{u}", at=x_step_at(z, u))
-                cuts = [0, T + GPSIMD_TOKENS, 2 * T] if (z, u) == LAST_STEP else [0, 2 * T]
-                load_parts(x_raw[z, u][:].rearrange("p e t -> p (e t)"), rows[:, 2 * u : 2 * u + 2, :].rearrange("p e t -> p (e t)"), cuts)
-                if (z, u) == (0, 0):
-                    nc.sync.dma_start(offsets[:], offs)
+        w3_sc = sbuf([P, N], U8, "w3_sc")
+        nc.gpsimd.memset(w1_sc[:].bitcast(I32), 0)
+        nc.gpsimd.memset(w3_sc[:].bitcast(I32), 0)
         w1_rows = w1_scales.rearrange("z (q r) n -> r q z n", r=SCALE_ROWS)
-        for r in range(SCALE_ROWS):
-            nc.sync.dma_start(out=w1_sc[r:P:QUADRANT, :].bitcast(I32).rearrange("q (z n) -> q z n", z=PASSES), in_=w1_rows[r].bitcast(I32))
+        w3_rows = w3_scales[0].rearrange("(q r) n -> r q n", r=SCALE_ROWS)
+
+        x_row = {}
+        for z, j0, j1 in X_LOADS:
+            rows = xT[z * K_PASS : (z + 1) * K_PASS, :].rearrange("(p j) t -> p (j t)", j=PACK)
+            raw = sbuf([P, (j1 - j0) * T], F32, f"x_raw{z}{j0}")
+            nc.sync.dma_start(out=raw[:], in_=rows[:, j0 * T : j1 * T])
+            for j in range(j0, j1):
+                x_row[z, j] = raw[:, (j - j0) * T : (j - j0 + 1) * T]
+            if (z, j0) == (0, 0):
+                nc.sync.dma_start(offsets[:], offs)
         w1_codes = [sbuf([P, N], I32, f"w1_codes{z}") for z in range(PASSES)]
         w3_codes = sbuf([P, N], I32, "w3_codes")
         w2_raw = [sbuf([P, PACK, H], F32, f"w2_raw{z}") for z in range(PASSES)]
 
-        def load_w2(z):
+        def load_w2(z, cuts):
             run = w2[z * K_PASS : (z + 1) * K_PASS, :].rearrange("(p j) c -> p (j c)", j=PACK)
-            load_parts(w2_raw[z][:].rearrange("p j c -> p (j c)"), run, [0, (PACK - 1) * H + PACK * EARLY_M[z], PACK * H])
+            for a, b in zip(cuts, cuts[1:]):
+                nc.sync.dma_start(out=w2_raw[z][:].rearrange("p j c -> p (j c)")[:, a:b], in_=run[:, a:b])
 
         def load_words(tile, words):
             nc.sync.dma_start(out=tile[:], in_=words.rearrange("p n t -> p (n t)").bitcast(I32))
 
-        load_w2(0)
+        for r in range(SCALE_ROWS):
+            nc.sync.dma_start(out=w1_sc[r:P:QUADRANT, :].bitcast(I32).rearrange("q (z n) -> q z n", z=PASSES), in_=w1_rows[r].bitcast(I32))
+        load_w2(0, [0, PACK * H])
         load_words(w1_codes[0], w1_words[0])
-        load_w2(1)
+        load_w2(1, [0, (PACK - 1) * H + PACK * EARLY_M, PACK * H])
         load_words(w1_codes[1], w1_words[1])
         load_words(w3_codes, w3_words[0])
+        for r in range(SCALE_ROWS):
+            nc.sync.dma_start(out=w3_sc[r:P:QUADRANT, :].bitcast(I32), in_=w3_rows[r].bitcast(I32))
 
-        pairs = {}
-        picked = {}
-        woven = {}
-        x_first = sbuf([P, S], U32, "x_first")
-        x_last = [sbuf([P, HALF], U32, "x_last0"), sbuf([P, HALF], U32, "x_last1", at=LAST_HIGH_AT)]
+        picked = [sbuf([P, PACK, S], F32, f"picked{z}") for z in range(PASSES)]
+        x_codes = [sbuf([P, S], U32, f"x_codes{z}") for z in range(PASSES)]
         x_sc = [sbuf([P, S], U8, f"x_sc{z}") for z in range(PASSES)]
+        woven = {}
 
-        def x_operand(z, a, b):
-            words = x_first[:, a:b] if z == 0 else x_last[a // HALF][:, a % HALF : a % HALF + b - a]
-            return words.bitcast(FP8X4), x_sc[z][:, a:b]
+        def gather(engine, z, j, a, b):
+            copy(engine, picked[z][:, j, a:b], x_row[z, j].indirect(offsets[:, a // LIST_COLUMN : b // LIST_COLUMN]))
 
-        def round_pairs(z, u):
-            pairs[z, u] = sbuf([P, T], U32, f"pairs{z}{u}")
-            vector_from = GPSIMD_TOKENS if (z, u) == LAST_STEP else 0
-            scalar_from = T - SCALAR_TOKENS[z, u]
-            if vector_from:
-                nc.gpsimd.tensor_scalar(
-                    out=pairs[z, u][:, :vector_from].bitcast(BF16).rearrange("p (t e) -> p t e", e=2),
-                    in0=x_raw[z, u][:, :, :vector_from].rearrange("p e t -> p t e"),
-                    scalar1=1.0,
-                    scalar2=0.0,
-                    op0=mybir.AluOpType.mult,
-                    op1=mybir.AluOpType.add,
-                )
-            for engine, a, b in (("scalar", scalar_from, T), ("vector", vector_from, scalar_from)):
-                copy(
-                    engine,
-                    pairs[z, u][:, a:b].bitcast(BF16).rearrange("p (c i e) -> p c e i", i=4, e=2),
-                    x_raw[z, u][:, :, a:b].rearrange("p e (c i) -> p c e i", i=4),
-                )
+        def weave(engine, z, a, b):
+            woven[z, a] = sbuf([P, (b - a) * PACK], BF16, f"woven{z}{a}")
+            copy(
+                engine,
+                woven[z, a][:].rearrange("p (c i j) -> p c j i", i=4, j=PACK),
+                picked[z][:, :, a:b].rearrange("p j (c i) -> p c j i", i=4),
+            )
 
-        def gather(z, u, a, b):
-            if z not in picked:
-                picked[z] = sbuf([P, 2, S], U32, f"picked{z}")
-            nc.vector.tensor_copy(out=picked[z][:, u, a:b], in_=pairs[z, u][:].indirect(offsets[:, a // LIST_COLUMN : b // LIST_COLUMN]))
-
-        def weave(engine, z, a, b, at=None):
-            woven[z, a] = sbuf([P, b - a, 2], U32, f"woven{z}{a}", at=at)
-            source = picked[z][:, :, a:b]
-            if engine == "scalar":
-                nc.scalar.copy(out=woven[z, a][:], in_=source.rearrange("p u s -> p s u"))
-            else:
-                nc.vector.tensor_copy(
-                    out=woven[z, a][:].rearrange("p s u -> p (s u)").bitcast(BF16).rearrange("p (s u e) -> p s u e", u=2, e=2),
-                    in_=source.bitcast(BF16).rearrange("p u (s e) -> p s u e", e=2),
-                )
-
-        def quantise_x(z, a, b, woven_from):
-            words, scales = x_operand(z, a, b)
-            source = woven[z, woven_from][:, a - woven_from : b - woven_from, :]
-            nc.vector.quantize_mx(out=words, scales=scales, in_=source.rearrange("p s u -> p (s u)").bitcast(BF16))
+        def quantise_x(z, a, b):
+            nc.vector.quantize_mx(out=x_codes[z][:, a:b].bitcast(FP8X4), scales=x_sc[z][:, a:b], in_=woven[z, a][:])
 
         w2_codes = [sbuf([P, H], U32, f"w2_codes{z}") for z in range(PASSES)]
         w2_sc = [sbuf([P, H], U8, f"w2_sc{z}") for z in range(PASSES)]
         dealt = {}
 
-        def round_w2(engine, z, first, m0, m1, at=None):
+        def round_w2(engine, z, first, m0, m1):
             if (z, first) not in dealt:
-                dealt[z, first] = sbuf([P, 2 * P * PACK], BF16, f"dealt{z}{first}", at=at)
+                dealt[z, first] = sbuf([P, 2 * P * PACK], BF16, f"dealt{z}{first}")
             source = w2_raw[z][:].rearrange("p j (m t) -> p m j t", t=PACK)[:, m0:m1, :, first : first + 2]
             copy(engine, dealt[z, first][:].rearrange("p (t m j) -> p m j t", t=2, j=PACK)[:, m0:m1, :, :], source)
 
@@ -166,70 +123,57 @@ def tile_picked_lora_relu_e_kernel(tc, xT, w1_words, w1_scales, w2, w3_words, w3
             cols = slice(first * P, (first + 2) * P)
             nc.vector.quantize_mx(out=w2_codes[z][:, cols].bitcast(FP8X4), scales=w2_sc[z][:, cols], in_=dealt[z, first][:])
 
-        for z, u in ((0, 0), (0, 1), (1, 0)):
-            round_pairs(z, u)
-            gather(z, u, 0, S)
-        weave("scalar", 0, 0, S, at=x_step_at(1, 0))
-        quantise_x(0, 0, HALF, 0)
-        round_pairs(*LAST_STEP)
-        quantise_x(0, HALF, S, 0)
-        w3_sc = sbuf([P, N], U8, "w3_sc", at=x_step_at(*LAST_STEP))
-        nc.gpsimd.memset(w3_sc[:].bitcast(I32), 0)
-        gather(*LAST_STEP, 0, HALF)
-        gather(*LAST_STEP, HALF, S)
-        round_w2("vector", 0, HIGH, SCALAR_HIGH_M, P)
-        for half in range(2):
-            weave("vector", 1, half * HALF, (half + 1) * HALF)
-        round_w2("scalar", 0, LOW, 0, EARLY_M[0])
-        round_w2("scalar", 0, LOW, EARLY_M[0], P)
-        quantise_w2(0, LOW)
-        quantise_x(1, 0, HALF, 0)
+        for j in range(PACK):
+            gather("scalar" if j % 2 else "vector", 0, j, 0, S)
+        weave("vector", 0, 0, S)
+        gather("scalar", 1, 0, 0, S)
+        gather("vector", 1, 1, 0, S)
+        quantise_x(0, 0, S)
+        gather("scalar", 1, 2, 0, S)
+        gather("vector", 1, 3, 0, HALF)
+        gather("scalar", 1, 3, HALF, S)
+        weave("vector", 1, 0, HALF)
+        weave("scalar", 1, HALF, S)
+        quantise_x(1, 0, HALF)
+        quantise_x(1, HALF, S)
+        round_w2("vector", 0, LOW, 0, P)
         round_w2("scalar", 0, HIGH, 0, SCALAR_HIGH_M)
-        round_w2("vector", 1, HIGH, 0, EARLY_M[1], at=LAST_HIGH_AT)
-        round_w2("vector", 1, HIGH, EARLY_M[1], P)
+        round_w2("vector", 0, HIGH, SCALAR_HIGH_M, P)
+        quantise_w2(0, LOW)
         quantise_w2(0, HIGH)
-        round_w2("scalar", 1, LOW, 0, EARLY_M[1])
-        round_w2("scalar", 1, LOW, EARLY_M[1], P)
+        for m0, m1 in ((0, EARLY_M), (EARLY_M, P)):
+            round_w2("vector", 1, HIGH, m0, m1)
+            round_w2("scalar", 1, LOW, m0, m1)
         quantise_w2(1, HIGH)
         quantise_w2(1, LOW)
-        quantise_x(1, HALF, S, HALF)
 
         out_ps = [psum.tile([P, count * CHUNK], F32, name=f"out_ps{c}", offset=(CHUNKS + g) * BANK) for g, (c, count, engine) in enumerate(OUT_GROUPS)]
-
-        for i, width in enumerate(WARM_UP):
-            unread = psum.tile([P, width], F32, name=f"unread{i}", offset=i * BANK)
-            words, scales = x_operand(0, 0, width)
-            nc.tensor.matmul_mx(out=unread[:], lhsT=x_first[:, S - CHUNK : S].bitcast(FP8X4), lhsT_scale=w3_sc[:], rhs=words, rhs_scale=scales, start=True, stop=True)
-
-        w3_rows = w3_scales[0].rearrange("(q r) n -> r q n", r=SCALE_ROWS)
-        for r in range(SCALE_ROWS):
-            nc.sync.dma_start(out=w3_sc[r:P:QUADRANT, :].bitcast(I32), in_=w3_rows[r].bitcast(I32))
 
         h_ps = [psum.tile([P, PACK, CHUNK], F32, name=f"h_ps{c}", offset=c * BANK) for c in range(CHUNKS)]
 
         def h_passes(z, first, c):
-            words, scales = x_operand(z, c * CHUNK, (c + 1) * CHUNK)
+            tokens = slice(c * CHUNK, (c + 1) * CHUNK)
             for t in (first, first + 1):
                 cols = slice(t * P, (t + 1) * P)
                 nc.tensor.matmul_mx(
                     out=h_ps[c][:, t, :],
                     lhsT=w2_codes[z][:, cols].bitcast(FP8X4),
                     lhsT_scale=w2_sc[z][:, cols],
-                    rhs=words,
-                    rhs_scale=scales,
+                    rhs=x_codes[z][:, tokens].bitcast(FP8X4),
+                    rhs_scale=x_sc[z][:, tokens],
                     start=(z == 0 and t == LOW),
                     stop=(z == 1 and t == LOW + 1),
                 )
 
         def w1_pass(z, g):
             c, count, engine = OUT_GROUPS[g]
-            words, scales = x_operand(z, c * CHUNK, (c + count) * CHUNK)
+            tokens = slice(c * CHUNK, (c + count) * CHUNK)
             nc.tensor.matmul_mx(
                 out=out_ps[g][:],
                 lhsT=w1_codes[z][:].bitcast(FP8X4),
                 lhsT_scale=w1_sc[:, z * N : (z + 1) * N],
-                rhs=words,
-                rhs_scale=scales,
+                rhs=x_codes[z][:, tokens].bitcast(FP8X4),
+                rhs_scale=x_sc[z][:, tokens],
                 start=(z == 0),
                 stop=False,
             )

@@ -28,9 +28,13 @@ BANK = 2048
 HALF = S // 2
 LOW, HIGH = 0, 2
 
-X_LOADS = [(0, 0, 2), (0, 2, 4), (1, 0, 2), (1, 2, 3), (1, 3, 4)]
+X_LOADS = [(0, 0, 2), (0, 2, 4)] + [(1, j, j + 1) for j in range(PACK)]
+SCALAR_TOKENS = 352
 EARLY_M = P // 2
-SCALAR_HIGH_M = 88
+VECTOR_M = {LOW: 88, HIGH: 56}
+VECTOR_LAST_M = 104
+SCALAR_LAST = 352
+SCALAR_WEAVES = 160
 OUT_GROUPS = [(0, 2, "scalar"), (2, 1, "scalar"), (3, 1, "vector")]
 
 
@@ -45,30 +49,31 @@ def tile_picked_lora_relu_e_kernel(tc, xT, w1_words, w1_scales, w2, w3_words, w3
 
     with ExitStack() as ctx:
         keep = ctx.enter_context(tc.tile_pool(name="keep", bufs=1))
+        shared = ctx.enter_context(tc.tile_pool(name="shared", bufs=1))
         psum = ctx.enter_context(tc.psum_pool(name="psum", bufs=1))
 
-        def sbuf(shape, dtype, name):
+        def sbuf(shape, dtype, name, held=False):
+            if held:
+                return shared.tile(shape, dtype, name=name, align_bytes=64, offset=0)
             return keep.tile(shape, dtype, name=name, align_bytes=64)
 
         offsets = keep.tile([P, S // LIST_COLUMN], U16, name="offsets")
 
         w1_sc = sbuf([P, PASSES * N], U8, "w1_sc")
         w3_sc = sbuf([P, N], U8, "w3_sc")
-        nc.gpsimd.memset(w1_sc[:].bitcast(I32), 0)
-        nc.gpsimd.memset(w3_sc[:].bitcast(I32), 0)
+        nc.vector.memset(w1_sc[:].bitcast(I32), 0)
+        nc.vector.memset(w3_sc[:].bitcast(I32), 0)
         w1_rows = w1_scales.rearrange("z (q r) n -> r q z n", r=SCALE_ROWS)
         w3_rows = w3_scales[0].rearrange("(q r) n -> r q n", r=SCALE_ROWS)
 
-        x_row = {}
+        x_raw = {}
         for z, j0, j1 in X_LOADS:
             rows = xT[z * K_PASS : (z + 1) * K_PASS, :].rearrange("(p j) t -> p (j t)", j=PACK)
-            raw = sbuf([P, (j1 - j0) * T], F32, f"x_raw{z}{j0}")
-            nc.sync.dma_start(out=raw[:], in_=rows[:, j0 * T : j1 * T])
-            for j in range(j0, j1):
-                x_row[z, j] = raw[:, (j - j0) * T : (j - j0 + 1) * T]
+            x_raw[z, j0] = sbuf([P, (j1 - j0) * T], F32, f"x_raw{z}{j0}")
+            nc.sync.dma_start(out=x_raw[z, j0][:], in_=rows[:, j0 * T : j1 * T])
             if (z, j0) == (0, 0):
                 nc.sync.dma_start(offsets[:], offs)
-        w1_codes = [sbuf([P, N], I32, f"w1_codes{z}") for z in range(PASSES)]
+        w1_codes = sbuf([P, PASSES, N], I32, "w1_codes")
         w3_codes = sbuf([P, N], I32, "w3_codes")
         w2_raw = [sbuf([P, PACK, H], F32, f"w2_raw{z}") for z in range(PASSES)]
 
@@ -77,37 +82,59 @@ def tile_picked_lora_relu_e_kernel(tc, xT, w1_words, w1_scales, w2, w3_words, w3
             for a, b in zip(cuts, cuts[1:]):
                 nc.sync.dma_start(out=w2_raw[z][:].rearrange("p j c -> p (j c)")[:, a:b], in_=run[:, a:b])
 
-        def load_words(tile, words):
-            nc.sync.dma_start(out=tile[:], in_=words.rearrange("p n t -> p (n t)").bitcast(I32))
-
+        load_w2(0, [0, PACK * H])
+        load_w2(1, [0, (PACK - 1) * H + PACK * EARLY_M, PACK * H])
         for r in range(SCALE_ROWS):
             nc.sync.dma_start(out=w1_sc[r:P:QUADRANT, :].bitcast(I32).rearrange("q (z n) -> q z n", z=PASSES), in_=w1_rows[r].bitcast(I32))
-        load_w2(0, [0, PACK * H])
-        load_words(w1_codes[0], w1_words[0])
-        load_w2(1, [0, (PACK - 1) * H + PACK * EARLY_M, PACK * H])
-        load_words(w1_codes[1], w1_words[1])
-        load_words(w3_codes, w3_words[0])
+        nc.sync.dma_start(out=w1_codes[:], in_=w1_words.rearrange("z p n t -> p z (n t)").bitcast(I32))
+        nc.sync.dma_start(out=w3_codes[:], in_=w3_words[0].rearrange("p n t -> p (n t)").bitcast(I32))
         for r in range(SCALE_ROWS):
             nc.sync.dma_start(out=w3_sc[r:P:QUADRANT, :].bitcast(I32), in_=w3_rows[r].bitcast(I32))
 
-        picked = [sbuf([P, PACK, S], F32, f"picked{z}") for z in range(PASSES)]
-        x_codes = [sbuf([P, S], U32, f"x_codes{z}") for z in range(PASSES)]
+        picked_pairs = sbuf([P, 2, S], U32, "picked_pairs")
+        picked_rows = sbuf([P, PACK, S], F32, "picked_rows")
+        x_first = sbuf([P, S], U32, "x_first")
+        x_last = [sbuf([P, HALF], U32, "x_last0"), sbuf([P, HALF], U32, "x_last1", held=True)]
         x_sc = [sbuf([P, S], U8, f"x_sc{z}") for z in range(PASSES)]
-        woven = {}
+        woven = {(0, 0): sbuf([P, S * PACK], BF16, "woven0")}
+        for half in range(2):
+            woven[1, half * HALF] = sbuf([P, HALF * PACK], BF16, f"woven1{half}")
 
-        def gather(engine, z, j, a, b):
-            copy(engine, picked[z][:, j, a:b], x_row[z, j].indirect(offsets[:, a // LIST_COLUMN : b // LIST_COLUMN]))
+        def x_operand(z, a, b):
+            words = x_first[:, a:b] if z == 0 else x_last[a // HALF][:, a % HALF : a % HALF + b - a]
+            return words.bitcast(FP8X4), x_sc[z][:, a:b]
 
-        def weave(engine, z, a, b):
-            woven[z, a] = sbuf([P, (b - a) * PACK], BF16, f"woven{z}{a}")
+        def gather_pairs(u):
+            pairs = sbuf([P, T], U32, f"pairs{u}")
+            rows = x_raw[0, 2 * u][:].rearrange("p (e t) -> p e t", e=2)
+            for engine, a, b in (("scalar", T - SCALAR_TOKENS, T), ("vector", 0, T - SCALAR_TOKENS)):
+                copy(
+                    engine,
+                    pairs[:, a:b].bitcast(BF16).rearrange("p (c i e) -> p c e i", i=4, e=2),
+                    rows[:, :, a:b].rearrange("p e (c i) -> p c e i", i=4),
+                )
+            nc.vector.tensor_copy(out=picked_pairs[:, u, :], in_=pairs[:].indirect(offsets[:]))
+
+        def weave_pairs():
+            nc.vector.tensor_copy(
+                out=woven[0, 0][:].rearrange("p (s u e) -> p s u e", u=2, e=2),
+                in_=picked_pairs[:].bitcast(BF16).rearrange("p u (s e) -> p s u e", e=2),
+            )
+
+        def gather(engine, j, a, b):
+            copy(engine, picked_rows[:, j, a:b], x_raw[1, j][:].indirect(offsets[:, a // LIST_COLUMN : b // LIST_COLUMN]))
+
+        def weave(engine, a, b):
+            start = a // HALF * HALF
             copy(
                 engine,
-                woven[z, a][:].rearrange("p (c i j) -> p c j i", i=4, j=PACK),
-                picked[z][:, :, a:b].rearrange("p j (c i) -> p c j i", i=4),
+                woven[1, start][:, (a - start) * PACK : (b - start) * PACK].rearrange("p (c i j) -> p c j i", i=2, j=PACK),
+                picked_rows[:, :, a:b].rearrange("p j (c i) -> p c j i", i=2),
             )
 
         def quantise_x(z, a, b):
-            nc.vector.quantize_mx(out=x_codes[z][:, a:b].bitcast(FP8X4), scales=x_sc[z][:, a:b], in_=woven[z, a][:])
+            words, scales = x_operand(z, a, b)
+            nc.vector.quantize_mx(out=words, scales=scales, in_=woven[z, a][:])
 
         w2_codes = [sbuf([P, H], U32, f"w2_codes{z}") for z in range(PASSES)]
         w2_sc = [sbuf([P, H], U8, f"w2_sc{z}") for z in range(PASSES)]
@@ -115,7 +142,7 @@ def tile_picked_lora_relu_e_kernel(tc, xT, w1_words, w1_scales, w2, w3_words, w3
 
         def round_w2(engine, z, first, m0, m1):
             if (z, first) not in dealt:
-                dealt[z, first] = sbuf([P, 2 * P * PACK], BF16, f"dealt{z}{first}")
+                dealt[z, first] = sbuf([P, 2 * P * PACK], BF16, f"dealt{z}{first}", held=(z, first) == (1, HIGH))
             source = w2_raw[z][:].rearrange("p j (m t) -> p m j t", t=PACK)[:, m0:m1, :, first : first + 2]
             copy(engine, dealt[z, first][:].rearrange("p (t m j) -> p m j t", t=2, j=PACK)[:, m0:m1, :, :], source)
 
@@ -123,63 +150,70 @@ def tile_picked_lora_relu_e_kernel(tc, xT, w1_words, w1_scales, w2, w3_words, w3
             cols = slice(first * P, (first + 2) * P)
             nc.vector.quantize_mx(out=w2_codes[z][:, cols].bitcast(FP8X4), scales=w2_sc[z][:, cols], in_=dealt[z, first][:])
 
-        for j in range(PACK):
-            gather("scalar" if j % 2 else "vector", 0, j, 0, S)
-        weave("vector", 0, 0, S)
-        gather("scalar", 1, 0, 0, S)
-        gather("vector", 1, 1, 0, S)
+        for u in range(2):
+            gather_pairs(u)
+        gather("scalar", 0, 0, S)
+        weave_pairs()
+        gather("scalar", 1, 0, S)
         quantise_x(0, 0, S)
-        gather("scalar", 1, 2, 0, S)
-        gather("vector", 1, 3, 0, HALF)
-        gather("scalar", 1, 3, HALF, S)
-        weave("vector", 1, 0, HALF)
-        weave("scalar", 1, HALF, S)
+        gather("vector", 2, 0, S)
+        gather("scalar", 3, 0, SCALAR_LAST)
+        gather("vector", 3, SCALAR_LAST, S)
+        weave("vector", 0, HALF)
+        weave("scalar", S - SCALAR_WEAVES, S)
+        weave("vector", HALF, S - SCALAR_WEAVES)
         quantise_x(1, 0, HALF)
-        quantise_x(1, HALF, S)
-        round_w2("vector", 0, LOW, 0, P)
-        round_w2("scalar", 0, HIGH, 0, SCALAR_HIGH_M)
-        round_w2("vector", 0, HIGH, SCALAR_HIGH_M, P)
+        round_w2("vector", 0, LOW, 0, VECTOR_M[LOW])
+        round_w2("scalar", 0, LOW, VECTOR_M[LOW], P)
+        round_w2("vector", 0, HIGH, 0, VECTOR_M[HIGH])
+        round_w2("scalar", 0, HIGH, VECTOR_M[HIGH], P)
         quantise_w2(0, LOW)
         quantise_w2(0, HIGH)
-        for m0, m1 in ((0, EARLY_M), (EARLY_M, P)):
-            round_w2("vector", 1, HIGH, m0, m1)
-            round_w2("scalar", 1, LOW, m0, m1)
+        round_w2("vector", 1, HIGH, 0, EARLY_M)
+        round_w2("scalar", 1, LOW, 0, EARLY_M)
+        round_w2("vector", 1, HIGH, EARLY_M, P)
+        round_w2("scalar", 1, LOW, EARLY_M, VECTOR_LAST_M)
+        round_w2("vector", 1, LOW, VECTOR_LAST_M, P)
         quantise_w2(1, HIGH)
         quantise_w2(1, LOW)
+        quantise_x(1, HALF, S)
 
-        out_ps = [psum.tile([P, count * CHUNK], F32, name=f"out_ps{c}", offset=(CHUNKS + g) * BANK) for g, (c, count, engine) in enumerate(OUT_GROUPS)]
+        out_ps = [psum.tile([P, count * CHUNK], F32, name=f"out_ps{c}", offset=g * BANK) for g, (c, count, engine) in enumerate(OUT_GROUPS)]
+
+        unread = psum.tile([P, S], F32, name="unread", offset=CHUNKS * BANK)
+        stationary, stationary_sc = x_operand(1, 0, CHUNK)
+        moving, moving_sc = x_operand(0, 0, S)
+        nc.tensor.matmul_mx(out=unread[:], lhsT=stationary, lhsT_scale=stationary_sc, rhs=moving, rhs_scale=moving_sc, start=True, stop=True)
 
         h_ps = [psum.tile([P, PACK, CHUNK], F32, name=f"h_ps{c}", offset=c * BANK) for c in range(CHUNKS)]
 
         def h_passes(z, first, c):
-            tokens = slice(c * CHUNK, (c + 1) * CHUNK)
+            words, scales = x_operand(z, c * CHUNK, (c + 1) * CHUNK)
             for t in (first, first + 1):
                 cols = slice(t * P, (t + 1) * P)
                 nc.tensor.matmul_mx(
                     out=h_ps[c][:, t, :],
                     lhsT=w2_codes[z][:, cols].bitcast(FP8X4),
                     lhsT_scale=w2_sc[z][:, cols],
-                    rhs=x_codes[z][:, tokens].bitcast(FP8X4),
-                    rhs_scale=x_sc[z][:, tokens],
+                    rhs=words,
+                    rhs_scale=scales,
                     start=(z == 0 and t == LOW),
                     stop=(z == 1 and t == LOW + 1),
                 )
 
         def w1_pass(z, g):
             c, count, engine = OUT_GROUPS[g]
-            tokens = slice(c * CHUNK, (c + count) * CHUNK)
+            words, scales = x_operand(z, c * CHUNK, (c + count) * CHUNK)
             nc.tensor.matmul_mx(
                 out=out_ps[g][:],
-                lhsT=w1_codes[z][:].bitcast(FP8X4),
+                lhsT=w1_codes[:, z, :].bitcast(FP8X4),
                 lhsT_scale=w1_sc[:, z * N : (z + 1) * N],
-                rhs=x_codes[z][:, tokens].bitcast(FP8X4),
-                rhs_scale=x_sc[z][:, tokens],
+                rhs=words,
+                rhs_scale=scales,
                 start=(z == 0),
                 stop=False,
             )
 
-        for g in range(len(OUT_GROUPS)):
-            w1_pass(0, g)
         for first in (LOW, HIGH):
             for c in range(CHUNKS):
                 h_passes(0, first, c)
@@ -201,7 +235,8 @@ def tile_picked_lora_relu_e_kernel(tc, xT, w1_words, w1_scales, w2, w3_words, w3
                 else:
                     nc.scalar.activation(out=dst, in_=src, func=RELU)
         for g in range(len(OUT_GROUPS)):
-            w1_pass(1, g)
+            for z in range(PASSES):
+                w1_pass(z, g)
         for g, (c, count, engine) in enumerate(OUT_GROUPS):
             h_codes = sbuf([P, count * CHUNK], U32, f"h_codes{c}")
             h_sc = sbuf([P, count * CHUNK], U8, f"h_sc{c}")

@@ -31,10 +31,10 @@ LOW, HIGH = 0, 2
 X_LOADS = [(0, 0, 2), (0, 2, 4)] + [(1, j, j + 1) for j in range(PACK)]
 SCALAR_TOKENS = 352
 EARLY_M = P // 2
-VECTOR_M = {LOW: 88, HIGH: 56}
+VECTOR_M = {LOW: 80, HIGH: 56}
 VECTOR_LAST_M = 104
-SCALAR_LAST = 352
-SCALAR_WEAVES = 160
+SCALAR_THIRD = 288
+SCALAR_WEAVES = 192
 OUT_GROUPS = [(0, 2, "scalar"), (2, 1, "scalar"), (3, 1, "vector")]
 
 
@@ -52,10 +52,10 @@ def tile_picked_lora_relu_e_kernel(tc, xT, w1_words, w1_scales, w2, w3_words, w3
         shared = ctx.enter_context(tc.tile_pool(name="shared", bufs=1))
         psum = ctx.enter_context(tc.psum_pool(name="psum", bufs=1))
 
-        def sbuf(shape, dtype, name, held=False):
-            if held:
-                return shared.tile(shape, dtype, name=name, align_bytes=64, offset=0)
-            return keep.tile(shape, dtype, name=name, align_bytes=64)
+        def sbuf(shape, dtype, name, at=None):
+            if at is None:
+                return keep.tile(shape, dtype, name=name, align_bytes=64)
+            return shared.tile(shape, dtype, name=name, align_bytes=64, offset=at)
 
         offsets = keep.tile([P, S // LIST_COLUMN], U16, name="offsets")
 
@@ -93,16 +93,20 @@ def tile_picked_lora_relu_e_kernel(tc, xT, w1_words, w1_scales, w2, w3_words, w3
 
         picked_pairs = sbuf([P, 2, S], U32, "picked_pairs")
         picked_rows = sbuf([P, PACK, S], F32, "picked_rows")
-        x_first = sbuf([P, S], U32, "x_first")
-        x_last = [sbuf([P, HALF], U32, "x_last0"), sbuf([P, HALF], U32, "x_last1", held=True)]
-        x_sc = [sbuf([P, S], U8, f"x_sc{z}") for z in range(PASSES)]
-        woven = {(0, 0): sbuf([P, S * PACK], BF16, "woven0")}
-        for half in range(2):
-            woven[1, half * HALF] = sbuf([P, HALF * PACK], BF16, f"woven1{half}")
+        batches = [[(0, 0), (0, 1), (0, 2), (0, 3)], [(1, 0), (1, 1)], [(1, 2), (1, 3)]]
+        held_at = [None, None, 0]
+        woven = [sbuf([P, len(batch) * CHUNK * PACK], BF16, f"woven{i}") for i, batch in enumerate(batches)]
+        x_codes = [sbuf([P, len(batch) * CHUNK], U32, f"x_codes{i}", at=held_at[i]) for i, batch in enumerate(batches)]
+        x_sc = [sbuf([P, len(batch) * CHUNK], U8, f"x_sc{i}") for i, batch in enumerate(batches)]
+
+        def place(z, a, b):
+            i = [(z, a // CHUNK) in batch for batch in batches].index(True)
+            start = batches[i].index((z, a // CHUNK)) * CHUNK + a % CHUNK
+            return i, start, start + b - a
 
         def x_operand(z, a, b):
-            words = x_first[:, a:b] if z == 0 else x_last[a // HALF][:, a % HALF : a % HALF + b - a]
-            return words.bitcast(FP8X4), x_sc[z][:, a:b]
+            i, start, end = place(z, a, b)
+            return x_codes[i][:, start:end].bitcast(FP8X4), x_sc[i][:, start:end]
 
         def gather_pairs(u):
             pairs = sbuf([P, T], U32, f"pairs{u}")
@@ -115,26 +119,26 @@ def tile_picked_lora_relu_e_kernel(tc, xT, w1_words, w1_scales, w2, w3_words, w3
                 )
             nc.vector.tensor_copy(out=picked_pairs[:, u, :], in_=pairs[:].indirect(offsets[:]))
 
-        def weave_pairs():
+        def weave_pairs(a, b):
+            i, start, end = place(0, a, b)
             nc.vector.tensor_copy(
-                out=woven[0, 0][:].rearrange("p (s u e) -> p s u e", u=2, e=2),
-                in_=picked_pairs[:].bitcast(BF16).rearrange("p u (s e) -> p s u e", e=2),
+                out=woven[i][:, start * PACK : end * PACK].rearrange("p (s u e) -> p s u e", u=2, e=2),
+                in_=picked_pairs[:, :, a:b].bitcast(BF16).rearrange("p u (s e) -> p s u e", e=2),
             )
 
         def gather(engine, j, a, b):
             copy(engine, picked_rows[:, j, a:b], x_raw[1, j][:].indirect(offsets[:, a // LIST_COLUMN : b // LIST_COLUMN]))
 
         def weave(engine, a, b):
-            start = a // HALF * HALF
+            i, start, end = place(1, a, b)
             copy(
                 engine,
-                woven[1, start][:, (a - start) * PACK : (b - start) * PACK].rearrange("p (c i j) -> p c j i", i=2, j=PACK),
+                woven[i][:, start * PACK : end * PACK].rearrange("p (c i j) -> p c j i", i=2, j=PACK),
                 picked_rows[:, :, a:b].rearrange("p j (c i) -> p c j i", i=2),
             )
 
-        def quantise_x(z, a, b):
-            words, scales = x_operand(z, a, b)
-            nc.vector.quantize_mx(out=words, scales=scales, in_=woven[z, a][:])
+        def quantise_x(i):
+            nc.vector.quantize_mx(out=x_codes[i][:].bitcast(FP8X4), scales=x_sc[i][:], in_=woven[i][:])
 
         w2_codes = [sbuf([P, H], U32, f"w2_codes{z}") for z in range(PASSES)]
         w2_sc = [sbuf([P, H], U8, f"w2_sc{z}") for z in range(PASSES)]
@@ -142,7 +146,7 @@ def tile_picked_lora_relu_e_kernel(tc, xT, w1_words, w1_scales, w2, w3_words, w3
 
         def round_w2(engine, z, first, m0, m1):
             if (z, first) not in dealt:
-                dealt[z, first] = sbuf([P, 2 * P * PACK], BF16, f"dealt{z}{first}", held=(z, first) == (1, HIGH))
+                dealt[z, first] = sbuf([P, 2 * P * PACK], BF16, f"dealt{z}{first}", at=0 if (z, first) == (0, LOW) else None)
             source = w2_raw[z][:].rearrange("p j (m t) -> p m j t", t=PACK)[:, m0:m1, :, first : first + 2]
             copy(engine, dealt[z, first][:].rearrange("p (t m j) -> p m j t", t=2, j=PACK)[:, m0:m1, :, :], source)
 
@@ -153,21 +157,22 @@ def tile_picked_lora_relu_e_kernel(tc, xT, w1_words, w1_scales, w2, w3_words, w3
         for u in range(2):
             gather_pairs(u)
         gather("scalar", 0, 0, S)
-        weave_pairs()
+        weave_pairs(0, S)
         gather("scalar", 1, 0, S)
-        quantise_x(0, 0, S)
-        gather("vector", 2, 0, S)
-        gather("scalar", 3, 0, SCALAR_LAST)
-        gather("vector", 3, SCALAR_LAST, S)
+        quantise_x(0)
+        for j, split in ((2, SCALAR_THIRD), (3, HALF)):
+            gather("scalar", j, 0, split)
+            gather("vector", j, split, S)
         weave("vector", 0, HALF)
         weave("scalar", S - SCALAR_WEAVES, S)
         weave("vector", HALF, S - SCALAR_WEAVES)
-        quantise_x(1, 0, HALF)
+        quantise_x(1)
         round_w2("vector", 0, LOW, 0, VECTOR_M[LOW])
         round_w2("scalar", 0, LOW, VECTOR_M[LOW], P)
         round_w2("vector", 0, HIGH, 0, VECTOR_M[HIGH])
         round_w2("scalar", 0, HIGH, VECTOR_M[HIGH], P)
         quantise_w2(0, LOW)
+        quantise_x(2)
         quantise_w2(0, HIGH)
         round_w2("vector", 1, HIGH, 0, EARLY_M)
         round_w2("scalar", 1, LOW, 0, EARLY_M)
@@ -176,14 +181,14 @@ def tile_picked_lora_relu_e_kernel(tc, xT, w1_words, w1_scales, w2, w3_words, w3
         round_w2("vector", 1, LOW, VECTOR_LAST_M, P)
         quantise_w2(1, HIGH)
         quantise_w2(1, LOW)
-        quantise_x(1, HALF, S)
 
         out_ps = [psum.tile([P, count * CHUNK], F32, name=f"out_ps{c}", offset=g * BANK) for g, (c, count, engine) in enumerate(OUT_GROUPS)]
 
-        unread = psum.tile([P, S], F32, name="unread", offset=CHUNKS * BANK)
         stationary, stationary_sc = x_operand(1, 0, CHUNK)
-        moving, moving_sc = x_operand(0, 0, S)
-        nc.tensor.matmul_mx(out=unread[:], lhsT=stationary, lhsT_scale=stationary_sc, rhs=moving, rhs_scale=moving_sc, start=True, stop=True)
+        moving, moving_sc = x_operand(0, 0, CHUNK)
+        for i in range(4):
+            unread = psum.tile([P, CHUNK], F32, name=f"unread{i}", offset=(CHUNKS + i) * BANK)
+            nc.tensor.matmul_mx(out=unread[:], lhsT=stationary, lhsT_scale=stationary_sc, rhs=moving, rhs_scale=moving_sc, start=True, stop=True)
 
         h_ps = [psum.tile([P, PACK, CHUNK], F32, name=f"h_ps{c}", offset=c * BANK) for c in range(CHUNKS)]
 
@@ -237,6 +242,7 @@ def tile_picked_lora_relu_e_kernel(tc, xT, w1_words, w1_scales, w2, w3_words, w3
         for g in range(len(OUT_GROUPS)):
             for z in range(PASSES):
                 w1_pass(z, g)
+        result = keep.tile([P, S], F32, name="result")
         for g, (c, count, engine) in enumerate(OUT_GROUPS):
             h_codes = sbuf([P, count * CHUNK], U32, f"h_codes{c}")
             h_sc = sbuf([P, count * CHUNK], U8, f"h_sc{c}")
@@ -250,6 +256,6 @@ def tile_picked_lora_relu_e_kernel(tc, xT, w1_words, w1_scales, w2, w3_words, w3
                 start=False,
                 stop=True,
             )
-            result = keep.tile([P, count * CHUNK], F32, name=f"result{c}")
-            copy(engine, result[:], out_ps[g][:])
-            nc.sync.dma_start(out=out[:, c * CHUNK : (c + count) * CHUNK], in_=result[:])
+            copy(engine, result[:, c * CHUNK : (c + count) * CHUNK], out_ps[g][:])
+        for a in (0, HALF):
+            nc.sync.dma_start(out=out[:, a : a + HALF], in_=result[:, a : a + HALF])

@@ -146,13 +146,15 @@ def tile_picked_lora_relu_e_kernel(tc, xT, w1_words, w1_scales, w2, w3_words, w3
 
         def round_w2(engine, z, first, m0, m1):
             if (z, first) not in dealt:
-                dealt[z, first] = sbuf([P, 2 * P * PACK], BF16, f"dealt{z}{first}", at=0 if (z, first) == (0, LOW) else None)
+                dealt[z, first] = sbuf([P, 2 * P * PACK], BF16, f"dealt{z}{first}", at=0 if (z, first) == (1, HIGH) else None)
             source = w2_raw[z][:].rearrange("p j (m t) -> p m j t", t=PACK)[:, m0:m1, :, first : first + 2]
             copy(engine, dealt[z, first][:].rearrange("p (t m j) -> p m j t", t=2, j=PACK)[:, m0:m1, :, :], source)
 
-        def quantise_w2(z, first):
-            cols = slice(first * P, (first + 2) * P)
-            nc.vector.quantize_mx(out=w2_codes[z][:, cols].bitcast(FP8X4), scales=w2_sc[z][:, cols], in_=dealt[z, first][:])
+        def quantise_w2(z, t0, t1):
+            first = t0 - t0 % 2
+            cols = slice(t0 * P, t1 * P)
+            source = dealt[z, first][:, (t0 - first) * P * PACK : (t1 - first) * P * PACK]
+            nc.vector.quantize_mx(out=w2_codes[z][:, cols].bitcast(FP8X4), scales=w2_sc[z][:, cols], in_=source)
 
         for u in range(2):
             gather_pairs(u)
@@ -171,16 +173,17 @@ def tile_picked_lora_relu_e_kernel(tc, xT, w1_words, w1_scales, w2, w3_words, w3
         round_w2("scalar", 0, LOW, VECTOR_M[LOW], P)
         round_w2("vector", 0, HIGH, 0, VECTOR_M[HIGH])
         round_w2("scalar", 0, HIGH, VECTOR_M[HIGH], P)
-        quantise_w2(0, LOW)
-        quantise_x(2)
-        quantise_w2(0, HIGH)
+        quantise_w2(0, LOW, LOW + 1)
+        quantise_w2(0, LOW + 1, HIGH)
+        quantise_w2(0, HIGH, PACK)
         round_w2("vector", 1, HIGH, 0, EARLY_M)
         round_w2("scalar", 1, LOW, 0, EARLY_M)
         round_w2("vector", 1, HIGH, EARLY_M, P)
         round_w2("scalar", 1, LOW, EARLY_M, VECTOR_LAST_M)
         round_w2("vector", 1, LOW, VECTOR_LAST_M, P)
-        quantise_w2(1, HIGH)
-        quantise_w2(1, LOW)
+        quantise_w2(1, HIGH, PACK)
+        quantise_w2(1, LOW, HIGH)
+        quantise_x(2)
 
         out_ps = [psum.tile([P, count * CHUNK], F32, name=f"out_ps{c}", offset=g * BANK) for g, (c, count, engine) in enumerate(OUT_GROUPS)]
 
@@ -192,9 +195,9 @@ def tile_picked_lora_relu_e_kernel(tc, xT, w1_words, w1_scales, w2, w3_words, w3
 
         h_ps = [psum.tile([P, PACK, CHUNK], F32, name=f"h_ps{c}", offset=c * BANK) for c in range(CHUNKS)]
 
-        def h_passes(z, first, c):
+        def h_passes(z, quarters, c):
             words, scales = x_operand(z, c * CHUNK, (c + 1) * CHUNK)
-            for t in (first, first + 1):
+            for t in quarters:
                 cols = slice(t * P, (t + 1) * P)
                 nc.tensor.matmul_mx(
                     out=h_ps[c][:, t, :],
@@ -219,15 +222,14 @@ def tile_picked_lora_relu_e_kernel(tc, xT, w1_words, w1_scales, w2, w3_words, w3
                 stop=False,
             )
 
-        for first in (LOW, HIGH):
+        for t in range(PACK):
             for c in range(CHUNKS):
-                h_passes(0, first, c)
+                h_passes(0, [t], c)
         for first in (HIGH, LOW):
             for c in range(CHUNKS // 2):
-                h_passes(1, first, c)
+                h_passes(1, [first, first + 1], c)
         for c in range(CHUNKS // 2, CHUNKS):
-            for first in (HIGH, LOW):
-                h_passes(1, first, c)
+            h_passes(1, [HIGH, HIGH + 1, LOW, LOW + 1], c)
 
         h_bf = {}
         for c, count, engine in OUT_GROUPS:

@@ -31,11 +31,12 @@ LOW, HIGH = 0, 2
 X_LOADS = [(0, 0, 2), (0, 2, 4)] + [(1, j, j + 1) for j in range(PACK)]
 SCALAR_TOKENS = 352
 EARLY_M = P // 2
-VECTOR_M = {LOW: 80, HIGH: 56}
+VECTOR_M = {LOW: 80, HIGH: 40}
 VECTOR_LAST_M = 104
 SCALAR_THIRD = 288
 SCALAR_WEAVES = 192
-OUT_GROUPS = [(0, 2, "scalar"), (2, 1, "scalar"), (3, 1, "vector")]
+H_BATCHES = [(0, 2), (2, 1), (3, 1)]
+OUT_BANKS = [0, 1, 2, CHUNKS]
 
 
 def tile_picked_lora_relu_e_kernel(tc, xT, w1_words, w1_scales, w2, w3_words, w3_scales, offs, out):
@@ -182,10 +183,11 @@ def tile_picked_lora_relu_e_kernel(tc, xT, w1_words, w1_scales, w2, w3_words, w3
         round_w2("scalar", 1, LOW, EARLY_M, VECTOR_LAST_M)
         round_w2("vector", 1, LOW, VECTOR_LAST_M, P)
         quantise_w2(1, HIGH, PACK)
-        quantise_w2(1, LOW, HIGH)
+        quantise_w2(1, LOW, LOW + 1)
+        quantise_w2(1, LOW + 1, HIGH)
         quantise_x(2)
 
-        out_ps = [psum.tile([P, count * CHUNK], F32, name=f"out_ps{c}", offset=g * BANK) for g, (c, count, engine) in enumerate(OUT_GROUPS)]
+        out_ps = [psum.tile([P, CHUNK], F32, name=f"out_ps{c}", offset=bank * BANK) for c, bank in enumerate(OUT_BANKS)]
 
         stationary, stationary_sc = x_operand(1, 0, CHUNK)
         moving, moving_sc = x_operand(0, 0, CHUNK)
@@ -209,30 +211,26 @@ def tile_picked_lora_relu_e_kernel(tc, xT, w1_words, w1_scales, w2, w3_words, w3
                     stop=(z == 1 and t == LOW + 1),
                 )
 
-        def w1_pass(z, g):
-            c, count, engine = OUT_GROUPS[g]
-            words, scales = x_operand(z, c * CHUNK, (c + count) * CHUNK)
+        def w1_pass(z, c):
+            words, scales = x_operand(z, c * CHUNK, (c + 1) * CHUNK)
             nc.tensor.matmul_mx(
-                out=out_ps[g][:],
+                out=out_ps[c][:],
                 lhsT=w1_codes[:, z, :].bitcast(FP8X4),
                 lhsT_scale=w1_sc[:, z * N : (z + 1) * N],
                 rhs=words,
                 rhs_scale=scales,
-                start=(z == 0),
+                start=(z == PASSES - 1),
                 stop=False,
             )
 
         for t in range(PACK):
             for c in range(CHUNKS):
                 h_passes(0, [t], c)
-        for first in (HIGH, LOW):
-            for c in range(CHUNKS // 2):
-                h_passes(1, [first, first + 1], c)
-        for c in range(CHUNKS // 2, CHUNKS):
+        for c in range(CHUNKS):
             h_passes(1, [HIGH, HIGH + 1, LOW, LOW + 1], c)
 
         h_bf = {}
-        for c, count, engine in OUT_GROUPS:
+        for c, count in H_BATCHES:
             h_bf[c] = sbuf([P, count * CHUNK * PACK], BF16, f"h_bf{c}")
             for i in range(count):
                 dst = h_bf[c][:, i * CHUNK * PACK : (i + 1) * CHUNK * PACK].rearrange("p (n t) -> p n t", t=PACK)
@@ -241,23 +239,25 @@ def tile_picked_lora_relu_e_kernel(tc, xT, w1_words, w1_scales, w2, w3_words, w3
                     nc.vector.tensor_scalar_max(out=dst, in0=src, scalar1=0.0)
                 else:
                     nc.scalar.activation(out=dst, in_=src, func=RELU)
-        for g in range(len(OUT_GROUPS)):
-            for z in range(PASSES):
-                w1_pass(z, g)
+        for c in range(CHUNKS):
+            for z in reversed(range(PASSES)):
+                w1_pass(z, c)
         result = keep.tile([P, S], F32, name="result")
-        for g, (c, count, engine) in enumerate(OUT_GROUPS):
+        for c, count in H_BATCHES:
             h_codes = sbuf([P, count * CHUNK], U32, f"h_codes{c}")
             h_sc = sbuf([P, count * CHUNK], U8, f"h_sc{c}")
             nc.vector.quantize_mx(out=h_codes[:].bitcast(FP8X4), scales=h_sc[:], in_=h_bf[c][:])
-            nc.tensor.matmul_mx(
-                out=out_ps[g][:],
-                lhsT=w3_codes[:].bitcast(FP8X4),
-                lhsT_scale=w3_sc[:],
-                rhs=h_codes[:].bitcast(FP8X4),
-                rhs_scale=h_sc[:],
-                start=False,
-                stop=True,
-            )
-            copy(engine, result[:, c * CHUNK : (c + count) * CHUNK], out_ps[g][:])
+            for i in range(count):
+                nc.tensor.matmul_mx(
+                    out=out_ps[c + i][:],
+                    lhsT=w3_codes[:].bitcast(FP8X4),
+                    lhsT_scale=w3_sc[:],
+                    rhs=h_codes[:, i * CHUNK : (i + 1) * CHUNK].bitcast(FP8X4),
+                    rhs_scale=h_sc[:, i * CHUNK : (i + 1) * CHUNK],
+                    start=False,
+                    stop=True,
+                )
+        for c in range(CHUNKS):
+            copy("vector" if c % 2 else "scalar", result[:, c * CHUNK : (c + 1) * CHUNK], out_ps[c][:])
         for a in (0, HALF):
             nc.sync.dma_start(out=out[:, a : a + HALF], in_=result[:, a : a + HALF])

@@ -37,6 +37,7 @@ SCALAR_THIRD = 288
 SCALAR_WEAVES = 192
 H_BATCHES = [(0, 2), (2, 1), (3, 1)]
 OUT_BANKS = [0, 1, 2, CHUNKS]
+DEALT_AT = {(0, LOW): 0, (1, HIGH): 2 * P * PACK * 2}
 
 
 def tile_picked_lora_relu_e_kernel(tc, xT, w1_words, w1_scales, w2, w3_words, w3_scales, offs, out):
@@ -94,20 +95,14 @@ def tile_picked_lora_relu_e_kernel(tc, xT, w1_words, w1_scales, w2, w3_words, w3
 
         picked_pairs = sbuf([P, 2, S], U32, "picked_pairs")
         picked_rows = sbuf([P, PACK, S], F32, "picked_rows")
-        batches = [[(0, 0), (0, 1), (0, 2), (0, 3)], [(1, 0), (1, 1)], [(1, 2), (1, 3)]]
-        held_at = [None, None, 0]
-        woven = [sbuf([P, len(batch) * CHUNK * PACK], BF16, f"woven{i}") for i, batch in enumerate(batches)]
-        x_codes = [sbuf([P, len(batch) * CHUNK], U32, f"x_codes{i}", at=held_at[i]) for i, batch in enumerate(batches)]
-        x_sc = [sbuf([P, len(batch) * CHUNK], U8, f"x_sc{i}") for i, batch in enumerate(batches)]
+        woven = [sbuf([P, S * PACK], BF16, f"woven{z}") for z in range(PASSES)]
+        x_sc = [sbuf([P, S], U8, f"x_sc{z}") for z in range(PASSES)]
+        x_codes = {}
 
-        def place(z, a, b):
-            i = [(z, a // CHUNK) in batch for batch in batches].index(True)
-            start = batches[i].index((z, a // CHUNK)) * CHUNK + a % CHUNK
-            return i, start, start + b - a
-
-        def x_operand(z, a, b):
-            i, start, end = place(z, a, b)
-            return x_codes[i][:, start:end].bitcast(FP8X4), x_sc[i][:, start:end]
+        def x_operand(z, c):
+            first = max(c0 for z0, c0 in x_codes if z0 == z and c0 <= c)
+            words = x_codes[z, first][:, (c - first) * CHUNK : (c - first + 1) * CHUNK]
+            return words.bitcast(FP8X4), x_sc[z][:, c * CHUNK : (c + 1) * CHUNK]
 
         def gather_pairs(u):
             pairs = sbuf([P, T], U32, f"pairs{u}")
@@ -120,26 +115,26 @@ def tile_picked_lora_relu_e_kernel(tc, xT, w1_words, w1_scales, w2, w3_words, w3
                 )
             nc.vector.tensor_copy(out=picked_pairs[:, u, :], in_=pairs[:].indirect(offsets[:]))
 
-        def weave_pairs(a, b):
-            i, start, end = place(0, a, b)
+        def weave_pairs():
             nc.vector.tensor_copy(
-                out=woven[i][:, start * PACK : end * PACK].rearrange("p (s u e) -> p s u e", u=2, e=2),
-                in_=picked_pairs[:, :, a:b].bitcast(BF16).rearrange("p u (s e) -> p s u e", e=2),
+                out=woven[0][:].rearrange("p (s u e) -> p s u e", u=2, e=2),
+                in_=picked_pairs[:].bitcast(BF16).rearrange("p u (s e) -> p s u e", e=2),
             )
 
         def gather(engine, j, a, b):
             copy(engine, picked_rows[:, j, a:b], x_raw[1, j][:].indirect(offsets[:, a // LIST_COLUMN : b // LIST_COLUMN]))
 
         def weave(engine, a, b):
-            i, start, end = place(1, a, b)
             copy(
                 engine,
-                woven[i][:, start * PACK : end * PACK].rearrange("p (c i j) -> p c j i", i=2, j=PACK),
+                woven[1][:, a * PACK : b * PACK].rearrange("p (c i j) -> p c j i", i=2, j=PACK),
                 picked_rows[:, :, a:b].rearrange("p j (c i) -> p c j i", i=2),
             )
 
-        def quantise_x(i):
-            nc.vector.quantize_mx(out=x_codes[i][:].bitcast(FP8X4), scales=x_sc[i][:], in_=woven[i][:])
+        def quantise_x(z, c0, c1, at=None):
+            a, b = c0 * CHUNK, c1 * CHUNK
+            x_codes[z, c0] = sbuf([P, b - a], U32, f"x_codes{z}{c0}", at=at)
+            nc.vector.quantize_mx(out=x_codes[z, c0][:].bitcast(FP8X4), scales=x_sc[z][:, a:b], in_=woven[z][:, a * PACK : b * PACK])
 
         w2_codes = [sbuf([P, H], U32, f"w2_codes{z}") for z in range(PASSES)]
         w2_sc = [sbuf([P, H], U8, f"w2_sc{z}") for z in range(PASSES)]
@@ -147,7 +142,7 @@ def tile_picked_lora_relu_e_kernel(tc, xT, w1_words, w1_scales, w2, w3_words, w3
 
         def round_w2(engine, z, first, m0, m1):
             if (z, first) not in dealt:
-                dealt[z, first] = sbuf([P, 2 * P * PACK], BF16, f"dealt{z}{first}", at=0 if (z, first) == (1, HIGH) else None)
+                dealt[z, first] = sbuf([P, 2 * P * PACK], BF16, f"dealt{z}{first}", at=DEALT_AT.get((z, first)))
             source = w2_raw[z][:].rearrange("p j (m t) -> p m j t", t=PACK)[:, m0:m1, :, first : first + 2]
             copy(engine, dealt[z, first][:].rearrange("p (t m j) -> p m j t", t=2, j=PACK)[:, m0:m1, :, :], source)
 
@@ -160,22 +155,23 @@ def tile_picked_lora_relu_e_kernel(tc, xT, w1_words, w1_scales, w2, w3_words, w3
         for u in range(2):
             gather_pairs(u)
         gather("scalar", 0, 0, S)
-        weave_pairs(0, S)
+        weave_pairs()
         gather("scalar", 1, 0, S)
-        quantise_x(0)
+        quantise_x(0, 0, CHUNKS)
         for j, split in ((2, SCALAR_THIRD), (3, HALF)):
             gather("scalar", j, 0, split)
             gather("vector", j, split, S)
         weave("vector", 0, HALF)
         weave("scalar", S - SCALAR_WEAVES, S)
         weave("vector", HALF, S - SCALAR_WEAVES)
-        quantise_x(1)
+        quantise_x(1, 0, 2)
         round_w2("vector", 0, LOW, 0, VECTOR_M[LOW])
         round_w2("scalar", 0, LOW, VECTOR_M[LOW], P)
         round_w2("vector", 0, HIGH, 0, VECTOR_M[HIGH])
         round_w2("scalar", 0, HIGH, VECTOR_M[HIGH], P)
         quantise_w2(0, LOW, LOW + 1)
         quantise_w2(0, LOW + 1, HIGH)
+        quantise_x(1, 2, 3, at=DEALT_AT[0, LOW])
         quantise_w2(0, HIGH, PACK)
         round_w2("vector", 1, HIGH, 0, EARLY_M)
         round_w2("scalar", 1, LOW, 0, EARLY_M)
@@ -185,12 +181,12 @@ def tile_picked_lora_relu_e_kernel(tc, xT, w1_words, w1_scales, w2, w3_words, w3
         quantise_w2(1, HIGH, PACK)
         quantise_w2(1, LOW, LOW + 1)
         quantise_w2(1, LOW + 1, HIGH)
-        quantise_x(2)
+        quantise_x(1, 3, 4, at=DEALT_AT[1, HIGH])
 
         out_ps = [psum.tile([P, CHUNK], F32, name=f"out_ps{c}", offset=bank * BANK) for c, bank in enumerate(OUT_BANKS)]
 
-        stationary, stationary_sc = x_operand(1, 0, CHUNK)
-        moving, moving_sc = x_operand(0, 0, CHUNK)
+        stationary, stationary_sc = x_operand(1, 0)
+        moving, moving_sc = x_operand(0, 0)
         for i in range(4):
             unread = psum.tile([P, CHUNK], F32, name=f"unread{i}", offset=(CHUNKS + i) * BANK)
             nc.tensor.matmul_mx(out=unread[:], lhsT=stationary, lhsT_scale=stationary_sc, rhs=moving, rhs_scale=moving_sc, start=True, stop=True)
@@ -198,7 +194,7 @@ def tile_picked_lora_relu_e_kernel(tc, xT, w1_words, w1_scales, w2, w3_words, w3
         h_ps = [psum.tile([P, PACK, CHUNK], F32, name=f"h_ps{c}", offset=c * BANK) for c in range(CHUNKS)]
 
         def h_passes(z, quarters, c):
-            words, scales = x_operand(z, c * CHUNK, (c + 1) * CHUNK)
+            words, scales = x_operand(z, c)
             for t in quarters:
                 cols = slice(t * P, (t + 1) * P)
                 nc.tensor.matmul_mx(
@@ -212,7 +208,7 @@ def tile_picked_lora_relu_e_kernel(tc, xT, w1_words, w1_scales, w2, w3_words, w3
                 )
 
         def w1_pass(z, c):
-            words, scales = x_operand(z, c * CHUNK, (c + 1) * CHUNK)
+            words, scales = x_operand(z, c)
             nc.tensor.matmul_mx(
                 out=out_ps[c][:],
                 lhsT=w1_codes[:, z, :].bitcast(FP8X4),

@@ -35,7 +35,7 @@ VECTOR_M = {LOW: 80, HIGH: 40}
 VECTOR_LAST_M = 104
 SCALAR_THIRD = 288
 SCALAR_WEAVES = 192
-H_BATCHES = [(0, 2), (2, 1), (3, 1)]
+H_BATCHES = [(0, 2), (2, 2)]
 OUT_BANKS = [0, 1, 2, CHUNKS]
 DEALT_AT = {(0, LOW): 0, (1, HIGH): 2 * P * PACK * 2}
 
@@ -179,8 +179,7 @@ def tile_picked_lora_relu_e_kernel(tc, xT, w1_words, w1_scales, w2, w3_words, w3
         round_w2("scalar", 1, LOW, EARLY_M, VECTOR_LAST_M)
         round_w2("vector", 1, LOW, VECTOR_LAST_M, P)
         quantise_w2(1, HIGH, PACK)
-        quantise_w2(1, LOW, LOW + 1)
-        quantise_w2(1, LOW + 1, HIGH)
+        quantise_w2(1, LOW, HIGH)
         quantise_x(1, 3, 4, at=DEALT_AT[1, HIGH])
 
         out_ps = [psum.tile([P, CHUNK], F32, name=f"out_ps{c}", offset=bank * BANK) for c, bank in enumerate(OUT_BANKS)]

@@ -32,7 +32,7 @@ X_LOADS = [(0, 0, 2), (0, 2, 4)] + [(1, j, j + 1) for j in range(PACK)]
 SCALAR_TOKENS = 352
 EARLY_M = P // 2
 VECTOR_M = {LOW: 80, HIGH: 40}
-VECTOR_LAST_M = 104
+VECTOR_LAST_M = 88
 SCALAR_THIRD = 288
 SCALAR_WEAVES = 192
 H_BATCHES = [(0, 2), (2, 2)]

from contextlib import ExitStack

import concourse.mybir as mybir

K, T, S, H, N = 1024, 1024, 512, 512, 128
FLOPS = 2 * S * (K * H + K * N + H * N)

F32 = mybir.dt.float32
BF16 = mybir.dt.bfloat16
I32 = mybir.dt.int32
U32 = mybir.dt.uint32
U16 = mybir.dt.uint16
U8 = mybir.dt.uint8
FP8X4 = mybir.dt.float8_e4m3fn_x4
COPY = mybir.ActivationFunctionType.Copy
RELU = mybir.ActivationFunctionType.Relu

P = 128
PACK = 4
K_PASS = P * PACK
PASSES = K // K_PASS
LIST_COLUMN = 16
SCALE_ROWS = 4
QUADRANT = 32
CHUNK = 128
CHUNKS = S // CHUNK
BANK = 2048
HALF = S // 2
LOW, HIGH = 0, 2

X_LOADS = [(0, 0, 2), (0, 2, 4)] + [(1, j, j + 1) for j in range(PACK)]
SCALAR_TOKENS = 352
EARLY_M = P // 2
VECTOR_M = {LOW: 80, HIGH: 40}
VECTOR_LAST_M = 88
SCALAR_THIRD = 288
SCALAR_WEAVES = 192
H_BATCHES = [(0, 2), (2, 2)]
OUT_BANKS = [0, 1, 2, CHUNKS]
DEALT_AT = {(0, LOW): 0, (1, HIGH): 2 * P * PACK * 2}


def tile_picked_lora_relu_e_kernel(tc, xT, w1_words, w1_scales, w2, w3_words, w3_scales, offs, out):
    nc = tc.nc

    def copy(engine, dst, src):
        if engine == "scalar":
            nc.scalar.activation(out=dst, in_=src, func=COPY)
        else:
            nc.vector.tensor_copy(out=dst, in_=src)

    with ExitStack() as ctx:
        keep = ctx.enter_context(tc.tile_pool(name="keep", bufs=1))
        shared = ctx.enter_context(tc.tile_pool(name="shared", bufs=1))
        psum = ctx.enter_context(tc.psum_pool(name="psum", bufs=1))

        def sbuf(shape, dtype, name, at=None):
            if at is None:
                return keep.tile(shape, dtype, name=name, align_bytes=64)
            return shared.tile(shape, dtype, name=name, align_bytes=64, offset=at)

        offsets = keep.tile([P, S // LIST_COLUMN], U16, name="offsets")

        w1_sc = sbuf([P, PASSES * N], U8, "w1_sc")
        w3_sc = sbuf([P, N], U8, "w3_sc")
        nc.vector.memset(w1_sc[:].bitcast(I32), 0)
        nc.vector.memset(w3_sc[:].bitcast(I32), 0)
        w1_rows = w1_scales.rearrange("z (q r) n -> r q z n", r=SCALE_ROWS)
        w3_rows = w3_scales[0].rearrange("(q r) n -> r q n", r=SCALE_ROWS)

        x_raw = {}
        for z, j0, j1 in X_LOADS:
            rows = xT[z * K_PASS : (z + 1) * K_PASS, :].rearrange("(p j) t -> p (j t)", j=PACK)
            x_raw[z, j0] = sbuf([P, (j1 - j0) * T], F32, f"x_raw{z}{j0}")
            nc.sync.dma_start(out=x_raw[z, j0][:], in_=rows[:, j0 * T : j1 * T])
            if (z, j0) == (0, 0):
                nc.sync.dma_start(offsets[:], offs)
        w1_codes = sbuf([P, PASSES, N], I32, "w1_codes")
        w3_codes = sbuf([P, N], I32, "w3_codes")
        w2_raw = [sbuf([P, PACK, H], F32, f"w2_raw{z}") for z in range(PASSES)]

        def load_w2(z, cuts):
            run = w2[z * K_PASS : (z + 1) * K_PASS, :].rearrange("(p j) c -> p (j c)", j=PACK)
            for a, b in zip(cuts, cuts[1:]):
                nc.sync.dma_start(out=w2_raw[z][:].rearrange("p j c -> p (j c)")[:, a:b], in_=run[:, a:b])

        load_w2(0, [0, PACK * H])
        load_w2(1, [0, (PACK - 1) * H + PACK * EARLY_M, PACK * H])
        for r in range(SCALE_ROWS):
            nc.sync.dma_start(out=w1_sc[r:P:QUADRANT, :].bitcast(I32).rearrange("q (z n) -> q z n", z=PASSES), in_=w1_rows[r].bitcast(I32))
        nc.sync.dma_start(out=w1_codes[:], in_=w1_words.rearrange("z p n t -> p z (n t)").bitcast(I32))
        nc.sync.dma_start(out=w3_codes[:], in_=w3_words[0].rearrange("p n t -> p (n t)").bitcast(I32))
        for r in range(SCALE_ROWS):
            nc.sync.dma_start(out=w3_sc[r:P:QUADRANT, :].bitcast(I32), in_=w3_rows[r].bitcast(I32))

        picked_pairs = sbuf([P, 2, S], U32, "picked_pairs")
        picked_rows = sbuf([P, PACK, S], F32, "picked_rows")
        woven = [sbuf([P, S * PACK], BF16, f"woven{z}") for z in range(PASSES)]
        x_sc = [sbuf([P, S], U8, f"x_sc{z}") for z in range(PASSES)]
        x_codes = {}

        def x_operand(z, c):
            first = max(c0 for z0, c0 in x_codes if z0 == z and c0 <= c)
            words = x_codes[z, first][:, (c - first) * CHUNK : (c - first + 1) * CHUNK]
            return words.bitcast(FP8X4), x_sc[z][:, c * CHUNK : (c + 1) * CHUNK]

        def gather_pairs(u):
            pairs = sbuf([P, T], U32, f"pairs{u}")
            rows = x_raw[0, 2 * u][:].rearrange("p (e t) -> p e t", e=2)
            for engine, a, b in (("scalar", T - SCALAR_TOKENS, T), ("vector", 0, T - SCALAR_TOKENS)):
                copy(
                    engine,
                    pairs[:, a:b].bitcast(BF16).rearrange("p (c i e) -> p c e i", i=4, e=2),
                    rows[:, :, a:b].rearrange("p e (c i) -> p c e i", i=4),
                )
            nc.vector.tensor_copy(out=picked_pairs[:, u, :], in_=pairs[:].indirect(offsets[:]))

        def weave_pairs():
            nc.vector.tensor_copy(
                out=woven[0][:].rearrange("p (s u e) -> p s u e", u=2, e=2),
                in_=picked_pairs[:].bitcast(BF16).rearrange("p u (s e) -> p s u e", e=2),
            )

        def gather(engine, j, a, b):
            copy(engine, picked_rows[:, j, a:b], x_raw[1, j][:].indirect(offsets[:, a // LIST_COLUMN : b // LIST_COLUMN]))

        def weave(engine, a, b):
            copy(
                engine,
                woven[1][:, a * PACK : b * PACK].rearrange("p (c i j) -> p c j i", i=2, j=PACK),
                picked_rows[:, :, a:b].rearrange("p j (c i) -> p c j i", i=2),
            )

        def quantise_x(z, c0, c1, at=None):
            a, b = c0 * CHUNK, c1 * CHUNK
            x_codes[z, c0] = sbuf([P, b - a], U32, f"x_codes{z}{c0}", at=at)
            nc.vector.quantize_mx(out=x_codes[z, c0][:].bitcast(FP8X4), scales=x_sc[z][:, a:b], in_=woven[z][:, a * PACK : b * PACK])

        w2_codes = [sbuf([P, H], U32, f"w2_codes{z}") for z in range(PASSES)]
        w2_sc = [sbuf([P, H], U8, f"w2_sc{z}") for z in range(PASSES)]
        dealt = {}

        def round_w2(engine, z, first, m0, m1):
            if (z, first) not in dealt:
                dealt[z, first] = sbuf([P, 2 * P * PACK], BF16, f"dealt{z}{first}", at=DEALT_AT.get((z, first)))
            source = w2_raw[z][:].rearrange("p j (m t) -> p m j t", t=PACK)[:, m0:m1, :, first : first + 2]
            copy(engine, dealt[z, first][:].rearrange("p (t m j) -> p m j t", t=2, j=PACK)[:, m0:m1, :, :], source)

        def quantise_w2(z, t0, t1):
            first = t0 - t0 % 2
            cols = slice(t0 * P, t1 * P)
            source = dealt[z, first][:, (t0 - first) * P * PACK : (t1 - first) * P * PACK]
            nc.vector.quantize_mx(out=w2_codes[z][:, cols].bitcast(FP8X4), scales=w2_sc[z][:, cols], in_=source)

        for u in range(2):
            gather_pairs(u)
        gather("scalar", 0, 0, S)
        weave_pairs()
        gather("scalar", 1, 0, S)
        quantise_x(0, 0, CHUNKS)
        for j, split in ((2, SCALAR_THIRD), (3, HALF)):
            gather("scalar", j, 0, split)
            gather("vector", j, split, S)
        weave("vector", 0, HALF)
        weave("scalar", S - SCALAR_WEAVES, S)
        weave("vector", HALF, S - SCALAR_WEAVES)
        quantise_x(1, 0, 2)
        round_w2("vector", 0, LOW, 0, VECTOR_M[LOW])
        round_w2("scalar", 0, LOW, VECTOR_M[LOW], P)
        round_w2("vector", 0, HIGH, 0, VECTOR_M[HIGH])
        round_w2("scalar", 0, HIGH, VECTOR_M[HIGH], P)
        quantise_w2(0, LOW, LOW + 1)
        quantise_w2(0, LOW + 1, HIGH)
        quantise_x(1, 2, 3, at=DEALT_AT[0, LOW])
        quantise_w2(0, HIGH, PACK)
        round_w2("vector", 1, HIGH, 0, EARLY_M)
        round_w2("scalar", 1, LOW, 0, EARLY_M)
        round_w2("vector", 1, HIGH, EARLY_M, P)
        round_w2("scalar", 1, LOW, EARLY_M, VECTOR_LAST_M)
        round_w2("vector", 1, LOW, VECTOR_LAST_M, P)
        quantise_w2(1, HIGH, PACK)
        quantise_w2(1, LOW, HIGH)
        quantise_x(1, 3, 4, at=DEALT_AT[1, HIGH])

        out_ps = [psum.tile([P, CHUNK], F32, name=f"out_ps{c}", offset=bank * BANK) for c, bank in enumerate(OUT_BANKS)]

        stationary, stationary_sc = x_operand(1, 0)
        moving, moving_sc = x_operand(0, 0)
        for i in range(4):
            unread = psum.tile([P, CHUNK], F32, name=f"unread{i}", offset=(CHUNKS + i) * BANK)
            nc.tensor.matmul_mx(out=unread[:], lhsT=stationary, lhsT_scale=stationary_sc, rhs=moving, rhs_scale=moving_sc, start=True, stop=True)

        h_ps = [psum.tile([P, PACK, CHUNK], F32, name=f"h_ps{c}", offset=c * BANK) for c in range(CHUNKS)]

        def h_passes(z, quarters, c):
            words, scales = x_operand(z, c)
            for t in quarters:
                cols = slice(t * P, (t + 1) * P)
                nc.tensor.matmul_mx(
                    out=h_ps[c][:, t, :],
                    lhsT=w2_codes[z][:, cols].bitcast(FP8X4),
                    lhsT_scale=w2_sc[z][:, cols],
                    rhs=words,
                    rhs_scale=scales,
                    start=(z == 0 and t == LOW),
                    stop=(z == 1 and t == LOW + 1),
                )

        def w1_pass(z, c):
            words, scales = x_operand(z, c)
            nc.tensor.matmul_mx(
                out=out_ps[c][:],
                lhsT=w1_codes[:, z, :].bitcast(FP8X4),
                lhsT_scale=w1_sc[:, z * N : (z + 1) * N],
                rhs=words,
                rhs_scale=scales,
                start=(z == PASSES - 1),
                stop=False,
            )

        for t in range(PACK):
            for c in range(CHUNKS):
                h_passes(0, [t], c)
        for c in range(CHUNKS):
            h_passes(1, [HIGH, HIGH + 1, LOW, LOW + 1], c)

        h_bf = {}
        for c, count in H_BATCHES:
            h_bf[c] = sbuf([P, count * CHUNK * PACK], BF16, f"h_bf{c}")
            for i in range(count):
                dst = h_bf[c][:, i * CHUNK * PACK : (i + 1) * CHUNK * PACK].rearrange("p (n t) -> p n t", t=PACK)
                src = h_ps[c + i][:].rearrange("p t n -> p n t")
                if (c + i) % 2 == 0:
                    nc.vector.tensor_scalar_max(out=dst, in0=src, scalar1=0.0)
                else:
                    nc.scalar.activation(out=dst, in_=src, func=RELU)
        for c in range(CHUNKS):
            for z in reversed(range(PASSES)):
                w1_pass(z, c)
        result = keep.tile([P, S], F32, name="result")
        for c, count in H_BATCHES:
            h_codes = sbuf([P, count * CHUNK], U32, f"h_codes{c}")
            h_sc = sbuf([P, count * CHUNK], U8, f"h_sc{c}")
            nc.vector.quantize_mx(out=h_codes[:].bitcast(FP8X4), scales=h_sc[:], in_=h_bf[c][:])
            for i in range(count):
                nc.tensor.matmul_mx(
                    out=out_ps[c + i][:],
                    lhsT=w3_codes[:].bitcast(FP8X4),
                    lhsT_scale=w3_sc[:],
                    rhs=h_codes[:, i * CHUNK : (i + 1) * CHUNK].bitcast(FP8X4),
                    rhs_scale=h_sc[:, i * CHUNK : (i + 1) * CHUNK],
                    start=False,
                    stop=True,
                )
        for c in range(CHUNKS):
            copy("vector" if c % 2 else "scalar", result[:, c * CHUNK : (c + 1) * CHUNK], out_ps[c][:])
        for a in (0, HALF):
            nc.sync.dma_start(out=out[:, a : a + HALF], in_=result[:, a : a + HALF])
